import numpy as np
import ml_dtypes


def mxq(x, axis, fmt="e4m3"):
    dtype, down = {"e4m3": (ml_dtypes.float8_e4m3fn, 7), "e5m2": (ml_dtypes.float8_e5m2, 14)}[fmt]
    v = np.moveaxis(np.asarray(x, np.float32).astype(ml_dtypes.bfloat16).astype(np.float64), axis, -1)
    blocks = v.reshape(v.shape[:-1] + (-1, 32))
    amax = np.abs(blocks).max(-1, keepdims=True)
    byte = np.maximum(np.where(amax > 0, np.frexp(amax)[1] - 1 + 127, 0) - down, 1)
    scale = np.exp2(byte - 127.0)
    codes = (blocks / scale).astype(np.float32).astype(dtype).astype(np.float64)
    return np.moveaxis((codes * scale).reshape(v.shape), -1, axis)


WIDE = False


def mx_kscale(k):
    if not WIDE:
        return np.ones(k)
    levels = np.array([10, -10, 5, -5, 0])
    if k % 512:
        return np.exp2(np.random.permutation(np.resize(levels, k // 32))).repeat(32)
    a = np.empty((k // 512, 16))
    for p in range(k // 512):
        a[p, :8] = np.random.permutation(np.resize(levels, 8))
        for g in range(8):
            far = levels[np.abs(levels - a[p, g]) >= 10]
            a[p, g + 8] = far[np.random.randint(len(far))]
    return np.exp2(a.ravel()).repeat(32)


def f64(x):
    return np.asarray(x).astype(np.float64)


def striped(idx):
    return np.tile(idx.reshape(-1, 16).T, (8, 1)).astype(np.uint16)


def unstriped(offs):
    return offs[:16].T.reshape(-1).astype(np.int64)


def pack_weight(w):
    k, n = w.shape
    w = f64(np.asarray(w, np.float32).astype(ml_dtypes.bfloat16)).reshape(k // 32, 32, n)
    amax = np.abs(w).max(1)
    byte = np.clip(np.where(amax > 0, np.frexp(amax)[1] - 1 + 127 - 7, 1), 1, 254)
    scaled = (w * np.exp2(127.0 - byte)[:, None, :]).reshape(k, n).astype(np.float32)
    words = np.ascontiguousarray(scaled.reshape(k // 512, 128, 4, n).transpose(0, 1, 3, 2)).astype(ml_dtypes.float8_e4m3fn).view(np.uint8)
    return words, np.ascontiguousarray(byte.astype(np.uint8).reshape(k // 512, 16, n))


def unpack_weight(words, scales):
    g, p, n, _ = words.shape
    vals = np.ascontiguousarray(words).view(ml_dtypes.float8_e4m3fn).astype(np.float64) * np.repeat(np.exp2(scales.astype(np.float64) - 127.0), 8, axis=1)[..., None]
    return vals.transpose(0, 1, 3, 2).reshape(g * 512, n)


K, T, S, D, V, H, N = 1024, 2048, 1024, 3, 512, 512, 128
P = 2 ** 7


def setup_inputs():
    n = np.random.standard_normal
    s = mx_kscale(K)[:, None]
    u = mx_kscale(H)
    packed_xT = pack_weight(n((K, T)) * s)
    packed_w2 = pack_weight(n((H, N)) / np.sqrt(H) / u[:, None])
    return {
        "x_words": packed_xT[0],
        "x_scales": packed_xT[1],
        "w1": (n((K, H)) / np.sqrt(K) / s * u).astype(np.float32),
        "w2_words": packed_w2[0],
        "w2_scales": packed_w2[1],
        "gate": (np.tile(np.random.uniform(0.2, 1.0, (D, 1, V)) / np.sqrt(D), (1, P, 1))).astype(np.float32),
        "offs": striped(np.random.permutation(T)[:S]),
        "cen": striped(np.random.permutation(S)[:V]),
        "pos1": striped(np.random.permutation(S)[:V]),
        "pos2": striped(np.random.permutation(S)[:V]),
        "pos3": striped(np.random.permutation(S)[:V]),
    }


def reference(x_words, x_scales, w1, w2_words, w2_scales, gate, offs, cen, pos1, pos2, pos3):
    xq = unpack_weight(x_words, x_scales)[:, unstriped(offs)]
    h = mxq(f64(w1), 0, "e4m3").T @ xq
    z = h[:, unstriped(cen)] - (h[:, unstriped(pos1)] * f64(gate)[0, :1] + h[:, unstriped(pos2)] * f64(gate)[1, :1] + h[:, unstriped(pos3)] * f64(gate)[2, :1])
    return unpack_weight(w2_words, w2_scales).T @ mxq(z, 0, "e4m3")

@@ -1,0 +1,213 @@
+from contextlib import ExitStack
+
+import concourse.mybir as mybir
+from concourse.masks import make_identity
+
+K, T, S, D, V, H, N = 1024, 2048, 1024, 3, 512, 512, 128
+FLOPS = 2 * K * H * S + 2 * H * N * V
+
+F32 = mybir.dt.float32
+BF16 = mybir.dt.bfloat16
+I32 = mybir.dt.int32
+U32 = mybir.dt.uint32
+U16 = mybir.dt.uint16
+U8 = mybir.dt.uint8
+FP8X4 = mybir.dt.float8_e4m3fn_x4
+COPY = mybir.ActivationFunctionType.Copy
+MULT = mybir.AluOpType.mult
+ADD = mybir.AluOpType.add
+
+P = 128
+PACK = 4
+K_PASS = P * PACK
+PASSES = K // K_PASS
+BANK = 512
+ROW_TILES = H // P
+BLOCKS = V // P
+FIRST_PIECES = ((0, 512), (512, 768), (768, 1024))
+HALVES = ((0, 512), (512, 1024))
+LAST_CHUNKS = ((0, 2), (2, 3), (3, 4))
+
+
+def tile_picked_lapl_none_p_kernel(tc, x_words, x_scales, w1, w2_words, w2_scales, gate, offs, cen, pos1, pos2, pos3, out):
+    nc = tc.nc
+    with ExitStack() as ctx:
+        keep = ctx.enter_context(tc.tile_pool(name="keep", bufs=1))
+        psum = ctx.enter_context(tc.psum_pool(name="psum", bufs=1))
+
+        def load_list(name, src):
+            t = keep.tile(list(src.shape), U16, name=name)
+            nc.sync.dma_start(t[:], src)
+            return t
+
+        def load_words(name, src):
+            t = keep.tile([P, src.shape[1]], U32, name=name, align_bytes=64)
+            nc.sync.dma_start(t[:].bitcast(I32), src.rearrange("p n t -> p (n t)").bitcast(I32))
+            return t
+
+        def load_w1(g, c0, c1):
+            t = keep.tile([P, PACK, c1 - c0], F32, name="w1_raw_%d_%d" % (g, c0))
+            nc.sync.dma_start(t[:], w1[g * K_PASS : (g + 1) * K_PASS, c0:c1].rearrange("(p j) c -> p j c", j=PACK))
+            return t
+
+        xs_all = keep.tile([P, T], U8, name="xs_all", align_bytes=64)
+        nc.gpsimd.memset(xs_all[:].bitcast(I32), 0)
+        gate_col = keep.tile([P, D, 8], F32, name="gate_col")
+        nc.scalar.dma_start(gate_col[:, :, 0:4], gate[:, 0, :].rearrange("d (p b) -> p d b", b=4))
+        offs_sb = load_list("offs_sb", offs)
+        cen_sb = load_list("cen_sb", cen)
+        for q in range(4):
+            nc.sync.dma_start(xs_all[32 * q : 32 * q + 4 * PASSES, :].bitcast(I32), x_scales[:, 4 * q : 4 * q + 4, :].bitcast(I32))
+        xw_all = [None, None]
+        w1_raw = {}
+        xw_all[0] = load_words("xw_all0", x_words[0])
+        for g in range(PASSES):
+            w1_raw[0, g] = load_w1(g, 0, P)[:]
+        xw_all[1] = load_words("xw_all1", x_words[1])
+        pos_sb = [load_list("pos%d_sb" % d, src) for d, src in enumerate((pos1, pos2, pos3))]
+        for g in range(PASSES):
+            w1_raw[1, g] = load_w1(g, P, 2 * P)[:]
+        for g in range(PASSES):
+            both = load_w1(g, 2 * P, 4 * P)
+            w1_raw[2, g] = both[:, :, 0:P]
+            w1_raw[3, g] = both[:, :, P : 2 * P]
+        w2w = load_words("w2w", w2_words[0])
+        w2s = keep.tile([P, N], U8, name="w2s", align_bytes=64)
+        nc.gpsimd.memset(w2s[:], 0)
+        for q in range(4):
+            nc.sync.dma_start(w2s[32 * q : 32 * q + 4, :].bitcast(I32), w2_scales[0, 4 * q : 4 * q + 4, :].bitcast(I32))
+
+        ident = keep.tile([P, P], F32, name="ident")
+        make_identity(nc, ident[:])
+
+        neg_gate = []
+        for d in range(D):
+            spread = psum.tile([P, 4, P], F32, name="spread%d" % d, tag="zt%d" % d)
+            for b in range(4):
+                nc.tensor.transpose(spread[:, b, :], gate_col[:, d, b : b + 1].to_broadcast([P, P]), ident[:])
+            ng = keep.tile([P, V], F32, name="neg_gate%d" % d)
+            nc.scalar.activation(ng[:].rearrange("q (p b) -> q p b", b=4), spread[:].rearrange("q b p -> q p b"), COPY, scale=-1.0)
+            neg_gate.append(ng)
+
+        w1_codes, w1_planes, w1_bf = {}, {}, {}
+
+        def round_w1(a, g):
+            if a not in w1_bf:
+                w1_bf[a] = keep.tile([P, PASSES, P * PACK], BF16, name="w1_bf%d" % a, tag="stage%d" % a, align_bytes=64)
+                w1_codes[a] = keep.tile([P, PASSES, P], U32, name="w1_codes%d" % a, align_bytes=64)
+                w1_planes[a] = keep.tile([P, PASSES, P], U8, name="w1_planes%d" % a, align_bytes=64)
+            nc.scalar.activation(
+                w1_bf[a][:, g, :].rearrange("p (c i j) -> p c j i", i=4, j=PACK),
+                w1_raw[a, g].rearrange("p j (c i) -> p c j i", i=4),
+                COPY,
+            )
+
+        def quantize_w1(a, g0, g1):
+            nc.vector.quantize_mx(
+                out=w1_codes[a][:, g0:g1, :].rearrange("p g c -> p (g c)").bitcast(FP8X4),
+                scales=w1_planes[a][:, g0:g1, :].rearrange("p g c -> p (g c)"),
+                in_=w1_bf[a][:, g0:g1, :].rearrange("p g c -> p (g c)"),
+            )
+
+        xs = keep.tile([P, S], U8, name="xs", align_bytes=64)
+        nc.vector.tensor_copy(xs[:], xs_all[:].indirect(offs_sb[:]))
+        xw = [keep.tile([P, S], U32, name="xw0", align_bytes=64)]
+        nc.vector.tensor_copy(xw[0][:], xw_all[0][:].indirect(offs_sb[:]))
+        for g in range(PASSES):
+            round_w1(0, g)
+        quantize_w1(0, 0, PASSES)
+        xw.append(keep.tile([P, S], U32, name="xw1", tag="stage0", align_bytes=64))
+        for c0, c1 in FIRST_PIECES:
+            nc.vector.tensor_copy(xw[1][:, c0:c1], xw_all[1][:].indirect(offs_sb[:, c0 // 16 : c1 // 16]))
+
+        bank_use = []
+
+        def one_pass(acc, a, g, c0, c1):
+            nc.tensor.matmul_mx(
+                out=acc[:],
+                lhsT=w1_codes[a][:, g, :].bitcast(FP8X4),
+                lhsT_scale=w1_planes[a][:, g, :],
+                rhs=xw[g][:, c0:c1].bitcast(FP8X4),
+                rhs_scale=xs[4 * g : P, c0:c1],
+                start=(g == 0),
+                stop=(g == PASSES - 1),
+            )
+
+        def bank_tile(shape, name):
+            bank_use.append(name)
+            return psum.tile(shape, F32, name=name, tag="mm%d" % (len(bank_use) % 4))
+
+        def first_product(a, pieces):
+            h = keep.tile([P, S], F32, name="h%d" % a)
+            for c0, c1 in pieces:
+                acc = bank_tile([P, c1 - c0], "acc%d_%d" % (a, c0))
+                for g in range(PASSES):
+                    one_pass(acc, a, g, c0, c1)
+                nc.scalar.activation(h[:, c0:c1], acc[:], COPY)
+            return h
+
+        zt = [psum.tile([P, H], F32, name="zt%d" % b, tag="zt%d" % b) for b in range(BLOCKS)]
+        zt_bf = [keep.tile([P, 2, P, 2], BF16, name="zt_bf%d" % b) for b in range(BLOCKS)]
+
+        def laplacian(h, a, b0, b1, reuse):
+            width = (b1 - b0) * P
+            cols = slice(b0 * P, b1 * P)
+            entries = slice(b0 * P // 16, b1 * P // 16)
+            terms = [keep.tile([P, width], F32, name="term%d_%d_%d" % (a, b0, d), tag=reuse.get(d, ""), align_bytes=64) for d in range(D)]
+            for d in range(D):
+                nc.vector.tensor_tensor(terms[d][:], h[:].indirect(pos_sb[d][:, entries]), neg_gate[d][:, cols], MULT)
+            own = keep.tile([P, width], F32, name="own%d_%d" % (a, b0))
+            nc.vector.tensor_tensor(own[:], h[:].indirect(cen_sb[:, entries]), terms[0][:], ADD)
+            summands = terms[1:] + [own]
+            for s, term in enumerate(summands):
+                for b in range(b0, b1):
+                    nc.tensor.matmul(
+                        zt[b][:, a * P : (a + 1) * P],
+                        term[:, (b - b0) * P : (b - b0 + 1) * P],
+                        ident[:],
+                        start=(s == 0),
+                        stop=(s == len(summands) - 1),
+                        is_transpose=True,
+                    )
+
+        def round_z(b, a0, a1):
+            nc.scalar.activation(
+                zt_bf[b][:, :, 32 * a0 : 32 * a1, :],
+                zt[b][:, a0 * P : a1 * P].rearrange("v (p u e) -> v u p e", u=2, e=2),
+                COPY,
+            )
+
+        def second_product(c, b0, b1):
+            nb = b1 - b0
+            width = nb * P
+            back = bank_tile([P, nb, 2, P], "back%d" % c)
+            for b in range(b0, b1):
+                round_z(b, ROW_TILES - 1, ROW_TILES)
+                words = zt_bf[b][:].rearrange("v u p e -> v (u p e)").bitcast(F32)
+                for u in range(2):
+                    nc.tensor.transpose(back[:, b - b0, u, :], words[:, u * P : (u + 1) * P], ident[:])
+            z_bf = keep.tile([P, width * PACK], BF16, name="z_bf%d" % c, align_bytes=64)
+            nc.scalar.copy(z_bf[:].bitcast(F32).rearrange("p (b v u) -> p b v u", b=nb, u=2), back[:].rearrange("p b u v -> p b v u"))
+            z_codes = keep.tile([P, width], U32, name="z_codes%d" % c, align_bytes=64)
+            z_plane = keep.tile([P, width], U8, name="z_plane%d" % c, align_bytes=64)
+            nc.vector.quantize_mx(out=z_codes[:].bitcast(FP8X4), scales=z_plane[:], in_=z_bf[:])
+            res = bank_tile([P, width], "res%d" % c)
+            nc.tensor.matmul_mx(out=res[:], lhsT=w2w[:].bitcast(FP8X4), lhsT_scale=w2s[:], rhs=z_codes[:].bitcast(FP8X4), rhs_scale=z_plane[:], start=True, stop=True)
+            res_sb = keep.tile([P, width], F32, name="res_sb%d" % c)
+            nc.scalar.activation(res_sb[:], res[:], COPY)
+            nc.sync.dma_start(out[:, b0 * P : b1 * P], res_sb[:])
+
+        h = first_product(0, FIRST_PIECES)
+        for a in range(ROW_TILES - 1):
+            for g in range(PASSES):
+                round_w1(a + 1, g)
+            quantize_w1(a + 1, 0, PASSES)
+            h_next = first_product(a + 1, HALVES)
+            laplacian(h, a, 0, BLOCKS, {1 if a == 0 else 0: "stage%d" % (a + 1)})
+            h = h_next
+        for b in range(BLOCKS):
+            round_z(b, 0, ROW_TILES - 1)
+        for b0, b1 in LAST_CHUNKS:
+            laplacian(h, ROW_TILES - 1, b0, b1, {})
+        for c, (b0, b1) in enumerate(LAST_CHUNKS):
+            second_product(c, b0, b1)

@@ -26,7 +26,6 @@ ROW_TILES = H // P
 BLOCKS = V // P
 FIRST_PIECES = ((0, 512), (512, 768), (768, 1024))
 HALVES = ((0, 512), (512, 1024))
-LAST_CHUNKS = ((0, 2), (2, 3), (3, 4))
 
 
 def tile_picked_lapl_none_p_kernel(tc, x_words, x_scales, w1, w2_words, w2_scales, gate, offs, cen, pos1, pos2, pos3, out):
@@ -45,28 +44,29 @@ def tile_picked_lapl_none_p_kernel(tc, x_words, x_scales, w1, w2_words, w2_scale
             nc.sync.dma_start(t[:].bitcast(I32), src.rearrange("p n t -> p (n t)").bitcast(I32))
             return t
 
-        def load_w1(g, c0, c1):
-            t = keep.tile([P, PACK, c1 - c0], F32, name="w1_raw_%d_%d" % (g, c0))
+        def load_w1(g, c0, c1, tag=""):
+            t = keep.tile([P, PACK, c1 - c0], F32, name="w1_raw_%d_%d" % (g, c0), tag=tag)
             nc.sync.dma_start(t[:], w1[g * K_PASS : (g + 1) * K_PASS, c0:c1].rearrange("(p j) c -> p j c", j=PACK))
             return t
 
         xs_all = keep.tile([P, T], U8, name="xs_all", align_bytes=64)
         nc.gpsimd.memset(xs_all[:].bitcast(I32), 0)
-        gate_col = keep.tile([P, D, 8], F32, name="gate_col")
-        nc.scalar.dma_start(gate_col[:, :, 0:4], gate[:, 0, :].rearrange("d (p b) -> p d b", b=4))
         offs_sb = load_list("offs_sb", offs)
         cen_sb = load_list("cen_sb", cen)
         for q in range(4):
-            nc.sync.dma_start(xs_all[32 * q : 32 * q + 4 * PASSES, :].bitcast(I32), x_scales[:, 4 * q : 4 * q + 4, :].bitcast(I32))
+            queue = nc.sync if q < 2 else nc.scalar
+            queue.dma_start(xs_all[32 * q : 32 * q + 4 * PASSES, :].bitcast(I32), x_scales[:, 4 * q : 4 * q + 4, :].bitcast(I32))
+        gate_col = keep.tile([P, D, 8], F32, name="gate_col")
+        nc.scalar.dma_start(gate_col[:, :, 0:4], gate[:, 0, :].rearrange("d (p b) -> p d b", b=4))
         xw_all = [None, None]
         w1_raw = {}
         xw_all[0] = load_words("xw_all0", x_words[0])
-        for g in range(PASSES):
-            w1_raw[0, g] = load_w1(g, 0, P)[:]
+        w1_raw[0, 0] = load_w1(0, 0, P)[:]
         xw_all[1] = load_words("xw_all1", x_words[1])
+        w1_raw[0, 1] = load_w1(1, 0, P)[:]
+        w1_raw[1, 0] = load_w1(0, P, 2 * P, "raw1")[:]
         pos_sb = [load_list("pos%d_sb" % d, src) for d, src in enumerate((pos1, pos2, pos3))]
-        for g in range(PASSES):
-            w1_raw[1, g] = load_w1(g, P, 2 * P)[:]
+        w1_raw[1, 1] = load_w1(1, P, 2 * P)[:]
         for g in range(PASSES):
             both = load_w1(g, 2 * P, 4 * P)
             w1_raw[2, g] = both[:, :, 0:P]
@@ -91,43 +91,48 @@ def tile_picked_lapl_none_p_kernel(tc, x_words, x_scales, w1, w2_words, w2_scale
 
         w1_codes, w1_planes, w1_bf = {}, {}, {}
 
-        def round_w1(a, g):
-            if a not in w1_bf:
-                w1_bf[a] = keep.tile([P, PASSES, P * PACK], BF16, name="w1_bf%d" % a, tag="stage%d" % a, align_bytes=64)
-                w1_codes[a] = keep.tile([P, PASSES, P], U32, name="w1_codes%d" % a, align_bytes=64)
-                w1_planes[a] = keep.tile([P, PASSES, P], U8, name="w1_planes%d" % a, align_bytes=64)
-            nc.scalar.activation(
-                w1_bf[a][:, g, :].rearrange("p (c i j) -> p c j i", i=4, j=PACK),
-                w1_raw[a, g].rearrange("p j (c i) -> p c j i", i=4),
-                COPY,
-            )
+        def round_w1(a, g0, g1):
+            n = g1 - g0
+            w1_bf[a, g0] = keep.tile([P, n, P * PACK], BF16, name="w1_bf%d_%d" % (a, g0), tag="stage%d_%d" % (a, g0), align_bytes=64)
+            for g in range(g0, g1):
+                nc.scalar.activation(
+                    w1_bf[a, g0][:, g - g0, :].rearrange("p (c i j) -> p c j i", i=4, j=PACK),
+                    w1_raw[a, g].rearrange("p j (c i) -> p c j i", i=4),
+                    COPY,
+                )
 
         def quantize_w1(a, g0, g1):
-            nc.vector.quantize_mx(
-                out=w1_codes[a][:, g0:g1, :].rearrange("p g c -> p (g c)").bitcast(FP8X4),
-                scales=w1_planes[a][:, g0:g1, :].rearrange("p g c -> p (g c)"),
-                in_=w1_bf[a][:, g0:g1, :].rearrange("p g c -> p (g c)"),
-            )
+            n = g1 - g0
+            codes = keep.tile([P, n * P], U32, name="w1_codes%d_%d" % (a, g0), align_bytes=64)
+            planes = keep.tile([P, n * P], U8, name="w1_planes%d_%d" % (a, g0), align_bytes=64)
+            nc.vector.quantize_mx(out=codes[:].bitcast(FP8X4), scales=planes[:], in_=w1_bf[a, g0][:].rearrange("p g c -> p (g c)"))
+            for g in range(g0, g1):
+                w1_codes[a, g] = codes[:, (g - g0) * P : (g - g0 + 1) * P]
+                w1_planes[a, g] = planes[:, (g - g0) * P : (g - g0 + 1) * P]
 
         xs = keep.tile([P, S], U8, name="xs", align_bytes=64)
         nc.vector.tensor_copy(xs[:], xs_all[:].indirect(offs_sb[:]))
-        xw = [keep.tile([P, S], U32, name="xw0", align_bytes=64)]
-        nc.vector.tensor_copy(xw[0][:], xw_all[0][:].indirect(offs_sb[:]))
-        for g in range(PASSES):
-            round_w1(0, g)
-        quantize_w1(0, 0, PASSES)
-        xw.append(keep.tile([P, S], U32, name="xw1", tag="stage0", align_bytes=64))
-        for c0, c1 in FIRST_PIECES:
-            nc.vector.tensor_copy(xw[1][:, c0:c1], xw_all[1][:].indirect(offs_sb[:, c0 // 16 : c1 // 16]))
+        xw0 = keep.tile([P, S], U32, name="xw0", align_bytes=64)
+        nc.vector.tensor_copy(xw0[:], xw_all[0][:].indirect(offs_sb[:]))
+        xw = {(0, 0): xw0[:, 0:BANK], (0, 1): xw0[:, BANK:S]}
+        for n in range(2):
+            round_w1(0, n, n + 1)
+            quantize_w1(0, n, n + 1)
+            half = keep.tile([P, BANK], U32, name="xw1_%d" % n, tag="stage0_%d" % n, align_bytes=64)
+            xw[1, n] = half[:]
+            for c0, c1 in FIRST_PIECES:
+                if c0 // BANK == n:
+                    nc.vector.tensor_copy(half[:, c0 - n * BANK : c1 - n * BANK], xw_all[1][:].indirect(offs_sb[:, c0 // 16 : c1 // 16]))
 
         bank_use = []
 
         def one_pass(acc, a, g, c0, c1):
+            n = c0 // BANK
             nc.tensor.matmul_mx(
                 out=acc[:],
-                lhsT=w1_codes[a][:, g, :].bitcast(FP8X4),
-                lhsT_scale=w1_planes[a][:, g, :],
-                rhs=xw[g][:, c0:c1].bitcast(FP8X4),
+                lhsT=w1_codes[a, g].bitcast(FP8X4),
+                lhsT_scale=w1_planes[a, g],
+                rhs=xw[g, n][:, c0 - n * BANK : c1 - n * BANK].bitcast(FP8X4),
                 rhs_scale=xs[4 * g : P, c0:c1],
                 start=(g == 0),
                 stop=(g == PASSES - 1),
@@ -137,8 +142,8 @@ def tile_picked_lapl_none_p_kernel(tc, x_words, x_scales, w1, w2_words, w2_scale
             bank_use.append(name)
             return psum.tile(shape, F32, name=name, tag="mm%d" % (len(bank_use) % 4))
 
-        def first_product(a, pieces):
-            h = keep.tile([P, S], F32, name="h%d" % a)
+        def first_product(a, pieces, tag=""):
+            h = keep.tile([P, S], F32, name="h%d" % a, tag=tag)
             for c0, c1 in pieces:
                 acc = bank_tile([P, c1 - c0], "acc%d_%d" % (a, c0))
                 for g in range(PASSES):
@@ -147,6 +152,7 @@ def tile_picked_lapl_none_p_kernel(tc, x_words, x_scales, w1, w2_words, w2_scale
             return h
 
         zt = [psum.tile([P, H], F32, name="zt%d" % b, tag="zt%d" % b) for b in range(BLOCKS)]
+        zt_part = {(a, b): zt[b][:, a * P : (a + 1) * P] for a in range(ROW_TILES) for b in range(BLOCKS)}
         zt_bf = [keep.tile([P, 2, P, 2], BF16, name="zt_bf%d" % b) for b in range(BLOCKS)]
 
         def laplacian(h, a, b0, b1, reuse):
@@ -158,11 +164,14 @@ def tile_picked_lapl_none_p_kernel(tc, x_words, x_scales, w1, w2_words, w2_scale
                 nc.vector.tensor_tensor(terms[d][:], h[:].indirect(pos_sb[d][:, entries]), neg_gate[d][:, cols], MULT)
             own = keep.tile([P, width], F32, name="own%d_%d" % (a, b0))
             nc.vector.tensor_tensor(own[:], h[:].indirect(cen_sb[:, entries]), terms[0][:], ADD)
+            if (a, b0) in ((3, 0), (3, 3)):
+                probe = keep.tile([P, 8], F32, name="probe%d" % b0)
+                nc.gpsimd.tensor_copy(probe[:, 0:1], own[:, 0:1])
             summands = terms[1:] + [own]
             for s, term in enumerate(summands):
                 for b in range(b0, b1):
                     nc.tensor.matmul(
-                        zt[b][:, a * P : (a + 1) * P],
+                        zt_part[a, b],
                         term[:, (b - b0) * P : (b - b0 + 1) * P],
                         ident[:],
                         start=(s == 0),
@@ -171,43 +180,65 @@ def tile_picked_lapl_none_p_kernel(tc, x_words, x_scales, w1, w2_words, w2_scale
                     )
 
         def round_z(b, a0, a1):
+            src = zt_part[a0, b] if a1 == a0 + 1 else zt[b][:, a0 * P : a1 * P]
             nc.scalar.activation(
                 zt_bf[b][:, :, 32 * a0 : 32 * a1, :],
-                zt[b][:, a0 * P : a1 * P].rearrange("v (p u e) -> v u p e", u=2, e=2),
+                src.rearrange("v (p u e) -> v u p e", u=2, e=2),
                 COPY,
             )
 
-        def second_product(c, b0, b1):
+        def turn_back(b0, b1, tag):
             nb = b1 - b0
-            width = nb * P
-            back = bank_tile([P, nb, 2, P], "back%d" % c)
+            back = psum.tile([P, nb, 2, P], F32, name="back%d" % b0, tag=tag)
             for b in range(b0, b1):
                 round_z(b, ROW_TILES - 1, ROW_TILES)
                 words = zt_bf[b][:].rearrange("v u p e -> v (u p e)").bitcast(F32)
                 for u in range(2):
                     nc.tensor.transpose(back[:, b - b0, u, :], words[:, u * P : (u + 1) * P], ident[:])
-            z_bf = keep.tile([P, width * PACK], BF16, name="z_bf%d" % c, align_bytes=64)
+            z_bf = keep.tile([P, nb * P * PACK], BF16, name="z_bf%d" % b0, align_bytes=64)
             nc.scalar.copy(z_bf[:].bitcast(F32).rearrange("p (b v u) -> p b v u", b=nb, u=2), back[:].rearrange("p b u v -> p b v u"))
-            z_codes = keep.tile([P, width], U32, name="z_codes%d" % c, align_bytes=64)
-            z_plane = keep.tile([P, width], U8, name="z_plane%d" % c, align_bytes=64)
+            return z_bf
+
+        def second_product(z_bf, b0, b1, tag):
+            width = (b1 - b0) * P
+            z_codes = keep.tile([P, width], U32, name="z_codes%d" % b0, align_bytes=64)
+            z_plane = keep.tile([P, width], U8, name="z_plane%d" % b0, align_bytes=64)
             nc.vector.quantize_mx(out=z_codes[:].bitcast(FP8X4), scales=z_plane[:], in_=z_bf[:])
-            res = bank_tile([P, width], "res%d" % c)
+            res = psum.tile([P, width], F32, name="res%d" % b0, tag=tag)
             nc.tensor.matmul_mx(out=res[:], lhsT=w2w[:].bitcast(FP8X4), lhsT_scale=w2s[:], rhs=z_codes[:].bitcast(FP8X4), rhs_scale=z_plane[:], start=True, stop=True)
-            res_sb = keep.tile([P, width], F32, name="res_sb%d" % c)
-            nc.scalar.activation(res_sb[:], res[:], COPY)
+            res_sb = keep.tile([P, width], F32, name="res_sb%d" % b0)
+            nc.vector.tensor_copy(res_sb[:], res[:])
             nc.sync.dma_start(out[:, b0 * P : b1 * P], res_sb[:])
 
-        h = first_product(0, FIRST_PIECES)
-        for a in range(ROW_TILES - 1):
-            for g in range(PASSES):
-                round_w1(a + 1, g)
-            quantize_w1(a + 1, 0, PASSES)
-            h_next = first_product(a + 1, HALVES)
-            laplacian(h, a, 0, BLOCKS, {1 if a == 0 else 0: "stage%d" % (a + 1)})
-            h = h_next
-        for b in range(BLOCKS):
-            round_z(b, 0, ROW_TILES - 1)
-        for b0, b1 in LAST_CHUNKS:
-            laplacian(h, ROW_TILES - 1, b0, b1, {})
-        for c, (b0, b1) in enumerate(LAST_CHUNKS):
-            second_product(c, b0, b1)
+        round_w1(1, 0, 1)
+        h = first_product(0, FIRST_PIECES, "raw1")
+        quantize_w1(1, 0, 1)
+        round_w1(1, 1, 2)
+        quantize_w1(1, 1, 2)
+        h_next = first_product(1, HALVES)
+        laplacian(h, 0, 0, BLOCKS, {0: "stage1_0", 1: "stage1_1"})
+        h1 = h_next
+        round_w1(2, 0, PASSES)
+        quantize_w1(2, 0, PASSES)
+        h2 = first_product(2, HALVES)
+        round_w1(3, 0, PASSES)
+        quantize_w1(3, 0, PASSES)
+        h3 = first_product(3, HALVES)
+        laplacian(h1, 1, 0, BLOCKS, {0: "stage2_0", 2: "stage3_0"})
+        round_z(3, 0, 2)
+        laplacian(h2, 2, 0, 3, {})
+        for b in range(3):
+            round_z(b, 0, 3)
+        laplacian(h3, 3, 0, 2, {})
+        z01 = turn_back(0, 2, "mm2")
+        laplacian(h3, 3, 2, 3, {})
+        z2 = turn_back(2, 3, "mm3")
+        zt_part[2, 3] = psum.tile([P, P], F32, name="zt_late2", tag="mm2")[:]
+        laplacian(h2, 2, 3, 4, {})
+        round_z(3, 2, 3)
+        zt_part[3, 3] = psum.tile([P, P], F32, name="zt_late3", tag="mm3")[:]
+        laplacian(h3, 3, 3, 4, {})
+        z3 = turn_back(3, 4, "zt3")
+        second_product(z01, 0, 2, "zt0")
+        second_product(z2, 2, 3, "zt1")
+        second_product(z3, 3, 4, "zt2")

@@ -21,11 +21,16 @@ P = 128
 PACK = 4
 K_PASS = P * PACK
 PASSES = K // K_PASS
+QUADRANTS = 4
+LIST_COLUMN = 16
 BANK = 512
 ROW_TILES = H // P
 BLOCKS = V // P
-FIRST_PIECES = ((0, 512), (512, 768), (768, 1024))
-HALVES = ((0, 512), (512, 1024))
+PRODUCT_BANKS = 4
+GATE_RUN = V // P
+GATE_PAD = 8
+HALVES = ((0, BANK), (BANK, S))
+FIRST_PIECES = ((0, BANK), (BANK, BANK + BANK // 2), (BANK + BANK // 2, S))
 
 
 def tile_picked_lapl_none_p_kernel(tc, x_words, x_scales, w1, w2_words, w2_scales, gate, offs, cen, pos1, pos2, pos3, out):
@@ -34,211 +39,206 @@ def tile_picked_lapl_none_p_kernel(tc, x_words, x_scales, w1, w2_words, w2_scale
         keep = ctx.enter_context(tc.tile_pool(name="keep", bufs=1))
         psum = ctx.enter_context(tc.psum_pool(name="psum", bufs=1))
 
+        def raw_tag(a, g):
+            return "w1_raw%d_%d" % (a, g)
+
         def load_list(name, src):
-            t = keep.tile(list(src.shape), U16, name=name)
-            nc.sync.dma_start(t[:], src)
-            return t
+            tile = keep.tile(list(src.shape), U16, name=name)
+            nc.sync.dma_start(tile[:], src)
+            return tile
 
         def load_words(name, src):
-            t = keep.tile([P, src.shape[1]], U32, name=name, align_bytes=64)
-            nc.sync.dma_start(t[:].bitcast(I32), src.rearrange("p n t -> p (n t)").bitcast(I32))
-            return t
+            tile = keep.tile([P, src.shape[1]], U32, name=name, align_bytes=64)
+            nc.sync.dma_start(tile[:].bitcast(I32), src.rearrange("p n t -> p (n t)").bitcast(I32))
+            return tile
 
-        def load_w1(g, c0, c1, tag=""):
-            t = keep.tile([P, PACK, c1 - c0], F32, name="w1_raw_%d_%d" % (g, c0), tag=tag)
-            nc.sync.dma_start(t[:], w1[g * K_PASS : (g + 1) * K_PASS, c0:c1].rearrange("(p j) c -> p j c", j=PACK))
-            return t
+        w1_raw = {}
 
-        xs_all = keep.tile([P, T], U8, name="xs_all", align_bytes=64)
-        nc.gpsimd.memset(xs_all[:].bitcast(I32), 0)
+        def load_w1(a, g):
+            w1_raw[a, g] = keep.tile([P, PACK, P], F32, name=raw_tag(a, g), tag=raw_tag(a, g), align_bytes=64)
+            rows = w1[g * K_PASS : (g + 1) * K_PASS, a * P : (a + 1) * P]
+            nc.sync.dma_start(w1_raw[a, g][:], rows.rearrange("(p j) c -> p j c", j=PACK))
+
+        x_planes_all = keep.tile([P, T], U8, name="x_planes_all", align_bytes=64)
+        nc.gpsimd.memset(x_planes_all[:].bitcast(I32), 0)
         offs_sb = load_list("offs_sb", offs)
         cen_sb = load_list("cen_sb", cen)
-        for q in range(4):
-            queue = nc.sync if q < 2 else nc.scalar
-            queue.dma_start(xs_all[32 * q : 32 * q + 4 * PASSES, :].bitcast(I32), x_scales[:, 4 * q : 4 * q + 4, :].bitcast(I32))
-        gate_col = keep.tile([P, D, 8], F32, name="gate_col")
-        nc.scalar.dma_start(gate_col[:, :, 0:4], gate[:, 0, :].rearrange("d (p b) -> p d b", b=4))
-        xw_all = [None, None]
-        w1_raw = {}
-        xw_all[0] = load_words("xw_all0", x_words[0])
-        w1_raw[0, 0] = load_w1(0, 0, P)[:]
-        xw_all[1] = load_words("xw_all1", x_words[1])
-        w1_raw[0, 1] = load_w1(1, 0, P)[:]
-        w1_raw[1, 0] = load_w1(0, P, 2 * P, "raw1")[:]
-        pos_sb = [load_list("pos%d_sb" % d, src) for d, src in enumerate((pos1, pos2, pos3))]
-        w1_raw[1, 1] = load_w1(1, P, 2 * P)[:]
+        for q in range(QUADRANTS):
+            nc.sync.dma_start(x_planes_all[32 * q : 32 * q + 4 * PASSES, :].bitcast(I32), x_scales[:, 4 * q : 4 * q + 4, :].bitcast(I32))
+        gate_col = keep.tile([P, D, GATE_PAD], F32, name="gate_col")
+        nc.scalar.dma_start(gate_col[:, :, 0:GATE_RUN], gate[:, 0, :].rearrange("d (p e) -> p d e", e=GATE_RUN))
+        x_words_all = []
         for g in range(PASSES):
-            both = load_w1(g, 2 * P, 4 * P)
-            w1_raw[2, g] = both[:, :, 0:P]
-            w1_raw[3, g] = both[:, :, P : 2 * P]
-        w2w = load_words("w2w", w2_words[0])
-        w2s = keep.tile([P, N], U8, name="w2s", align_bytes=64)
-        nc.gpsimd.memset(w2s[:], 0)
-        for q in range(4):
-            nc.sync.dma_start(w2s[32 * q : 32 * q + 4, :].bitcast(I32), w2_scales[0, 4 * q : 4 * q + 4, :].bitcast(I32))
+            x_words_all.append(load_words("x_words_all%d" % g, x_words[g]))
+            load_w1(0, g)
+        load_w1(1, 0)
+        pos_sb = [load_list("pos%d_sb" % d, src) for d, src in enumerate((pos1, pos2, pos3))]
+        load_w1(1, 1)
+        for a in range(2, ROW_TILES):
+            for g in range(PASSES):
+                load_w1(a, g)
+        w2_codes = load_words("w2_codes", w2_words[0])
+        w2_plane = keep.tile([P, N], U8, name="w2_plane", align_bytes=64)
+        nc.gpsimd.memset(w2_plane[:], 0)
+        for q in range(QUADRANTS):
+            nc.sync.dma_start(w2_plane[32 * q : 32 * q + 4, :].bitcast(I32), w2_scales[0, 4 * q : 4 * q + 4, :].bitcast(I32))
 
         ident = keep.tile([P, P], F32, name="ident")
         make_identity(nc, ident[:])
 
         neg_gate = []
         for d in range(D):
-            spread = psum.tile([P, 4, P], F32, name="spread%d" % d, tag="zt%d" % d)
-            for b in range(4):
-                nc.tensor.transpose(spread[:, b, :], gate_col[:, d, b : b + 1].to_broadcast([P, P]), ident[:])
-            ng = keep.tile([P, V], F32, name="neg_gate%d" % d)
-            nc.scalar.activation(ng[:].rearrange("q (p b) -> q p b", b=4), spread[:].rearrange("q b p -> q p b"), COPY, scale=-1.0)
-            neg_gate.append(ng)
+            spread = psum.tile([P, GATE_RUN, P], F32, name="spread%d" % d, tag="targets%d" % d)
+            for e in range(GATE_RUN):
+                nc.tensor.transpose(spread[:, e, :], gate_col[:, d, e : e + 1].to_broadcast([P, P]), ident[:])
+            negated = keep.tile([P, V], F32, name="neg_gate%d" % d)
+            nc.scalar.activation(negated[:].rearrange("q (p e) -> q p e", e=GATE_RUN), spread[:].rearrange("q e p -> q p e"), COPY, scale=-1.0)
+            neg_gate.append(negated)
 
-        w1_codes, w1_planes, w1_bf = {}, {}, {}
+        w1_bf, w1_codes, w1_planes = {}, {}, {}
 
         def round_w1(a, g0, g1):
-            n = g1 - g0
-            w1_bf[a, g0] = keep.tile([P, n, P * PACK], BF16, name="w1_bf%d_%d" % (a, g0), tag="stage%d_%d" % (a, g0), align_bytes=64)
+            w1_bf[a, g0] = keep.tile([P, g1 - g0, P * PACK], BF16, name="w1_bf%d_%d" % (a, g0), align_bytes=64)
             for g in range(g0, g1):
                 nc.scalar.activation(
-                    w1_bf[a, g0][:, g - g0, :].rearrange("p (c i j) -> p c j i", i=4, j=PACK),
-                    w1_raw[a, g].rearrange("p j (c i) -> p c j i", i=4),
+                    w1_bf[a, g0][:, g - g0, :].rearrange("p (c j) -> p c j", j=PACK),
+                    w1_raw[a, g][:].rearrange("p j c -> p c j"),
                     COPY,
                 )
 
         def quantize_w1(a, g0, g1):
-            n = g1 - g0
-            codes = keep.tile([P, n * P], U32, name="w1_codes%d_%d" % (a, g0), align_bytes=64)
-            planes = keep.tile([P, n * P], U8, name="w1_planes%d_%d" % (a, g0), align_bytes=64)
+            codes = keep.tile([P, (g1 - g0) * P], U32, name="w1_codes%d_%d" % (a, g0), align_bytes=64)
+            planes = keep.tile([P, (g1 - g0) * P], U8, name="w1_planes%d_%d" % (a, g0), align_bytes=64)
             nc.vector.quantize_mx(out=codes[:].bitcast(FP8X4), scales=planes[:], in_=w1_bf[a, g0][:].rearrange("p g c -> p (g c)"))
             for g in range(g0, g1):
                 w1_codes[a, g] = codes[:, (g - g0) * P : (g - g0 + 1) * P]
                 w1_planes[a, g] = planes[:, (g - g0) * P : (g - g0 + 1) * P]
 
-        xs = keep.tile([P, S], U8, name="xs", align_bytes=64)
-        nc.vector.tensor_copy(xs[:], xs_all[:].indirect(offs_sb[:]))
-        xw0 = keep.tile([P, S], U32, name="xw0", align_bytes=64)
-        nc.vector.tensor_copy(xw0[:], xw_all[0][:].indirect(offs_sb[:]))
-        xw = {(0, 0): xw0[:, 0:BANK], (0, 1): xw0[:, BANK:S]}
-        for n in range(2):
+        x_planes = keep.tile([P, S], U8, name="x_planes", align_bytes=64)
+        nc.vector.tensor_copy(x_planes[:], x_planes_all[:].indirect(offs_sb[:]))
+        x_first = keep.tile([P, S], U32, name="x_first", align_bytes=64)
+        nc.vector.tensor_copy(x_first[:], x_words_all[0][:].indirect(offs_sb[:]))
+        x_codes = {(0, n): x_first[:, c0:c1] for n, (c0, c1) in enumerate(HALVES)}
+        for n in range(len(HALVES)):
             round_w1(0, n, n + 1)
             quantize_w1(0, n, n + 1)
-            half = keep.tile([P, BANK], U32, name="xw1_%d" % n, tag="stage0_%d" % n, align_bytes=64)
-            xw[1, n] = half[:]
+            half = keep.tile([P, BANK], U32, name="x_second%d" % n, tag=raw_tag(0, n), align_bytes=64)
+            x_codes[1, n] = half[:]
             for c0, c1 in FIRST_PIECES:
                 if c0 // BANK == n:
-                    nc.vector.tensor_copy(half[:, c0 - n * BANK : c1 - n * BANK], xw_all[1][:].indirect(offs_sb[:, c0 // 16 : c1 // 16]))
+                    entries = offs_sb[:, c0 // LIST_COLUMN : c1 // LIST_COLUMN]
+                    nc.vector.tensor_copy(half[:, c0 - n * BANK : c1 - n * BANK], x_words_all[1][:].indirect(entries))
 
-        bank_use = []
-
-        def one_pass(acc, a, g, c0, c1):
-            n = c0 // BANK
-            nc.tensor.matmul_mx(
-                out=acc[:],
-                lhsT=w1_codes[a, g].bitcast(FP8X4),
-                lhsT_scale=w1_planes[a, g],
-                rhs=xw[g, n][:, c0 - n * BANK : c1 - n * BANK].bitcast(FP8X4),
-                rhs_scale=xs[4 * g : P, c0:c1],
-                start=(g == 0),
-                stop=(g == PASSES - 1),
-            )
-
-        def bank_tile(shape, name):
-            bank_use.append(name)
-            return psum.tile(shape, F32, name=name, tag="mm%d" % (len(bank_use) % 4))
+        pieces_made = []
 
         def first_product(a, pieces, tag=""):
-            h = keep.tile([P, S], F32, name="h%d" % a, tag=tag)
+            h = keep.tile([P, S], F32, name="h%d" % a, tag=tag, align_bytes=64)
             for c0, c1 in pieces:
-                acc = bank_tile([P, c1 - c0], "acc%d_%d" % (a, c0))
+                pieces_made.append((a, c0))
+                acc = psum.tile([P, c1 - c0], F32, name="acc%d_%d" % (a, c0), tag="product%d" % (len(pieces_made) % PRODUCT_BANKS))
+                n = c0 // BANK
                 for g in range(PASSES):
-                    one_pass(acc, a, g, c0, c1)
+                    nc.tensor.matmul_mx(
+                        out=acc[:],
+                        lhsT=w1_codes[a, g].bitcast(FP8X4),
+                        lhsT_scale=w1_planes[a, g],
+                        rhs=x_codes[g, n][:, c0 - n * BANK : c1 - n * BANK].bitcast(FP8X4),
+                        rhs_scale=x_planes[4 * g : P, c0:c1],
+                        start=(g == 0),
+                        stop=(g == PASSES - 1),
+                    )
                 nc.scalar.activation(h[:, c0:c1], acc[:], COPY)
             return h
 
-        zt = [psum.tile([P, H], F32, name="zt%d" % b, tag="zt%d" % b) for b in range(BLOCKS)]
+        zt = [psum.tile([P, H], F32, name="zt%d" % b, tag="targets%d" % b) for b in range(BLOCKS)]
         zt_part = {(a, b): zt[b][:, a * P : (a + 1) * P] for a in range(ROW_TILES) for b in range(BLOCKS)}
         zt_bf = [keep.tile([P, 2, P, 2], BF16, name="zt_bf%d" % b) for b in range(BLOCKS)]
 
-        def laplacian(h, a, b0, b1, reuse):
+        def laplacian(h, a, b0, b1, tags):
             width = (b1 - b0) * P
-            cols = slice(b0 * P, b1 * P)
-            entries = slice(b0 * P // 16, b1 * P // 16)
-            terms = [keep.tile([P, width], F32, name="term%d_%d_%d" % (a, b0, d), tag=reuse.get(d, ""), align_bytes=64) for d in range(D)]
+            entries = slice(b0 * P // LIST_COLUMN, b1 * P // LIST_COLUMN)
+            terms = [keep.tile([P, width], F32, name="term%d_%d_%d" % (a, b0, d), tag=tags.get(d, ""), align_bytes=64) for d in range(D)]
             for d in range(D):
-                nc.vector.tensor_tensor(terms[d][:], h[:].indirect(pos_sb[d][:, entries]), neg_gate[d][:, cols], MULT)
+                nc.vector.tensor_tensor(terms[d][:], h[:].indirect(pos_sb[d][:, entries]), neg_gate[d][:, b0 * P : b1 * P], MULT)
             own = keep.tile([P, width], F32, name="own%d_%d" % (a, b0))
             nc.vector.tensor_tensor(own[:], h[:].indirect(cen_sb[:, entries]), terms[0][:], ADD)
-            if (a, b0) in ((3, 0), (3, 3)):
-                probe = keep.tile([P, 8], F32, name="probe%d" % b0)
-                nc.gpsimd.tensor_copy(probe[:, 0:1], own[:, 0:1])
             summands = terms[1:] + [own]
-            for s, term in enumerate(summands):
+            for s, summand in enumerate(summands):
                 for b in range(b0, b1):
                     nc.tensor.matmul(
                         zt_part[a, b],
-                        term[:, (b - b0) * P : (b - b0 + 1) * P],
+                        summand[:, (b - b0) * P : (b - b0 + 1) * P],
                         ident[:],
                         start=(s == 0),
                         stop=(s == len(summands) - 1),
                         is_transpose=True,
                     )
 
-        def round_z(b, a0, a1):
-            src = zt_part[a0, b] if a1 == a0 + 1 else zt[b][:, a0 * P : a1 * P]
+        def round_z(b, a0, summed):
+            p0 = a0 * P // PACK
             nc.scalar.activation(
-                zt_bf[b][:, :, 32 * a0 : 32 * a1, :],
-                src.rearrange("v (p u e) -> v u p e", u=2, e=2),
+                zt_bf[b][:, :, p0 : p0 + summed.shape[1] // PACK, :],
+                summed.rearrange("v (p u e) -> v u p e", u=2, e=2),
                 COPY,
             )
 
         def turn_back(b0, b1, tag):
-            nb = b1 - b0
-            back = psum.tile([P, nb, 2, P], F32, name="back%d" % b0, tag=tag)
+            back = psum.tile([P, b1 - b0, 2, P], F32, name="back%d" % b0, tag=tag)
             for b in range(b0, b1):
-                round_z(b, ROW_TILES - 1, ROW_TILES)
                 words = zt_bf[b][:].rearrange("v u p e -> v (u p e)").bitcast(F32)
                 for u in range(2):
                     nc.tensor.transpose(back[:, b - b0, u, :], words[:, u * P : (u + 1) * P], ident[:])
-            z_bf = keep.tile([P, nb * P * PACK], BF16, name="z_bf%d" % b0, align_bytes=64)
-            nc.scalar.copy(z_bf[:].bitcast(F32).rearrange("p (b v u) -> p b v u", b=nb, u=2), back[:].rearrange("p b u v -> p b v u"))
+            z_bf = keep.tile([P, (b1 - b0) * P * PACK], BF16, name="z_bf%d" % b0, align_bytes=64)
+            nc.scalar.copy(z_bf[:].bitcast(F32).rearrange("p (b v u) -> p b v u", b=b1 - b0, u=2), back[:].rearrange("p b u v -> p b v u"))
             return z_bf
 
-        def second_product(z_bf, b0, b1, tag):
-            width = (b1 - b0) * P
-            z_codes = keep.tile([P, width], U32, name="z_codes%d" % b0, align_bytes=64)
-            z_plane = keep.tile([P, width], U8, name="z_plane%d" % b0, align_bytes=64)
+        def second_product(res, z_bf, b0):
+            z_codes = keep.tile([P, res.shape[1]], U32, name="z_codes%d" % b0, align_bytes=64)
+            z_plane = keep.tile([P, res.shape[1]], U8, name="z_plane%d" % b0, align_bytes=64)
             nc.vector.quantize_mx(out=z_codes[:].bitcast(FP8X4), scales=z_plane[:], in_=z_bf[:])
-            res = psum.tile([P, width], F32, name="res%d" % b0, tag=tag)
-            nc.tensor.matmul_mx(out=res[:], lhsT=w2w[:].bitcast(FP8X4), lhsT_scale=w2s[:], rhs=z_codes[:].bitcast(FP8X4), rhs_scale=z_plane[:], start=True, stop=True)
-            res_sb = keep.tile([P, width], F32, name="res_sb%d" % b0)
-            nc.vector.tensor_copy(res_sb[:], res[:])
-            nc.sync.dma_start(out[:, b0 * P : b1 * P], res_sb[:])
+            nc.tensor.matmul_mx(
+                out=res, lhsT=w2_codes[:].bitcast(FP8X4), lhsT_scale=w2_plane[:], rhs=z_codes[:].bitcast(FP8X4), rhs_scale=z_plane[:], start=True, stop=True
+            )
 
-        round_w1(1, 0, 1)
-        h = first_product(0, FIRST_PIECES, "raw1")
-        quantize_w1(1, 0, 1)
-        round_w1(1, 1, 2)
-        quantize_w1(1, 1, 2)
-        h_next = first_product(1, HALVES)
-        laplacian(h, 0, 0, BLOCKS, {0: "stage1_0", 1: "stage1_1"})
-        h1 = h_next
+        def store(res, c0):
+            res_sb = keep.tile([P, res.shape[1]], F32, name="res_sb%d" % c0)
+            nc.scalar.activation(res_sb[:], res, COPY)
+            nc.sync.dma_start(out[:, c0 : c0 + res.shape[1]], res_sb[:])
+
+        h0 = first_product(0, FIRST_PIECES)
+        for g in range(PASSES):
+            round_w1(1, g, g + 1)
+            quantize_w1(1, g, g + 1)
         round_w1(2, 0, PASSES)
+        h1 = first_product(1, HALVES, raw_tag(2, 1))
+        laplacian(h0, 0, 0, BLOCKS, {1: raw_tag(1, 0), 2: raw_tag(1, 1)})
         quantize_w1(2, 0, PASSES)
         h2 = first_product(2, HALVES)
         round_w1(3, 0, PASSES)
         quantize_w1(3, 0, PASSES)
         h3 = first_product(3, HALVES)
-        laplacian(h1, 1, 0, BLOCKS, {0: "stage2_0", 2: "stage3_0"})
-        round_z(3, 0, 2)
+        laplacian(h1, 1, 0, BLOCKS, {2: raw_tag(3, 1)})
+        for b in range(BLOCKS):
+            round_z(b, 0, zt[b][:, 0 : 2 * P])
+
         laplacian(h2, 2, 0, 3, {})
-        for b in range(3):
-            round_z(b, 0, 3)
         laplacian(h3, 3, 0, 2, {})
-        z01 = turn_back(0, 2, "mm2")
+        for b in range(2):
+            round_z(b, 2, zt[b][:, 2 * P : H])
+        z_01 = turn_back(0, 2, "product2")
         laplacian(h3, 3, 2, 3, {})
-        z2 = turn_back(2, 3, "mm3")
-        zt_part[2, 3] = psum.tile([P, P], F32, name="zt_late2", tag="mm2")[:]
-        laplacian(h2, 2, 3, 4, {})
-        round_z(3, 2, 3)
-        zt_part[3, 3] = psum.tile([P, P], F32, name="zt_late3", tag="mm3")[:]
-        laplacian(h3, 3, 3, 4, {})
-        z3 = turn_back(3, 4, "zt3")
-        second_product(z01, 0, 2, "zt0")
-        second_product(z2, 2, 3, "zt1")
-        second_product(z3, 3, 4, "zt2")
+        round_z(2, 2, zt[2][:, 2 * P : H])
+        z_2 = turn_back(2, 3, "product3")
+        for a, h, tag in ((2, h2, "product2"), (3, h3, "product3")):
+            zt_part[a, 3] = psum.tile([P, P], F32, name="zt_late%d" % a, tag=tag)[:]
+            laplacian(h, a, 3, 4, {})
+            round_z(3, a, zt_part[a, 3])
+        z_3 = turn_back(3, 4, "targets3")
+
+        res_012 = psum.tile([P, 3 * P], F32, name="res_012", tag="product3")
+        second_product(res_012[:, 0 : 2 * P], z_01, 0)
+        second_product(res_012[:, 2 * P : 3 * P], z_2, 2)
+        store(res_012[:], 0)
+        res_3 = psum.tile([P, P], F32, name="res_3", tag="targets0")
+        second_product(res_3[:], z_3, 3)
+        store(res_3[:], 3 * P)

@@ -30,13 +30,17 @@ PRODUCT_BANKS = 4
 GATE_RUN = V // P
 GATE_PAD = 8
 HALVES = ((0, BANK), (BANK, S))
-FIRST_PIECES = ((0, BANK), (BANK, BANK + BANK // 2), (BANK + BANK // 2, S))
+QUARTERS = tuple((c, c + S // 4) for c in range(0, S, S // 4))
+LAST_PIECE = 3 * S // 4
+LATER_PIECES = ((0, BANK), (BANK, LAST_PIECE), (LAST_PIECE, S))
+SECOND_ROWS = 8
 
 
 def tile_picked_lapl_none_p_kernel(tc, x_words, x_scales, w1, w2_words, w2_scales, gate, offs, cen, pos1, pos2, pos3, out):
     nc = tc.nc
     with ExitStack() as ctx:
         keep = ctx.enter_context(tc.tile_pool(name="keep", bufs=1))
+        shared = ctx.enter_context(tc.tile_pool(name="shared", bufs=1))
         psum = ctx.enter_context(tc.psum_pool(name="psum", bufs=1))
 
         def raw_tag(a, g):
@@ -47,42 +51,39 @@ def tile_picked_lapl_none_p_kernel(tc, x_words, x_scales, w1, w2_words, w2_scale
             nc.sync.dma_start(tile[:], src)
             return tile
 
-        def load_words(name, src):
-            tile = keep.tile([P, src.shape[1]], U32, name=name, align_bytes=64)
+        def load_words(name, src, tag="", offset=None):
+            if offset is None:
+                tile = keep.tile([P, src.shape[1]], U32, name=name, tag=tag or name, align_bytes=64)
+            else:
+                tile = shared.tile([P, src.shape[1]], U32, name=name, offset=offset, align_bytes=64)
             nc.sync.dma_start(tile[:].bitcast(I32), src.rearrange("p n t -> p (n t)").bitcast(I32))
             return tile
 
         w1_raw = {}
 
-        def load_w1(a, g):
-            w1_raw[a, g] = keep.tile([P, PACK, P], F32, name=raw_tag(a, g), tag=raw_tag(a, g), align_bytes=64)
-            rows = w1[g * K_PASS : (g + 1) * K_PASS, a * P : (a + 1) * P]
-            nc.sync.dma_start(w1_raw[a, g][:], rows.rearrange("(p j) c -> p j c", j=PACK))
+        def load_w1(a0, a1, g, offset):
+            raw = shared.tile([P, PACK, (a1 - a0) * P], F32, name=raw_tag(a0, g), offset=offset)
+            rows = w1[g * K_PASS : (g + 1) * K_PASS, a0 * P : a1 * P]
+            nc.sync.dma_start(raw[:], rows.rearrange("(p j) c -> p j c", j=PACK))
+            for a in range(a0, a1):
+                w1_raw[a, g] = raw[:, :, (a - a0) * P : (a - a0 + 1) * P]
 
-        x_planes_all = keep.tile([P, T], U8, name="x_planes_all", align_bytes=64)
-        nc.gpsimd.memset(x_planes_all[:].bitcast(I32), 0)
+        x_planes_all = shared.tile([P, T], U8, name="x_planes_all", offset=1024)
         offs_sb = load_list("offs_sb", offs)
+        nc.sync.dma_start(x_planes_all[0:32, :].bitcast(I32), x_scales.rearrange("g r t -> (g r) t").bitcast(I32))
+        nc.vector.memset(x_planes_all[32:64, :].bitcast(I32), 0)
+        nc.vector.memset(x_planes_all[64:P, :].bitcast(I32), 0)
+        x_words_all = [load_words("x_words_all0", x_words[0], offset=8192)]
+        load_w1(0, 1, 0, 5120)
         cen_sb = load_list("cen_sb", cen)
-        for q in range(QUADRANTS):
-            nc.sync.dma_start(x_planes_all[32 * q : 32 * q + 4 * PASSES, :].bitcast(I32), x_scales[:, 4 * q : 4 * q + 4, :].bitcast(I32))
-        gate_col = keep.tile([P, D, GATE_PAD], F32, name="gate_col")
-        nc.scalar.dma_start(gate_col[:, :, 0:GATE_RUN], gate[:, 0, :].rearrange("d (p e) -> p d e", e=GATE_RUN))
-        x_words_all = []
-        for g in range(PASSES):
-            x_words_all.append(load_words("x_words_all%d" % g, x_words[g]))
-            load_w1(0, g)
-        load_w1(1, 0)
         pos_sb = [load_list("pos%d_sb" % d, src) for d, src in enumerate((pos1, pos2, pos3))]
-        load_w1(1, 1)
-        for a in range(2, ROW_TILES):
-            for g in range(PASSES):
-                load_w1(a, g)
-        w2_codes = load_words("w2_codes", w2_words[0])
-        w2_plane = keep.tile([P, N], U8, name="w2_plane", align_bytes=64)
-        nc.gpsimd.memset(w2_plane[:], 0)
-        for q in range(QUADRANTS):
-            nc.sync.dma_start(w2_plane[32 * q : 32 * q + 4, :].bitcast(I32), w2_scales[0, 4 * q : 4 * q + 4, :].bitcast(I32))
+        gate_col = keep.tile([P, D, GATE_PAD], F32, name="gate_col")
+        nc.gpsimd.dma_start(gate_col[:, :, 0:GATE_RUN], gate[:, 0, :].rearrange("d (p e) -> p d e", e=GATE_RUN))
+        x_words_all.append(load_words("x_words_all1", x_words[1]))
 
+        x_plane = [keep.tile([P, S], U8, name="x_plane%d" % g, align_bytes=64) for g in range(PASSES)]
+        for g in range(PASSES):
+            nc.gpsimd.memset(x_plane[g][:].bitcast(I32), 0)
         ident = keep.tile([P, P], F32, name="ident")
         make_identity(nc, ident[:])
 
@@ -97,17 +98,17 @@ def tile_picked_lapl_none_p_kernel(tc, x_words, x_scales, w1, w2_words, w2_scale
 
         w1_bf, w1_codes, w1_planes = {}, {}, {}
 
-        def round_w1(a, g0, g1):
-            w1_bf[a, g0] = keep.tile([P, g1 - g0, P * PACK], BF16, name="w1_bf%d_%d" % (a, g0), align_bytes=64)
+        def round_w1(a, g0, g1, tag=""):
+            w1_bf[a, g0] = keep.tile([P, g1 - g0, P * PACK], BF16, name="w1_bf%d_%d" % (a, g0), tag=tag or "w1_bf%d_%d" % (a, g0), align_bytes=64)
             for g in range(g0, g1):
                 nc.scalar.activation(
                     w1_bf[a, g0][:, g - g0, :].rearrange("p (c j) -> p c j", j=PACK),
-                    w1_raw[a, g][:].rearrange("p j c -> p c j"),
+                    w1_raw[a, g].rearrange("p j c -> p c j"),
                     COPY,
                 )
 
         def quantize_w1(a, g0, g1):
-            codes = keep.tile([P, (g1 - g0) * P], U32, name="w1_codes%d_%d" % (a, g0), align_bytes=64)
+            codes = keep.tile([P, (g1 - g0) * P], U32, name="w1_codes%d_%d" % (a, g0), tag="w1_codes%d_%d" % (a, g0), align_bytes=64)
             planes = keep.tile([P, (g1 - g0) * P], U8, name="w1_planes%d_%d" % (a, g0), align_bytes=64)
             nc.vector.quantize_mx(out=codes[:].bitcast(FP8X4), scales=planes[:], in_=w1_bf[a, g0][:].rearrange("p g c -> p (g c)"))
             for g in range(g0, g1):
@@ -116,38 +117,70 @@ def tile_picked_lapl_none_p_kernel(tc, x_words, x_scales, w1, w2_words, w2_scale
 
         x_planes = keep.tile([P, S], U8, name="x_planes", align_bytes=64)
         nc.vector.tensor_copy(x_planes[:], x_planes_all[:].indirect(offs_sb[:]))
+
+        def place_rows(g, q):
+            rows = x_planes[16 * g + 4 * q : 16 * g + 4 * q + 4, :]
+            nc.sync.dma_start(x_plane[g][32 * q : 32 * q + 4, :].bitcast(I32), rows.bitcast(I32))
+
+        for n in range(6):
+            place_rows(n // QUADRANTS, n % QUADRANTS)
+        load_w1(0, 1, 1, 0)
+        place_rows(1, 2)
+        place_rows(1, 3)
+        load_w1(1, 2, 0, 2048)
         x_first = keep.tile([P, S], U32, name="x_first", align_bytes=64)
         nc.vector.tensor_copy(x_first[:], x_words_all[0][:].indirect(offs_sb[:]))
-        x_codes = {(0, n): x_first[:, c0:c1] for n, (c0, c1) in enumerate(HALVES)}
-        for n in range(len(HALVES)):
-            round_w1(0, n, n + 1)
-            quantize_w1(0, n, n + 1)
-            half = keep.tile([P, BANK], U32, name="x_second%d" % n, tag=raw_tag(0, n), align_bytes=64)
-            x_codes[1, n] = half[:]
-            for c0, c1 in FIRST_PIECES:
-                if c0 // BANK == n:
-                    entries = offs_sb[:, c0 // LIST_COLUMN : c1 // LIST_COLUMN]
-                    nc.vector.tensor_copy(half[:, c0 - n * BANK : c1 - n * BANK], x_words_all[1][:].indirect(entries))
+        round_w1(0, 0, 1)
+        load_w1(1, 2, 1, 8192)
+        load_w1(2, 3, 0, 10240)
+        load_w1(2, 3, 1, 12288)
+        load_w1(3, 4, 0, 4096)
+        load_w1(3, 4, 1, 6144)
+        quantize_w1(0, 0, 1)
+        w2_plane = keep.tile([P, N], U8, name="w2_plane", tag="w1_bf0_0", align_bytes=64)
+        nc.gpsimd.memset(w2_plane[:], 0)
+        for q in range(QUADRANTS):
+            nc.sync.dma_start(w2_plane[32 * q : 32 * q + 4, :].bitcast(I32), w2_scales[0, 4 * q : 4 * q + 4, :].bitcast(I32))
+        x_second = keep.tile([P, LAST_PIECE], U32, name="x_second", align_bytes=64)
+        nc.vector.tensor_copy(x_second[:], x_words_all[1][:].indirect(offs_sb[:, 0 : LAST_PIECE // LIST_COLUMN]))
+        round_w1(0, 1, 2)
+        quantize_w1(0, 1, 2)
+        x_last = shared.tile([P, S - LAST_PIECE], U32, name="x_last", offset=0, align_bytes=64)
+        nc.vector.tensor_copy(x_last[:], x_words_all[1][:].indirect(offs_sb[:, LAST_PIECE // LIST_COLUMN : S // LIST_COLUMN]))
+        w2_codes = load_words("w2_codes", w2_words[0], "x_words_all1")
+
+        def x_codes(g, c0, c1):
+            if g == 0:
+                return x_first[:, c0:c1]
+            return x_second[:, c0:c1] if c1 <= LAST_PIECE else x_last[:, c0 - LAST_PIECE : c1 - LAST_PIECE]
 
         pieces_made = []
 
-        def first_product(a, pieces, tag=""):
-            h = keep.tile([P, S], F32, name="h%d" % a, tag=tag, align_bytes=64)
+        def first_product(a, pieces, offset=None):
+            if offset is None:
+                h = keep.tile([P, S], F32, name="h%d" % a, align_bytes=64)
+            else:
+                h = shared.tile([P, S], F32, name="h%d" % a, offset=offset, align_bytes=64)
+            accs = []
             for c0, c1 in pieces:
                 pieces_made.append((a, c0))
-                acc = psum.tile([P, c1 - c0], F32, name="acc%d_%d" % (a, c0), tag="product%d" % (len(pieces_made) % PRODUCT_BANKS))
-                n = c0 // BANK
-                for g in range(PASSES):
+                accs.append(psum.tile([P, c1 - c0], F32, name="acc%d_%d" % (a, c0), tag="product%d" % (len(pieces_made) % PRODUCT_BANKS)))
+            for g in range(PASSES):
+                for acc, (c0, c1) in zip(accs, pieces):
                     nc.tensor.matmul_mx(
                         out=acc[:],
                         lhsT=w1_codes[a, g].bitcast(FP8X4),
                         lhsT_scale=w1_planes[a, g],
-                        rhs=x_codes[g, n][:, c0 - n * BANK : c1 - n * BANK].bitcast(FP8X4),
-                        rhs_scale=x_planes[4 * g : P, c0:c1],
+                        rhs=x_codes(g, c0, c1).bitcast(FP8X4),
+                        rhs_scale=x_plane[g][:, c0:c1],
                         start=(g == 0),
                         stop=(g == PASSES - 1),
                     )
-                nc.scalar.activation(h[:, c0:c1], acc[:], COPY)
+            for acc, (c0, c1) in zip(accs, pieces):
+                if (a, c0) == (0, S // 2):
+                    nc.vector.tensor_copy(h[:, c0:c1], acc[:])
+                else:
+                    nc.scalar.activation(h[:, c0:c1], acc[:], COPY)
             return h
 
         zt = [psum.tile([P, H], F32, name="zt%d" % b, tag="targets%d" % b) for b in range(BLOCKS)]
@@ -157,12 +190,15 @@ def tile_picked_lapl_none_p_kernel(tc, x_words, x_scales, w1, w2_words, w2_scale
         def laplacian(h, a, b0, b1, tags):
             width = (b1 - b0) * P
             entries = slice(b0 * P // LIST_COLUMN, b1 * P // LIST_COLUMN)
-            terms = [keep.tile([P, width], F32, name="term%d_%d_%d" % (a, b0, d), tag=tags.get(d, ""), align_bytes=64) for d in range(D)]
+            terms = [
+                shared.tile([P, width], F32, name="term%d_%d_%d" % (a, b0, d), offset=tags[d]) if d in tags else keep.tile([P, width], F32, name="term%d_%d_%d" % (a, b0, d))
+                for d in range(D)
+            ]
             for d in range(D):
                 nc.vector.tensor_tensor(terms[d][:], h[:].indirect(pos_sb[d][:, entries]), neg_gate[d][:, b0 * P : b1 * P], MULT)
             own = keep.tile([P, width], F32, name="own%d_%d" % (a, b0))
             nc.vector.tensor_tensor(own[:], h[:].indirect(cen_sb[:, entries]), terms[0][:], ADD)
-            summands = terms[1:] + [own]
+            summands = [terms[2], terms[1], own] if a == 0 else terms[1:] + [own]
             for s, summand in enumerate(summands):
                 for b in range(b0, b1):
                     nc.tensor.matmul(
@@ -205,19 +241,19 @@ def tile_picked_lapl_none_p_kernel(tc, x_words, x_scales, w1, w2_words, w2_scale
             nc.scalar.activation(res_sb[:], res, COPY)
             nc.sync.dma_start(out[:, c0 : c0 + res.shape[1]], res_sb[:])
 
-        h0 = first_product(0, FIRST_PIECES)
+        h0 = first_product(0, QUARTERS)
         for g in range(PASSES):
-            round_w1(1, g, g + 1)
+            round_w1(1, g, g + 1, ("w1_codes0_1", "w1_planes0_1")[g])
             quantize_w1(1, g, g + 1)
         round_w1(2, 0, PASSES)
-        h1 = first_product(1, HALVES, raw_tag(2, 1))
-        laplacian(h0, 0, 0, BLOCKS, {1: raw_tag(1, 0), 2: raw_tag(1, 1)})
+        h1 = first_product(1, LATER_PIECES, 10240)
         quantize_w1(2, 0, PASSES)
-        h2 = first_product(2, HALVES)
-        round_w1(3, 0, PASSES)
+        laplacian(h0, 0, 0, BLOCKS, {1: 2048, 2: 8192})
+        round_w1(3, 0, PASSES, "w1_codes1_1")
+        h2 = first_product(2, LATER_PIECES, 4096)
         quantize_w1(3, 0, PASSES)
-        h3 = first_product(3, HALVES)
-        laplacian(h1, 1, 0, BLOCKS, {2: raw_tag(3, 1)})
+        h3 = first_product(3, LATER_PIECES)
+        laplacian(h1, 1, 0, BLOCKS, {})
         for b in range(BLOCKS):
             round_z(b, 0, zt[b][:, 0 : 2 * P])
 

@@ -32,8 +32,6 @@ GATE_PAD = 8
 HALVES = ((0, BANK), (BANK, S))
 QUARTERS = tuple((c, c + S // 4) for c in range(0, S, S // 4))
 LAST_PIECE = 3 * S // 4
-LATER_PIECES = ((0, BANK), (BANK, LAST_PIECE), (LAST_PIECE, S))
-SECOND_ROWS = 8
 
 
 def tile_picked_lapl_none_p_kernel(tc, x_words, x_scales, w1, w2_words, w2_scales, gate, offs, cen, pos1, pos2, pos3, out):
@@ -141,7 +139,7 @@ def tile_picked_lapl_none_p_kernel(tc, x_words, x_scales, w1, w2_words, w2_scale
         nc.gpsimd.memset(w2_plane[:], 0)
         for q in range(QUADRANTS):
             nc.sync.dma_start(w2_plane[32 * q : 32 * q + 4, :].bitcast(I32), w2_scales[0, 4 * q : 4 * q + 4, :].bitcast(I32))
-        x_second = keep.tile([P, LAST_PIECE], U32, name="x_second", align_bytes=64)
+        x_second = shared.tile([P, LAST_PIECE], U32, name="x_second", offset=16384, align_bytes=64)
         nc.vector.tensor_copy(x_second[:], x_words_all[1][:].indirect(offs_sb[:, 0 : LAST_PIECE // LIST_COLUMN]))
         round_w1(0, 1, 2)
         quantize_w1(0, 1, 2)
@@ -166,16 +164,18 @@ def tile_picked_lapl_none_p_kernel(tc, x_words, x_scales, w1, w2_words, w2_scale
                 pieces_made.append((a, c0))
                 accs.append(psum.tile([P, c1 - c0], F32, name="acc%d_%d" % (a, c0), tag="product%d" % (len(pieces_made) % PRODUCT_BANKS)))
             for g in range(PASSES):
-                for acc, (c0, c1) in zip(accs, pieces):
-                    nc.tensor.matmul_mx(
-                        out=acc[:],
-                        lhsT=w1_codes[a, g].bitcast(FP8X4),
-                        lhsT_scale=w1_planes[a, g],
-                        rhs=x_codes(g, c0, c1).bitcast(FP8X4),
-                        rhs_scale=x_plane[g][:, c0:c1],
-                        start=(g == 0),
-                        stop=(g == PASSES - 1),
-                    )
+                for acc, (p0, p1) in zip(accs, pieces):
+                    cuts = (p0, LAST_PIECE, p1) if g == 1 and p0 < LAST_PIECE < p1 else (p0, p1)
+                    for c0, c1 in zip(cuts, cuts[1:]):
+                        nc.tensor.matmul_mx(
+                            out=acc[:, c0 - p0 : c1 - p0],
+                            lhsT=w1_codes[a, g].bitcast(FP8X4),
+                            lhsT_scale=w1_planes[a, g],
+                            rhs=x_codes(g, c0, c1).bitcast(FP8X4),
+                            rhs_scale=x_plane[g][:, c0:c1],
+                            start=(g == 0),
+                            stop=(g == PASSES - 1 and c1 == p1),
+                        )
             for acc, (c0, c1) in zip(accs, pieces):
                 if (a, c0) == (0, S // 2):
                     nc.vector.tensor_copy(h[:, c0:c1], acc[:])
@@ -185,7 +185,7 @@ def tile_picked_lapl_none_p_kernel(tc, x_words, x_scales, w1, w2_words, w2_scale
 
         zt = [psum.tile([P, H], F32, name="zt%d" % b, tag="targets%d" % b) for b in range(BLOCKS)]
         zt_part = {(a, b): zt[b][:, a * P : (a + 1) * P] for a in range(ROW_TILES) for b in range(BLOCKS)}
-        zt_bf = [keep.tile([P, 2, P, 2], BF16, name="zt_bf%d" % b) for b in range(BLOCKS)]
+        zt_bf = [shared.tile([P, 2, P, 2], BF16, name="zt_bf%d" % b, offset=(16384, 17408, 18432, 0)[b]) for b in range(BLOCKS)]
 
         def laplacian(h, a, b0, b1, tags):
             width = (b1 - b0) * P
@@ -196,7 +196,10 @@ def tile_picked_lapl_none_p_kernel(tc, x_words, x_scales, w1, w2_words, w2_scale
             ]
             for d in range(D):
                 nc.vector.tensor_tensor(terms[d][:], h[:].indirect(pos_sb[d][:, entries]), neg_gate[d][:, b0 * P : b1 * P], MULT)
-            own = keep.tile([P, width], F32, name="own%d_%d" % (a, b0))
+            if D in tags:
+                own = shared.tile([P, width], F32, name="own%d_%d" % (a, b0), offset=tags[D])
+            else:
+                own = keep.tile([P, width], F32, name="own%d_%d" % (a, b0))
             nc.vector.tensor_tensor(own[:], h[:].indirect(cen_sb[:, entries]), terms[0][:], ADD)
             summands = [terms[2], terms[1], own] if a == 0 else terms[1:] + [own]
             for s, summand in enumerate(summands):
@@ -246,14 +249,14 @@ def tile_picked_lapl_none_p_kernel(tc, x_words, x_scales, w1, w2_words, w2_scale
             round_w1(1, g, g + 1, ("w1_codes0_1", "w1_planes0_1")[g])
             quantize_w1(1, g, g + 1)
         round_w1(2, 0, PASSES)
-        h1 = first_product(1, LATER_PIECES, 10240)
+        h1 = first_product(1, HALVES)
         quantize_w1(2, 0, PASSES)
-        laplacian(h0, 0, 0, BLOCKS, {1: 2048, 2: 8192})
         round_w1(3, 0, PASSES, "w1_codes1_1")
-        h2 = first_product(2, LATER_PIECES, 4096)
+        h2 = first_product(2, HALVES)
+        laplacian(h0, 0, 0, BLOCKS, {1: 2048, 2: 8192, 3: 12288})
         quantize_w1(3, 0, PASSES)
-        h3 = first_product(3, LATER_PIECES)
-        laplacian(h1, 1, 0, BLOCKS, {})
+        h3 = first_product(3, HALVES)
+        laplacian(h1, 1, 0, BLOCKS, {2: 5120, 3: 7168})
         for b in range(BLOCKS):
             round_z(b, 0, zt[b][:, 0 : 2 * P])
 

@@ -185,7 +185,7 @@ def tile_picked_lapl_none_p_kernel(tc, x_words, x_scales, w1, w2_words, w2_scale
 
         zt = [psum.tile([P, H], F32, name="zt%d" % b, tag="targets%d" % b) for b in range(BLOCKS)]
         zt_part = {(a, b): zt[b][:, a * P : (a + 1) * P] for a in range(ROW_TILES) for b in range(BLOCKS)}
-        zt_bf = [shared.tile([P, 2, P, 2], BF16, name="zt_bf%d" % b, offset=(16384, 17408, 18432, 0)[b]) for b in range(BLOCKS)]
+        zt_bf = [shared.tile([P, 2, P, 2], BF16, name="zt_bf%d" % b, offset=(16384, 17408, 21504, 0)[b]) for b in range(BLOCKS)]
 
         def laplacian(h, a, b0, b1, tags):
             width = (b1 - b0) * P
@@ -221,14 +221,15 @@ def tile_picked_lapl_none_p_kernel(tc, x_words, x_scales, w1, w2_words, w2_scale
                 COPY,
             )
 
-        def turn_back(b0, b1, tag):
-            back = psum.tile([P, b1 - b0, 2, P], F32, name="back%d" % b0, tag=tag)
-            for b in range(b0, b1):
+        def turn_back(b0, b1, tags):
+            z_bf = keep.tile([P, (b1 - b0) * P * PACK], BF16, name="z_bf%d" % b0, align_bytes=64)
+            for b, tag in zip(range(b0, b1), tags):
+                back = psum.tile([P, 2, P], F32, name="back%d" % b, tag=tag)
                 words = zt_bf[b][:].rearrange("v u p e -> v (u p e)").bitcast(F32)
                 for u in range(2):
-                    nc.tensor.transpose(back[:, b - b0, u, :], words[:, u * P : (u + 1) * P], ident[:])
-            z_bf = keep.tile([P, (b1 - b0) * P * PACK], BF16, name="z_bf%d" % b0, align_bytes=64)
-            nc.scalar.copy(z_bf[:].bitcast(F32).rearrange("p (b v u) -> p b v u", b=b1 - b0, u=2), back[:].rearrange("p b u v -> p b v u"))
+                    nc.tensor.transpose(back[:, u, :], words[:, u * P : (u + 1) * P], ident[:])
+                block = z_bf[:, (b - b0) * P * PACK : (b - b0 + 1) * P * PACK]
+                (nc.vector.tensor_copy if b == 2 else nc.scalar.copy)(block.bitcast(F32).rearrange("p (v u) -> p v u", u=2), back[:].rearrange("p u v -> p v u"))
             return z_bf
 
         def second_product(res, z_bf, b0):
@@ -257,22 +258,27 @@ def tile_picked_lapl_none_p_kernel(tc, x_words, x_scales, w1, w2_words, w2_scale
         quantize_w1(3, 0, PASSES)
         h3 = first_product(3, HALVES)
         laplacian(h1, 1, 0, BLOCKS, {2: 5120, 3: 7168})
-        for b in range(BLOCKS):
+        for b in (0, 1, 3):
             round_z(b, 0, zt[b][:, 0 : 2 * P])
 
         laplacian(h2, 2, 0, 3, {})
-        laplacian(h3, 3, 0, 2, {})
         for b in range(2):
-            round_z(b, 2, zt[b][:, 2 * P : H])
-        z_01 = turn_back(0, 2, "product2")
+            round_z(b, 2, zt_part[2, b])
+        for b in range(2):
+            zt_part[3, b] = psum.tile([P, P], F32, name="zt_last%d" % b, tag="product%d" % b)[:]
+        laplacian(h3, 3, 0, 2, {D: 21504})
+        for b in range(2):
+            round_z(b, 3, zt_part[3, b])
+        round_z(2, 0, zt[2][:, 0 : 3 * P])
+        z_01 = turn_back(0, 2, ("product2", "product3"))
         laplacian(h3, 3, 2, 3, {})
-        round_z(2, 2, zt[2][:, 2 * P : H])
-        z_2 = turn_back(2, 3, "product3")
-        for a, h, tag in ((2, h2, "product2"), (3, h3, "product3")):
-            zt_part[a, 3] = psum.tile([P, P], F32, name="zt_late%d" % a, tag=tag)[:]
+        round_z(2, 3, zt_part[3, 2])
+        z_2 = turn_back(2, 3, ("product0",))
+        for a, h in ((2, h2), (3, h3)):
+            zt_part[a, 3] = psum.tile([P, P], F32, name="zt_late%d" % a, tag="product%d" % a)[:]
             laplacian(h, a, 3, 4, {})
             round_z(3, a, zt_part[a, 3])
-        z_3 = turn_back(3, 4, "targets3")
+        z_3 = turn_back(3, 4, ("targets3",))
 
         res_012 = psum.tile([P, 3 * P], F32, name="res_012", tag="product3")
         second_product(res_012[:, 0 : 2 * P], z_01, 0)

@@ -29,8 +29,9 @@ BLOCKS = V // P
 PRODUCT_BANKS = 4
 GATE_RUN = V // P
 GATE_PAD = 8
+LINE = 4
 HALVES = ((0, BANK), (BANK, S))
-QUARTERS = tuple((c, c + S // 4) for c in range(0, S, S // 4))
+FIRST_PIECES = ((0, 256), (256, 512), (512, 768), (768, 896), (896, 1024))
 LAST_PIECE = 3 * S // 4
 
 
@@ -76,7 +77,7 @@ def tile_picked_lapl_none_p_kernel(tc, x_words, x_scales, w1, w2_words, w2_scale
         cen_sb = load_list("cen_sb", cen)
         pos_sb = [load_list("pos%d_sb" % d, src) for d, src in enumerate((pos1, pos2, pos3))]
         gate_col = keep.tile([P, D, GATE_PAD], F32, name="gate_col")
-        nc.gpsimd.dma_start(gate_col[:, :, 0:GATE_RUN], gate[:, 0, :].rearrange("d (p e) -> p d e", e=GATE_RUN))
+        nc.scalar.dma_start(gate_col[:, :, 0:GATE_RUN], gate[:, 0, :].rearrange("d (p e) -> p d e", e=GATE_RUN))
         x_words_all.append(load_words("x_words_all1", x_words[1]))
 
         x_plane = [keep.tile([P, S], U8, name="x_plane%d" % g, align_bytes=64) for g in range(PASSES)]
@@ -100,8 +101,8 @@ def tile_picked_lapl_none_p_kernel(tc, x_words, x_scales, w1, w2_words, w2_scale
             w1_bf[a, g0] = keep.tile([P, g1 - g0, P * PACK], BF16, name="w1_bf%d_%d" % (a, g0), tag=tag or "w1_bf%d_%d" % (a, g0), align_bytes=64)
             for g in range(g0, g1):
                 nc.scalar.activation(
-                    w1_bf[a, g0][:, g - g0, :].rearrange("p (c j) -> p c j", j=PACK),
-                    w1_raw[a, g].rearrange("p j c -> p c j"),
+                    w1_bf[a, g0][:, g - g0, :].rearrange("p (c i j) -> p c j i", i=LINE, j=PACK),
+                    w1_raw[a, g].rearrange("p j (c i) -> p c j i", i=LINE),
                     COPY,
                 )
 
@@ -118,7 +119,7 @@ def tile_picked_lapl_none_p_kernel(tc, x_words, x_scales, w1, w2_words, w2_scale
 
         def place_rows(g, q):
             rows = x_planes[16 * g + 4 * q : 16 * g + 4 * q + 4, :]
-            nc.sync.dma_start(x_plane[g][32 * q : 32 * q + 4, :].bitcast(I32), rows.bitcast(I32))
+            (nc.gpsimd if (g, q) >= (1, 2) else nc.sync).dma_start(x_plane[g][32 * q : 32 * q + 4, :].bitcast(I32), rows.bitcast(I32))
 
         for n in range(6):
             place_rows(n // QUADRANTS, n % QUADRANTS)
@@ -161,8 +162,12 @@ def tile_picked_lapl_none_p_kernel(tc, x_words, x_scales, w1, w2_words, w2_scale
                 h = shared.tile([P, S], F32, name="h%d" % a, offset=offset, align_bytes=64)
             accs = []
             for c0, c1 in pieces:
-                pieces_made.append((a, c0))
-                accs.append(psum.tile([P, c1 - c0], F32, name="acc%d_%d" % (a, c0), tag="product%d" % (len(pieces_made) % PRODUCT_BANKS)))
+                if len(accs) == PRODUCT_BANKS:
+                    tag = "targets3"
+                else:
+                    pieces_made.append((a, c0))
+                    tag = "product%d" % (len(pieces_made) % PRODUCT_BANKS)
+                accs.append(psum.tile([P, c1 - c0], F32, name="acc%d_%d" % (a, c0), tag=tag))
             for g in range(PASSES):
                 for acc, (p0, p1) in zip(accs, pieces):
                     cuts = (p0, LAST_PIECE, p1) if g == 1 and p0 < LAST_PIECE < p1 else (p0, p1)
@@ -177,7 +182,7 @@ def tile_picked_lapl_none_p_kernel(tc, x_words, x_scales, w1, w2_words, w2_scale
                             stop=(g == PASSES - 1 and c1 == p1),
                         )
             for acc, (c0, c1) in zip(accs, pieces):
-                if (a, c0) == (0, S // 2):
+                if (a, c0) in ((0, 512), (0, 768)):
                     nc.vector.tensor_copy(h[:, c0:c1], acc[:])
                 else:
                     nc.scalar.activation(h[:, c0:c1], acc[:], COPY)
@@ -245,7 +250,7 @@ def tile_picked_lapl_none_p_kernel(tc, x_words, x_scales, w1, w2_words, w2_scale
             nc.scalar.activation(res_sb[:], res, COPY)
             nc.sync.dma_start(out[:, c0 : c0 + res.shape[1]], res_sb[:])
 
-        h0 = first_product(0, QUARTERS)
+        h0 = first_product(0, FIRST_PIECES)
         for g in range(PASSES):
             round_w1(1, g, g + 1, ("w1_codes0_1", "w1_planes0_1")[g])
             quantize_w1(1, g, g + 1)

@@ -121,9 +121,9 @@ def tile_picked_lapl_none_p_kernel(tc, x_words, x_scales, w1, w2_words, w2_scale
             rows = x_planes[16 * g + 4 * q : 16 * g + 4 * q + 4, :]
             (nc.gpsimd if (g, q) >= (1, 2) else nc.sync).dma_start(x_plane[g][32 * q : 32 * q + 4, :].bitcast(I32), rows.bitcast(I32))
 
+        load_w1(0, 1, 1, 0)
         for n in range(6):
             place_rows(n // QUADRANTS, n % QUADRANTS)
-        load_w1(0, 1, 1, 0)
         place_rows(1, 2)
         place_rows(1, 3)
         load_w1(1, 2, 0, 2048)

@@ -68,21 +68,21 @@ def tile_picked_lapl_none_p_kernel(tc, x_words, x_scales, w1, w2_words, w2_scale
                 w1_raw[a, g] = raw[:, :, (a - a0) * P : (a - a0 + 1) * P]
 
         x_planes_all = shared.tile([P, T], U8, name="x_planes_all", offset=1024)
-        offs_sb = load_list("offs_sb", offs)
         nc.sync.dma_start(x_planes_all[0:32, :].bitcast(I32), x_scales.rearrange("g r t -> (g r) t").bitcast(I32))
+        offs_sb = load_list("offs_sb", offs)
         nc.vector.memset(x_planes_all[32:64, :].bitcast(I32), 0)
         nc.vector.memset(x_planes_all[64:P, :].bitcast(I32), 0)
         x_words_all = [load_words("x_words_all0", x_words[0], offset=8192)]
+        gate_col = keep.tile([P, D, GATE_PAD], F32, name="gate_col")
+        nc.sync.dma_start(gate_col[:, :, 0:GATE_RUN], gate[:, 0, :].rearrange("d (p e) -> p d e", e=GATE_RUN))
         load_w1(0, 1, 0, 5120)
         cen_sb = load_list("cen_sb", cen)
         pos_sb = [load_list("pos%d_sb" % d, src) for d, src in enumerate((pos1, pos2, pos3))]
-        gate_col = keep.tile([P, D, GATE_PAD], F32, name="gate_col")
-        nc.scalar.dma_start(gate_col[:, :, 0:GATE_RUN], gate[:, 0, :].rearrange("d (p e) -> p d e", e=GATE_RUN))
         x_words_all.append(load_words("x_words_all1", x_words[1]))
 
         x_plane = [keep.tile([P, S], U8, name="x_plane%d" % g, align_bytes=64) for g in range(PASSES)]
         for g in range(PASSES):
-            nc.gpsimd.memset(x_plane[g][:].bitcast(I32), 0)
+            nc.vector.memset(x_plane[g][:].bitcast(I32), 0)
         ident = keep.tile([P, P], F32, name="ident")
         make_identity(nc, ident[:])
 
@@ -140,18 +140,22 @@ def tile_picked_lapl_none_p_kernel(tc, x_words, x_scales, w1, w2_words, w2_scale
         nc.gpsimd.memset(w2_plane[:], 0)
         for q in range(QUADRANTS):
             nc.sync.dma_start(w2_plane[32 * q : 32 * q + 4, :].bitcast(I32), w2_scales[0, 4 * q : 4 * q + 4, :].bitcast(I32))
-        x_second = shared.tile([P, LAST_PIECE], U32, name="x_second", offset=16384, align_bytes=64)
-        nc.vector.tensor_copy(x_second[:], x_words_all[1][:].indirect(offs_sb[:, 0 : LAST_PIECE // LIST_COLUMN]))
+        x_second = shared.tile([P, BANK], U32, name="x_second", offset=16384, align_bytes=64)
+        nc.vector.tensor_copy(x_second[:], x_words_all[1][:].indirect(offs_sb[:, 0 : BANK // LIST_COLUMN]))
         round_w1(0, 1, 2)
         quantize_w1(0, 1, 2)
-        x_last = shared.tile([P, S - LAST_PIECE], U32, name="x_last", offset=0, align_bytes=64)
+        x_third = shared.tile([P, LAST_PIECE - BANK], U32, name="x_third", offset=0, align_bytes=64)
+        nc.vector.tensor_copy(x_third[:], x_words_all[1][:].indirect(offs_sb[:, BANK // LIST_COLUMN : LAST_PIECE // LIST_COLUMN]))
+        x_last = shared.tile([P, S - LAST_PIECE], U32, name="x_last", offset=1024, align_bytes=64)
         nc.vector.tensor_copy(x_last[:], x_words_all[1][:].indirect(offs_sb[:, LAST_PIECE // LIST_COLUMN : S // LIST_COLUMN]))
         w2_codes = load_words("w2_codes", w2_words[0], "x_words_all1")
 
         def x_codes(g, c0, c1):
             if g == 0:
                 return x_first[:, c0:c1]
-            return x_second[:, c0:c1] if c1 <= LAST_PIECE else x_last[:, c0 - LAST_PIECE : c1 - LAST_PIECE]
+            if c1 <= BANK:
+                return x_second[:, c0:c1]
+            return x_third[:, c0 - BANK : c1 - BANK] if c1 <= LAST_PIECE else x_last[:, c0 - LAST_PIECE : c1 - LAST_PIECE]
 
         pieces_made = []
 
@@ -182,7 +186,7 @@ def tile_picked_lapl_none_p_kernel(tc, x_words, x_scales, w1, w2_words, w2_scale
                             stop=(g == PASSES - 1 and c1 == p1),
                         )
             for acc, (c0, c1) in zip(accs, pieces):
-                if (a, c0) in ((0, 512), (0, 768)):
+                if (a, c0) == (0, 768):
                     nc.vector.tensor_copy(h[:, c0:c1], acc[:])
                 else:
                     nc.scalar.activation(h[:, c0:c1], acc[:], COPY)

@@ -119,10 +119,11 @@ def tile_picked_lapl_none_p_kernel(tc, x_words, x_scales, w1, w2_words, w2_scale
 
         def place_rows(g, q):
             rows = x_planes[16 * g + 4 * q : 16 * g + 4 * q + 4, :]
-            (nc.gpsimd if (g, q) >= (1, 2) else nc.sync).dma_start(x_plane[g][32 * q : 32 * q + 4, :].bitcast(I32), rows.bitcast(I32))
+            nc.sync.dma_start(x_plane[g][32 * q : 32 * q + 4, :].bitcast(I32), rows.bitcast(I32))
 
+        place_rows(0, 0)
         load_w1(0, 1, 1, 0)
-        for n in range(6):
+        for n in range(1, 6):
             place_rows(n // QUADRANTS, n % QUADRANTS)
         place_rows(1, 2)
         place_rows(1, 3)

@@ -27,8 +27,8 @@ BANK = 512
 ROW_TILES = H // P
 BLOCKS = V // P
 PRODUCT_BANKS = 4
-GATE_RUN = V // P
-GATE_PAD = 8
+GATE_ROWS = 96
+GATE_RUN = D * V // GATE_ROWS
 LINE = 4
 HALVES = ((0, BANK), (BANK, S))
 FIRST_PIECES = ((0, 256), (256, 512), (512, 768), (768, 896), (896, 1024))
@@ -73,8 +73,9 @@ def tile_picked_lapl_none_p_kernel(tc, x_words, x_scales, w1, w2_words, w2_scale
         nc.vector.memset(x_planes_all[32:64, :].bitcast(I32), 0)
         nc.vector.memset(x_planes_all[64:P, :].bitcast(I32), 0)
         x_words_all = [load_words("x_words_all0", x_words[0], offset=8192)]
-        gate_col = keep.tile([P, D, GATE_PAD], F32, name="gate_col")
-        nc.sync.dma_start(gate_col[:, :, 0:GATE_RUN], gate[:, 0, :].rearrange("d (p e) -> p d e", e=GATE_RUN))
+        gate_col = keep.tile([P, GATE_RUN], F32, name="gate_col")
+        nc.vector.memset(gate_col[GATE_ROWS:P, :], 0.0)
+        nc.sync.dma_start(gate_col[0:GATE_ROWS, :], gate[:, 0, :].rearrange("d (m e) -> m d e", e=GATE_RUN))
         load_w1(0, 1, 0, 5120)
         cen_sb = load_list("cen_sb", cen)
         pos_sb = [load_list("pos%d_sb" % d, src) for d, src in enumerate((pos1, pos2, pos3))]
@@ -86,14 +87,17 @@ def tile_picked_lapl_none_p_kernel(tc, x_words, x_scales, w1, w2_words, w2_scale
         ident = keep.tile([P, P], F32, name="ident")
         make_identity(nc, ident[:])
 
-        neg_gate = []
-        for d in range(D):
-            spread = psum.tile([P, GATE_RUN, P], F32, name="spread%d" % d, tag="targets%d" % d)
-            for e in range(GATE_RUN):
-                nc.tensor.transpose(spread[:, e, :], gate_col[:, d, e : e + 1].to_broadcast([P, P]), ident[:])
-            negated = keep.tile([P, V], F32, name="neg_gate%d" % d)
-            nc.scalar.activation(negated[:].rearrange("q (p e) -> q p e", e=GATE_RUN), spread[:].rearrange("q e p -> q p e"), COPY, scale=-1.0)
-            neg_gate.append(negated)
+        neg_gate = keep.tile([P, D, V], F32, name="neg_gate")
+        for b in range(GATE_RUN // LINE):
+            spread = psum.tile([P, LINE, P], F32, name="spread%d" % b, tag="targets%d" % b)
+            for e in range(LINE):
+                nc.tensor.transpose(spread[:, e, :], gate_col[:, b * LINE + e : b * LINE + e + 1].to_broadcast([P, P]), ident[:])
+            nc.scalar.activation(
+                neg_gate[:].rearrange("q d (m e) -> q d m e", e=GATE_RUN)[:, :, :, b * LINE : (b + 1) * LINE],
+                spread[:, :, 0:GATE_ROWS].rearrange("q e (m d) -> q d m e", d=D),
+                COPY,
+                scale=-1.0,
+            )
 
         w1_bf, w1_codes, w1_planes = {}, {}, {}
 
@@ -195,7 +199,7 @@ def tile_picked_lapl_none_p_kernel(tc, x_words, x_scales, w1, w2_words, w2_scale
 
         zt = [psum.tile([P, H], F32, name="zt%d" % b, tag="targets%d" % b) for b in range(BLOCKS)]
         zt_part = {(a, b): zt[b][:, a * P : (a + 1) * P] for a in range(ROW_TILES) for b in range(BLOCKS)}
-        zt_bf = [shared.tile([P, 2, P, 2], BF16, name="zt_bf%d" % b, offset=(16384, 17408, 21504, 0)[b]) for b in range(BLOCKS)]
+        zt_bf = [shared.tile([P, 2, P, 2], BF16, name="zt_bf%d" % b, offset=(16384, 17408, 1024, 0)[b]) for b in range(BLOCKS)]
 
         def laplacian(h, a, b0, b1, tags):
             width = (b1 - b0) * P
@@ -205,7 +209,7 @@ def tile_picked_lapl_none_p_kernel(tc, x_words, x_scales, w1, w2_words, w2_scale
                 for d in range(D)
             ]
             for d in range(D):
-                nc.vector.tensor_tensor(terms[d][:], h[:].indirect(pos_sb[d][:, entries]), neg_gate[d][:, b0 * P : b1 * P], MULT)
+                nc.vector.tensor_tensor(terms[d][:], h[:].indirect(pos_sb[d][:, entries]), neg_gate[:, d, b0 * P : b1 * P], MULT)
             if D in tags:
                 own = shared.tile([P, width], F32, name="own%d_%d" % (a, b0), offset=tags[D])
             else:
@@ -231,16 +235,12 @@ def tile_picked_lapl_none_p_kernel(tc, x_words, x_scales, w1, w2_words, w2_scale
                 COPY,
             )
 
-        def turn_back(b0, b1, tags):
-            z_bf = keep.tile([P, (b1 - b0) * P * PACK], BF16, name="z_bf%d" % b0, align_bytes=64)
-            for b, tag in zip(range(b0, b1), tags):
-                back = psum.tile([P, 2, P], F32, name="back%d" % b, tag=tag)
-                words = zt_bf[b][:].rearrange("v u p e -> v (u p e)").bitcast(F32)
-                for u in range(2):
-                    nc.tensor.transpose(back[:, u, :], words[:, u * P : (u + 1) * P], ident[:])
-                block = z_bf[:, (b - b0) * P * PACK : (b - b0 + 1) * P * PACK]
-                (nc.vector.tensor_copy if b == 2 else nc.scalar.copy)(block.bitcast(F32).rearrange("p (v u) -> p v u", u=2), back[:].rearrange("p u v -> p v u"))
-            return z_bf
+        def turn_back(b, tag, block):
+            back = psum.tile([P, 2, P], F32, name="back%d" % b, tag=tag)
+            words = zt_bf[b][:].rearrange("v u p e -> v (u p e)").bitcast(F32)
+            for u in range(2):
+                nc.tensor.transpose(back[:, u, :], words[:, u * P : (u + 1) * P], ident[:])
+            (nc.vector.tensor_copy if b == 2 else nc.scalar.copy)(block.bitcast(F32).rearrange("p (v u) -> p v u", u=2), back[:].rearrange("p u v -> p v u"))
 
         def second_product(res, z_bf, b0):
             z_codes = keep.tile([P, res.shape[1]], U32, name="z_codes%d" % b0, align_bytes=64)
@@ -268,29 +268,30 @@ def tile_picked_lapl_none_p_kernel(tc, x_words, x_scales, w1, w2_words, w2_scale
         quantize_w1(3, 0, PASSES)
         h3 = first_product(3, HALVES)
         laplacian(h1, 1, 0, BLOCKS, {2: 5120, 3: 7168})
-        for b in (0, 1, 3):
+        for b in range(BLOCKS):
             round_z(b, 0, zt[b][:, 0 : 2 * P])
-
-        laplacian(h2, 2, 0, 3, {})
-        for b in range(2):
+        laplacian(h2, 2, 0, BLOCKS, {})
+        for b in range(BLOCKS):
             round_z(b, 2, zt_part[2, b])
-        for b in range(2):
-            zt_part[3, b] = psum.tile([P, P], F32, name="zt_last%d" % b, tag="product%d" % b)[:]
-        laplacian(h3, 3, 0, 2, {D: 21504})
+
+        laplacian(h3, 3, 0, 2, {})
         for b in range(2):
             round_z(b, 3, zt_part[3, b])
-        round_z(2, 0, zt[2][:, 0 : 3 * P])
-        z_01 = turn_back(0, 2, ("product2", "product3"))
+        z_01 = keep.tile([P, 2 * K_PASS], BF16, name="z_01", align_bytes=64)
+        turn_back(0, "product0", z_01[:, 0:K_PASS])
+        zt_part[3, 2] = psum.tile([P, P], F32, name="zt_late2", tag="targets1")[:]
         laplacian(h3, 3, 2, 3, {})
         round_z(2, 3, zt_part[3, 2])
-        z_2 = turn_back(2, 3, ("product0",))
-        for a, h in ((2, h2), (3, h3)):
-            zt_part[a, 3] = psum.tile([P, P], F32, name="zt_late%d" % a, tag="product%d" % a)[:]
-            laplacian(h, a, 3, 4, {})
-            round_z(3, a, zt_part[a, 3])
-        z_3 = turn_back(3, 4, ("targets3",))
+        turn_back(1, "product1", z_01[:, K_PASS : 2 * K_PASS])
+        zt_part[3, 3] = psum.tile([P, P], F32, name="zt_late3", tag="product0")[:]
+        laplacian(h3, 3, 3, 4, {})
+        round_z(3, 3, zt_part[3, 3])
+        z_2 = keep.tile([P, K_PASS], BF16, name="z_2", align_bytes=64)
+        turn_back(2, "product2", z_2[:])
+        z_3 = keep.tile([P, K_PASS], BF16, name="z_3", align_bytes=64)
+        turn_back(3, "product3", z_3[:])
 
-        res_012 = psum.tile([P, 3 * P], F32, name="res_012", tag="product3")
+        res_012 = psum.tile([P, 3 * P], F32, name="res_012", tag="product0")
         second_product(res_012[:, 0 : 2 * P], z_01, 0)
         second_product(res_012[:, 2 * P : 3 * P], z_2, 2)
         store(res_012[:], 0)

@@ -26,7 +26,6 @@ LIST_COLUMN = 16
 BANK = 512
 ROW_TILES = H // P
 BLOCKS = V // P
-PRODUCT_BANKS = 4
 GATE_ROWS = 96
 GATE_RUN = D * V // GATE_ROWS
 LINE = 4
@@ -112,7 +111,7 @@ def tile_picked_lapl_none_p_kernel(tc, x_words, x_scales, w1, w2_words, w2_scale
 
         def quantize_w1(a, g0, g1):
             codes = keep.tile([P, (g1 - g0) * P], U32, name="w1_codes%d_%d" % (a, g0), tag="w1_codes%d_%d" % (a, g0), align_bytes=64)
-            planes = keep.tile([P, (g1 - g0) * P], U8, name="w1_planes%d_%d" % (a, g0), align_bytes=64)
+            planes = keep.tile([P, (g1 - g0) * P], U8, name="w1_planes%d_%d" % (a, g0), tag="w1_planes%d_%d" % (a, g0), align_bytes=64)
             nc.vector.quantize_mx(out=codes[:].bitcast(FP8X4), scales=planes[:], in_=w1_bf[a, g0][:].rearrange("p g c -> p (g c)"))
             for g in range(g0, g1):
                 w1_codes[a, g] = codes[:, (g - g0) * P : (g - g0 + 1) * P]
@@ -162,34 +161,25 @@ def tile_picked_lapl_none_p_kernel(tc, x_words, x_scales, w1, w2_words, w2_scale
                 return x_second[:, c0:c1]
             return x_third[:, c0 - BANK : c1 - BANK] if c1 <= LAST_PIECE else x_last[:, c0 - LAST_PIECE : c1 - LAST_PIECE]
 
-        pieces_made = []
-
-        def first_product(a, pieces, offset=None):
-            if offset is None:
-                h = keep.tile([P, S], F32, name="h%d" % a, align_bytes=64)
-            else:
-                h = shared.tile([P, S], F32, name="h%d" % a, offset=offset, align_bytes=64)
-            accs = []
-            for c0, c1 in pieces:
-                if len(accs) == PRODUCT_BANKS:
-                    tag = "targets3"
-                else:
-                    pieces_made.append((a, c0))
-                    tag = "product%d" % (len(pieces_made) % PRODUCT_BANKS)
-                accs.append(psum.tile([P, c1 - c0], F32, name="acc%d_%d" % (a, c0), tag=tag))
-            for g in range(PASSES):
-                for acc, (p0, p1) in zip(accs, pieces):
-                    cuts = (p0, LAST_PIECE, p1) if g == 1 and p0 < LAST_PIECE < p1 else (p0, p1)
-                    for c0, c1 in zip(cuts, cuts[1:]):
-                        nc.tensor.matmul_mx(
-                            out=acc[:, c0 - p0 : c1 - p0],
-                            lhsT=w1_codes[a, g].bitcast(FP8X4),
-                            lhsT_scale=w1_planes[a, g],
-                            rhs=x_codes(g, c0, c1).bitcast(FP8X4),
-                            rhs_scale=x_plane[g][:, c0:c1],
-                            start=(g == 0),
-                            stop=(g == PASSES - 1 and c1 == p1),
-                        )
+        def first_product(a, pieces, banks):
+            h = keep.tile([P, S], F32, name="h%d" % a, align_bytes=64)
+            accs = [psum.tile([P, c1 - c0], F32, name="acc%d_%d" % (a, c0), tag=bank) for (c0, c1), bank in zip(pieces, banks)]
+            steps = [(g, n) for g in range(PASSES) for n in range(len(pieces))]
+            if a > 0:
+                steps = sorted(steps, key=lambda step: step[1])
+            for g, n in steps:
+                p0, p1 = pieces[n]
+                cuts = (p0, LAST_PIECE, p1) if g == 1 and p0 < LAST_PIECE < p1 else (p0, p1)
+                for c0, c1 in zip(cuts, cuts[1:]):
+                    nc.tensor.matmul_mx(
+                        out=accs[n][:, c0 - p0 : c1 - p0],
+                        lhsT=w1_codes[a, g].bitcast(FP8X4),
+                        lhsT_scale=w1_planes[a, g],
+                        rhs=x_codes(g, c0, c1).bitcast(FP8X4),
+                        rhs_scale=x_plane[g][:, c0:c1],
+                        start=(g == 0),
+                        stop=(g == PASSES - 1 and c1 == p1),
+                    )
             for acc, (c0, c1) in zip(accs, pieces):
                 if (a, c0) == (0, 768):
                     nc.vector.tensor_copy(h[:, c0:c1], acc[:])
@@ -197,50 +187,55 @@ def tile_picked_lapl_none_p_kernel(tc, x_words, x_scales, w1, w2_words, w2_scale
                     nc.scalar.activation(h[:, c0:c1], acc[:], COPY)
             return h
 
-        zt = [psum.tile([P, H], F32, name="zt%d" % b, tag="targets%d" % b) for b in range(BLOCKS)]
-        zt_part = {(a, b): zt[b][:, a * P : (a + 1) * P] for a in range(ROW_TILES) for b in range(BLOCKS)}
-        zt_bf = [shared.tile([P, 2, P, 2], BF16, name="zt_bf%d" % b, offset=(16384, 17408, 1024, 0)[b]) for b in range(BLOCKS)]
+        zt_bf = keep.tile([P, BLOCKS * H], BF16, name="zt_bf", align_bytes=64)
+        zt_pairs = zt_bf[:].rearrange("v (u b p e) -> v u b p e", u=2, b=BLOCKS, e=2)
+        zt_words = zt_bf[:].bitcast(F32).rearrange("v (u b p) -> v u b p", u=2, b=BLOCKS)
 
-        def laplacian(h, a, b0, b1, tags):
-            width = (b1 - b0) * P
-            entries = slice(b0 * P // LIST_COLUMN, b1 * P // LIST_COLUMN)
-            terms = [
-                shared.tile([P, width], F32, name="term%d_%d_%d" % (a, b0, d), offset=tags[d]) if d in tags else keep.tile([P, width], F32, name="term%d_%d_%d" % (a, b0, d))
-                for d in range(D)
-            ]
-            for d in range(D):
-                nc.vector.tensor_tensor(terms[d][:], h[:].indirect(pos_sb[d][:, entries]), neg_gate[:, d, b0 * P : b1 * P], MULT)
-            if D in tags:
-                own = shared.tile([P, width], F32, name="own%d_%d" % (a, b0), offset=tags[D])
-            else:
-                own = keep.tile([P, width], F32, name="own%d_%d" % (a, b0))
-            nc.vector.tensor_tensor(own[:], h[:].indirect(cen_sb[:, entries]), terms[0][:], ADD)
-            summands = [terms[2], terms[1], own] if a == 0 else terms[1:] + [own]
-            for s, summand in enumerate(summands):
-                for b in range(b0, b1):
-                    nc.tensor.matmul(
-                        zt_part[a, b],
-                        summand[:, (b - b0) * P : (b - b0 + 1) * P],
-                        ident[:],
-                        start=(s == 0),
-                        stop=(s == len(summands) - 1),
-                        is_transpose=True,
-                    )
+        def entries(b0, b1):
+            return slice(b0 * P // LIST_COLUMN, b1 * P // LIST_COLUMN)
 
-        def round_z(b, a0, summed):
-            p0 = a0 * P // PACK
-            nc.scalar.activation(
-                zt_bf[b][:, :, p0 : p0 + summed.shape[1] // PACK, :],
-                summed.rearrange("v (p u e) -> v u p e", u=2, e=2),
-                COPY,
+        def neighbour(h, a, d, b0, b1, tag=""):
+            name = "term%d_%d_%d" % (a, d, b0)
+            term = keep.tile([P, (b1 - b0) * P], F32, name=name, tag=tag or name, align_bytes=64)
+            nc.vector.tensor_tensor(term[:], h[:].indirect(pos_sb[d][:, entries(b0, b1)]), neg_gate[:, d, b0 * P : b1 * P], MULT)
+            return term[:]
+
+        def centre(h, a, tag=""):
+            own = keep.tile([P, V], F32, name="own%d" % a, tag=tag or "own%d" % a, align_bytes=64)
+            nc.scalar.activation(own[:], h[:].indirect(cen_sb[:]), COPY)
+            return own[:]
+
+        def add_turned(bank, summand, first=False, last=False):
+            count = summand.shape[1] // P
+            for n in range(count):
+                nc.tensor.matmul(
+                    bank[:, n * P : (n + 1) * P],
+                    summand[:, n * P : (n + 1) * P],
+                    ident[:],
+                    start=(first and n == 0),
+                    stop=(last and n == count - 1),
+                    is_transpose=True,
+                )
+
+        def round_z(bank, a, b0):
+            count = bank.shape[1] // P
+            rows = P // PACK
+            nc.scalar.copy(
+                zt_pairs[:, :, b0 : b0 + count, a * rows : (a + 1) * rows, :],
+                bank.rearrange("v (b p u e) -> v u b p e", b=count, u=2, e=2),
             )
 
-        def turn_back(b, tag, block):
-            back = psum.tile([P, 2, P], F32, name="back%d" % b, tag=tag)
-            words = zt_bf[b][:].rearrange("v u p e -> v (u p e)").bitcast(F32)
-            for u in range(2):
-                nc.tensor.transpose(back[:, u, :], words[:, u * P : (u + 1) * P], ident[:])
-            (nc.vector.tensor_copy if b == 2 else nc.scalar.copy)(block.bitcast(F32).rearrange("p (v u) -> p v u", u=2), back[:].rearrange("p u v -> p v u"))
+        def turn_back(b0, b1, tag):
+            back = psum.tile([P, b1 - b0, 2, P], F32, name="back%d" % b0, tag=tag)
+            for b in range(b0, b1):
+                for u in range(2):
+                    nc.tensor.transpose(back[:, b - b0, u, :], zt_words[:, u, b, :], ident[:])
+            return back
+
+        def empty_back(back, b0, copy):
+            z_bf = keep.tile([P, back.shape[1] * K_PASS], BF16, name="z_bf%d" % b0, align_bytes=64)
+            copy(z_bf[:].bitcast(F32).rearrange("p (b v u) -> p b v u", u=2, v=P), back[:].rearrange("p b u v -> p b v u"))
+            return z_bf
 
         def second_product(res, z_bf, b0):
             z_codes = keep.tile([P, res.shape[1]], U32, name="z_codes%d" % b0, align_bytes=64)
@@ -255,46 +250,56 @@ def tile_picked_lapl_none_p_kernel(tc, x_words, x_scales, w1, w2_words, w2_scale
             nc.scalar.activation(res_sb[:], res, COPY)
             nc.sync.dma_start(out[:, c0 : c0 + res.shape[1]], res_sb[:])
 
-        h0 = first_product(0, FIRST_PIECES)
-        for g in range(PASSES):
-            round_w1(1, g, g + 1, ("w1_codes0_1", "w1_planes0_1")[g])
-            quantize_w1(1, g, g + 1)
+        def sum_bank(a, tag):
+            return psum.tile([P, V], F32, name="sums%d" % a, tag=tag)[:]
+
+        h0 = first_product(0, FIRST_PIECES, ("product1", "product2", "product3", "product0", "targets3"))
+        round_w1(1, 0, PASSES, "w1_codes0_1")
+        quantize_w1(1, 0, PASSES)
+        h1 = first_product(1, HALVES, ("product1", "product2"))
+        sums = [sum_bank(0, "product1"), sum_bank(1, "targets1"), sum_bank(2, "targets2")]
         round_w1(2, 0, PASSES)
-        h1 = first_product(1, HALVES)
         quantize_w1(2, 0, PASSES)
-        round_w1(3, 0, PASSES, "w1_codes1_1")
-        h2 = first_product(2, HALVES)
-        laplacian(h0, 0, 0, BLOCKS, {1: 2048, 2: 8192, 3: 12288})
+        add_turned(sums[0], neighbour(h0, 0, 0, 0, BLOCKS), first=True)
+        add_turned(sums[0], neighbour(h0, 0, 1, 0, BLOCKS, "w1_codes0_1"))
+        add_turned(sums[0], neighbour(h0, 0, 2, 0, BLOCKS, "w1_bf2_0"))
+        own0 = centre(h0, 0, "w1_codes1_0")
+        round_w1(3, 0, PASSES, "w1_planes1_0")
+        h2 = first_product(2, HALVES, ("product3", "product0"))
+        add_turned(sums[0], own0, last=True)
+        for d in range(D):
+            add_turned(sums[1], neighbour(h1, 1, d, 0, BLOCKS), first=(d == 0))
         quantize_w1(3, 0, PASSES)
-        h3 = first_product(3, HALVES)
-        laplacian(h1, 1, 0, BLOCKS, {2: 5120, 3: 7168})
-        for b in range(BLOCKS):
-            round_z(b, 0, zt[b][:, 0 : 2 * P])
-        laplacian(h2, 2, 0, BLOCKS, {})
-        for b in range(BLOCKS):
-            round_z(b, 2, zt_part[2, b])
+        add_turned(sums[1], centre(h1, 1), last=True)
+        h3 = first_product(3, HALVES, ("targets0", "product2"))
+        for d in range(D):
+            add_turned(sums[2], neighbour(h2, 2, d, 0, BLOCKS), first=(d == 0))
+        add_turned(sums[2], centre(h2, 2), last=True)
+        own3 = centre(h3, 3)
+        for a in range(ROW_TILES - 1):
+            round_z(sums[a], a, 0)
 
-        laplacian(h3, 3, 0, 2, {})
-        for b in range(2):
-            round_z(b, 3, zt_part[3, b])
-        z_01 = keep.tile([P, 2 * K_PASS], BF16, name="z_01", align_bytes=64)
-        turn_back(0, "product0", z_01[:, 0:K_PASS])
-        zt_part[3, 2] = psum.tile([P, P], F32, name="zt_late2", tag="targets1")[:]
-        laplacian(h3, 3, 2, 3, {})
-        round_z(2, 3, zt_part[3, 2])
-        turn_back(1, "product1", z_01[:, K_PASS : 2 * K_PASS])
-        zt_part[3, 3] = psum.tile([P, P], F32, name="zt_late3", tag="product0")[:]
-        laplacian(h3, 3, 3, 4, {})
-        round_z(3, 3, zt_part[3, 3])
-        z_2 = keep.tile([P, K_PASS], BF16, name="z_2", align_bytes=64)
-        turn_back(2, "product2", z_2[:])
-        z_3 = keep.tile([P, K_PASS], BF16, name="z_3", align_bytes=64)
-        turn_back(3, "product3", z_3[:])
+        def last_unit(b0, b1, tag):
+            bank = psum.tile([P, (b1 - b0) * P], F32, name="sums3_%d" % b0, tag=tag)[:]
+            add_turned(bank, own3[:, b0 * P : b1 * P], first=True)
+            for d in range(D):
+                add_turned(bank, neighbour(h3, 3, d, b0, b1), last=(d == D - 1))
+            round_z(bank, 3, b0)
 
-        res_012 = psum.tile([P, 3 * P], F32, name="res_012", tag="product0")
+        last_unit(0, 2, "targets3")
+        last_unit(2, 3, "product3")
+        back_01 = turn_back(0, 2, "product0")
+        z_01 = empty_back(back_01, 0, nc.scalar.copy)
+        last_unit(3, 4, "targets3")
+        back_2 = turn_back(2, 3, "targets0")
+        z_2 = empty_back(back_2, 2, nc.vector.tensor_copy)
+        back_3 = turn_back(3, 4, "product2")
+        z_3 = empty_back(back_3, 3, nc.scalar.copy)
+
+        res_012 = psum.tile([P, 3 * P], F32, name="res_012", tag="product1")
         second_product(res_012[:, 0 : 2 * P], z_01, 0)
         second_product(res_012[:, 2 * P : 3 * P], z_2, 2)
         store(res_012[:], 0)
-        res_3 = psum.tile([P, P], F32, name="res_3", tag="targets0")
+        res_3 = psum.tile([P, P], F32, name="res_3", tag="targets1")
         second_product(res_3[:], z_3, 3)
         store(res_3[:], 3 * P)

@@ -100,13 +100,12 @@ def tile_picked_lapl_none_p_kernel(tc, x_words, x_scales, w1, w2_words, w2_scale
 
         w1_bf, w1_codes, w1_planes = {}, {}, {}
 
-        def round_w1(a, g0, g1, tag=""):
+        def round_w1(a, g0, g1, tag="", copy=nc.scalar.copy):
             w1_bf[a, g0] = keep.tile([P, g1 - g0, P * PACK], BF16, name="w1_bf%d_%d" % (a, g0), tag=tag or "w1_bf%d_%d" % (a, g0), align_bytes=64)
             for g in range(g0, g1):
-                nc.scalar.activation(
+                copy(
                     w1_bf[a, g0][:, g - g0, :].rearrange("p (c i j) -> p c j i", i=LINE, j=PACK),
                     w1_raw[a, g].rearrange("p j (c i) -> p c j i", i=LINE),
-                    COPY,
                 )
 
         def quantize_w1(a, g0, g1):
@@ -124,12 +123,11 @@ def tile_picked_lapl_none_p_kernel(tc, x_words, x_scales, w1, w2_words, w2_scale
             rows = x_planes[16 * g + 4 * q : 16 * g + 4 * q + 4, :]
             nc.sync.dma_start(x_plane[g][32 * q : 32 * q + 4, :].bitcast(I32), rows.bitcast(I32))
 
-        place_rows(0, 0)
+        for q in range(QUADRANTS):
+            place_rows(0, q)
         load_w1(0, 1, 1, 0)
-        for n in range(1, 6):
-            place_rows(n // QUADRANTS, n % QUADRANTS)
-        place_rows(1, 2)
-        place_rows(1, 3)
+        for q in range(QUADRANTS):
+            place_rows(1, q)
         load_w1(1, 2, 0, 2048)
         x_first = keep.tile([P, S], U32, name="x_first", align_bytes=64)
         nc.vector.tensor_copy(x_first[:], x_words_all[0][:].indirect(offs_sb[:]))
@@ -254,7 +252,7 @@ def tile_picked_lapl_none_p_kernel(tc, x_words, x_scales, w1, w2_words, w2_scale
             return psum.tile([P, V], F32, name="sums%d" % a, tag=tag)[:]
 
         h0 = first_product(0, FIRST_PIECES, ("product1", "product2", "product3", "product0", "targets3"))
-        round_w1(1, 0, PASSES, "w1_codes0_1")
+        round_w1(1, 0, PASSES, "w1_codes0_1", nc.vector.tensor_copy)
         quantize_w1(1, 0, PASSES)
         h1 = first_product(1, HALVES, ("product1", "product2"))
         sums = [sum_bank(0, "product1"), sum_bank(1, "targets1"), sum_bank(2, "targets2")]

@@ -192,11 +192,12 @@ def tile_picked_lapl_none_p_kernel(tc, x_words, x_scales, w1, w2_words, w2_scale
         def entries(b0, b1):
             return slice(b0 * P // LIST_COLUMN, b1 * P // LIST_COLUMN)
 
-        def neighbour(h, a, d, b0, b1, tag=""):
-            name = "term%d_%d_%d" % (a, d, b0)
-            term = keep.tile([P, (b1 - b0) * P], F32, name=name, tag=tag or name, align_bytes=64)
-            nc.vector.tensor_tensor(term[:], h[:].indirect(pos_sb[d][:, entries(b0, b1)]), neg_gate[:, d, b0 * P : b1 * P], MULT)
-            return term[:]
+        def neighbours(h, a, b0, b1, bank, tag="", opened=True, close=True):
+            name = "terms%d_%d" % (a, b0)
+            terms = keep.tile([P, D, (b1 - b0) * P], F32, name=name, tag=tag or name, align_bytes=64)
+            for d in range(D):
+                nc.vector.tensor_tensor(terms[:, d, :], h[:].indirect(pos_sb[d][:, entries(b0, b1)]), neg_gate[:, d, b0 * P : b1 * P], MULT)
+                add_turned(bank, terms[:, d, :], first=(d == 0 and not opened), last=(d == D - 1 and close))
 
         def centre(h, a, tag=""):
             own = keep.tile([P, V], F32, name="own%d" % a, tag=tag or "own%d" % a, align_bytes=64)
@@ -255,23 +256,20 @@ def tile_picked_lapl_none_p_kernel(tc, x_words, x_scales, w1, w2_words, w2_scale
         round_w1(1, 0, PASSES, "w1_codes0_1", nc.vector.tensor_copy)
         quantize_w1(1, 0, PASSES)
         h1 = first_product(1, HALVES, ("product1", "product2"))
-        sums = [sum_bank(0, "product1"), sum_bank(1, "targets1"), sum_bank(2, "targets2")]
+        sums = [sum_bank(0, "product1")]
+        add_turned(sums[0], centre(h0, 0), first=True)
+        neighbours(h0, 0, 0, BLOCKS, sums[0], "w1_codes0_1")
         round_w1(2, 0, PASSES)
         quantize_w1(2, 0, PASSES)
-        add_turned(sums[0], neighbour(h0, 0, 0, 0, BLOCKS), first=True)
-        add_turned(sums[0], neighbour(h0, 0, 1, 0, BLOCKS, "w1_codes0_1"))
-        add_turned(sums[0], neighbour(h0, 0, 2, 0, BLOCKS, "w1_bf2_0"))
-        own0 = centre(h0, 0, "w1_codes1_0")
         round_w1(3, 0, PASSES, "w1_planes1_0")
         h2 = first_product(2, HALVES, ("product3", "product0"))
-        add_turned(sums[0], own0, last=True)
-        for d in range(D):
-            add_turned(sums[1], neighbour(h1, 1, d, 0, BLOCKS), first=(d == 0))
+        sums.append(sum_bank(1, "product3"))
         quantize_w1(3, 0, PASSES)
+        neighbours(h1, 1, 0, BLOCKS, sums[1], "w1_bf2_0", opened=False, close=False)
         add_turned(sums[1], centre(h1, 1), last=True)
         h3 = first_product(3, HALVES, ("targets0", "product2"))
-        for d in range(D):
-            add_turned(sums[2], neighbour(h2, 2, d, 0, BLOCKS), first=(d == 0))
+        sums.append(sum_bank(2, "targets0"))
+        neighbours(h2, 2, 0, BLOCKS, sums[2], "w1_planes1_0", opened=False, close=False)
         add_turned(sums[2], centre(h2, 2), last=True)
         own3 = centre(h3, 3)
         for a in range(ROW_TILES - 1):
@@ -280,16 +278,15 @@ def tile_picked_lapl_none_p_kernel(tc, x_words, x_scales, w1, w2_words, w2_scale
         def last_unit(b0, b1, tag):
             bank = psum.tile([P, (b1 - b0) * P], F32, name="sums3_%d" % b0, tag=tag)[:]
             add_turned(bank, own3[:, b0 * P : b1 * P], first=True)
-            for d in range(D):
-                add_turned(bank, neighbour(h3, 3, d, b0, b1), last=(d == D - 1))
+            neighbours(h3, 3, b0, b1, bank)
             round_z(bank, 3, b0)
 
         last_unit(0, 2, "targets3")
-        last_unit(2, 3, "product3")
+        last_unit(2, 3, "targets1")
         back_01 = turn_back(0, 2, "product0")
         z_01 = empty_back(back_01, 0, nc.scalar.copy)
         last_unit(3, 4, "targets3")
-        back_2 = turn_back(2, 3, "targets0")
+        back_2 = turn_back(2, 3, "targets2")
         z_2 = empty_back(back_2, 2, nc.vector.tensor_copy)
         back_3 = turn_back(3, 4, "product2")
         z_3 = empty_back(back_3, 3, nc.scalar.copy)
@@ -298,6 +295,6 @@ def tile_picked_lapl_none_p_kernel(tc, x_words, x_scales, w1, w2_words, w2_scale
         second_product(res_012[:, 0 : 2 * P], z_01, 0)
         second_product(res_012[:, 2 * P : 3 * P], z_2, 2)
         store(res_012[:], 0)
-        res_3 = psum.tile([P, P], F32, name="res_3", tag="targets1")
+        res_3 = psum.tile([P, P], F32, name="res_3", tag="product3")
         second_product(res_3[:], z_3, 3)
         store(res_3[:], 3 * P)

@@ -146,44 +146,34 @@ def tile_picked_lapl_none_p_kernel(tc, x_words, x_scales, w1, w2_words, w2_scale
         nc.vector.tensor_copy(x_second[:], x_words_all[1][:].indirect(offs_sb[:, 0 : BANK // LIST_COLUMN]))
         round_w1(0, 1, 2)
         quantize_w1(0, 1, 2)
-        x_third = shared.tile([P, LAST_PIECE - BANK], U32, name="x_third", offset=0, align_bytes=64)
-        nc.vector.tensor_copy(x_third[:], x_words_all[1][:].indirect(offs_sb[:, BANK // LIST_COLUMN : LAST_PIECE // LIST_COLUMN]))
-        x_last = shared.tile([P, S - LAST_PIECE], U32, name="x_last", offset=1024, align_bytes=64)
-        nc.vector.tensor_copy(x_last[:], x_words_all[1][:].indirect(offs_sb[:, LAST_PIECE // LIST_COLUMN : S // LIST_COLUMN]))
+        x_third = shared.tile([P, S - BANK], U32, name="x_third", offset=0, align_bytes=64)
+        for c0, c1 in ((BANK, LAST_PIECE), (LAST_PIECE, S)):
+            nc.vector.tensor_copy(x_third[:, c0 - BANK : c1 - BANK], x_words_all[1][:].indirect(offs_sb[:, c0 // LIST_COLUMN : c1 // LIST_COLUMN]))
         w2_codes = load_words("w2_codes", w2_words[0], "x_words_all1")
 
         def x_codes(g, c0, c1):
             if g == 0:
                 return x_first[:, c0:c1]
-            if c1 <= BANK:
-                return x_second[:, c0:c1]
-            return x_third[:, c0 - BANK : c1 - BANK] if c1 <= LAST_PIECE else x_last[:, c0 - LAST_PIECE : c1 - LAST_PIECE]
+            return x_second[:, c0:c1] if c1 <= BANK else x_third[:, c0 - BANK : c1 - BANK]
 
-        def first_product(a, pieces, banks):
-            h = keep.tile([P, S], F32, name="h%d" % a, align_bytes=64)
+        def first_product(h, a, pieces, banks):
             accs = [psum.tile([P, c1 - c0], F32, name="acc%d_%d" % (a, c0), tag=bank) for (c0, c1), bank in zip(pieces, banks)]
-            steps = [(g, n) for g in range(PASSES) for n in range(len(pieces))]
-            if a > 0:
-                steps = sorted(steps, key=lambda step: step[1])
-            for g, n in steps:
-                p0, p1 = pieces[n]
-                cuts = (p0, LAST_PIECE, p1) if g == 1 and p0 < LAST_PIECE < p1 else (p0, p1)
-                for c0, c1 in zip(cuts, cuts[1:]):
+            for g in range(PASSES):
+                for acc, (c0, c1) in zip(accs, pieces):
                     nc.tensor.matmul_mx(
-                        out=accs[n][:, c0 - p0 : c1 - p0],
+                        out=acc[:],
                         lhsT=w1_codes[a, g].bitcast(FP8X4),
                         lhsT_scale=w1_planes[a, g],
                         rhs=x_codes(g, c0, c1).bitcast(FP8X4),
                         rhs_scale=x_plane[g][:, c0:c1],
                         start=(g == 0),
-                        stop=(g == PASSES - 1 and c1 == p1),
+                        stop=(g == PASSES - 1),
                     )
             for acc, (c0, c1) in zip(accs, pieces):
                 if (a, c0) == (0, 768):
                     nc.vector.tensor_copy(h[:, c0:c1], acc[:])
                 else:
                     nc.scalar.activation(h[:, c0:c1], acc[:], COPY)
-            return h
 
         zt_bf = keep.tile([P, BLOCKS * H], BF16, name="zt_bf", align_bytes=64)
         zt_pairs = zt_bf[:].rearrange("v (u b p e) -> v u b p e", u=2, b=BLOCKS, e=2)
@@ -192,15 +182,18 @@ def tile_picked_lapl_none_p_kernel(tc, x_words, x_scales, w1, w2_words, w2_scale
         def entries(b0, b1):
             return slice(b0 * P // LIST_COLUMN, b1 * P // LIST_COLUMN)
 
-        def neighbours(h, a, b0, b1, bank, tag="", opened=True, close=True):
-            name = "terms%d_%d" % (a, b0)
-            terms = keep.tile([P, D, (b1 - b0) * P], F32, name=name, tag=tag or name, align_bytes=64)
-            for d in range(D):
-                nc.vector.tensor_tensor(terms[:, d, :], h[:].indirect(pos_sb[d][:, entries(b0, b1)]), neg_gate[:, d, b0 * P : b1 * P], MULT)
-                add_turned(bank, terms[:, d, :], first=(d == 0 and not opened), last=(d == D - 1 and close))
+        def neighbours(h, a, lists, b0, b1, tag=""):
+            name = "terms%d_%d_%d" % (a, lists[0], b0)
+            terms = keep.tile([P, len(lists), (b1 - b0) * P], F32, name=name, tag=tag or name, align_bytes=64)
+            for n, d in enumerate(lists):
+                nc.vector.tensor_tensor(terms[:, n, :], h[:].indirect(pos_sb[d][:, entries(b0, b1)]), neg_gate[:, d, b0 * P : b1 * P], MULT)
+            return [terms[:, n, :] for n in range(len(lists))]
 
-        def centre(h, a, tag=""):
-            own = keep.tile([P, V], F32, name="own%d" % a, tag=tag or "own%d" % a, align_bytes=64)
+        def centre(h, a, offset=None):
+            if offset is None:
+                own = keep.tile([P, V], F32, name="own%d" % a, align_bytes=64)
+            else:
+                own = shared.tile([P, V], F32, name="own%d" % a, offset=offset, align_bytes=64)
             nc.scalar.activation(own[:], h[:].indirect(cen_sb[:]), COPY)
             return own[:]
 
@@ -215,6 +208,10 @@ def tile_picked_lapl_none_p_kernel(tc, x_words, x_scales, w1, w2_words, w2_scale
                     stop=(last and n == count - 1),
                     is_transpose=True,
                 )
+
+        def add_all(bank, summands):
+            for n, summand in enumerate(summands):
+                add_turned(bank, summand, first=(n == 0), last=(n == len(summands) - 1))
 
         def round_z(bank, a, b0):
             count = bank.shape[1] // P
@@ -252,41 +249,50 @@ def tile_picked_lapl_none_p_kernel(tc, x_words, x_scales, w1, w2_words, w2_scale
         def sum_bank(a, tag):
             return psum.tile([P, V], F32, name="sums%d" % a, tag=tag)[:]
 
-        h0 = first_product(0, FIRST_PIECES, ("product1", "product2", "product3", "product0", "targets3"))
+        h = [keep.tile([P, S], F32, name="h%d" % a, align_bytes=64) for a in range(ROW_TILES)]
+        first_product(h[0], 0, FIRST_PIECES, ("product1", "product2", "product3", "product0", "targets3"))
         round_w1(1, 0, PASSES, "w1_codes0_1", nc.vector.tensor_copy)
         quantize_w1(1, 0, PASSES)
-        h1 = first_product(1, HALVES, ("product1", "product2"))
-        sums = [sum_bank(0, "product1")]
-        add_turned(sums[0], centre(h0, 0), first=True)
-        neighbours(h0, 0, 0, BLOCKS, sums[0], "w1_codes0_1")
+        first_product(h[1], 1, HALVES, ("product1", "product2"))
+        own0 = centre(h[0], 0)
+        terms0 = neighbours(h[0], 0, (0, 1), 0, BLOCKS, "w1_codes0_1")
         round_w1(2, 0, PASSES)
         quantize_w1(2, 0, PASSES)
+        terms0 = terms0 + neighbours(h[0], 0, (2,), 0, BLOCKS, "w1_bf2_0")
+        first_product(h[2], 2, HALVES[:1], ("product3",))
         round_w1(3, 0, PASSES, "w1_planes1_0")
-        h2 = first_product(2, HALVES, ("product3", "product0"))
-        sums.append(sum_bank(1, "product3"))
+        sums0 = sum_bank(0, "product1")
+        first_product(h[2], 2, HALVES[1:], ("product3",))
+        add_all(sums0, [own0] + terms0)
+        round_z(sums0, 0, 0)
+        terms1 = neighbours(h[1], 1, (0,), 0, BLOCKS)
         quantize_w1(3, 0, PASSES)
-        neighbours(h1, 1, 0, BLOCKS, sums[1], "w1_bf2_0", opened=False, close=False)
-        add_turned(sums[1], centre(h1, 1), last=True)
-        h3 = first_product(3, HALVES, ("targets0", "product2"))
-        sums.append(sum_bank(2, "targets0"))
-        neighbours(h2, 2, 0, BLOCKS, sums[2], "w1_planes1_0", opened=False, close=False)
-        add_turned(sums[2], centre(h2, 2), last=True)
-        own3 = centre(h3, 3)
-        for a in range(ROW_TILES - 1):
-            round_z(sums[a], a, 0)
+        terms1 = terms1 + neighbours(h[1], 1, (1, 2), 0, BLOCKS, "w1_planes1_0")
+        own1 = centre(h[1], 1)
+        first_product(h[3], 3, FIRST_PIECES[:2], ("product3", "targets2"))
+        own2 = centre(h[2], 2, 16384)
+        first_product(h[3], 3, HALVES[1:], ("product3",))
+        sums1 = sum_bank(1, "targets1")
+        add_all(sums1, terms1[:2] + [own1] + terms1[2:])
+        round_z(sums1, 1, 0)
+        terms2 = neighbours(h[2], 2, (0, 1, 2), 0, BLOCKS)
+        own3 = centre(h[3], 3)
+        sums2 = sum_bank(2, "targets2")
+        add_all(sums2, [own2] + terms2)
+        round_z(sums2, 2, 0)
 
         def last_unit(b0, b1, tag):
             bank = psum.tile([P, (b1 - b0) * P], F32, name="sums3_%d" % b0, tag=tag)[:]
-            add_turned(bank, own3[:, b0 * P : b1 * P], first=True)
-            neighbours(h3, 3, b0, b1, bank)
+            terms = neighbours(h[3], 3, (0, 1, 2), b0, b1)
+            add_all(bank, terms[:2] + [own3[:, b0 * P : b1 * P]] + terms[2:])
             round_z(bank, 3, b0)
 
         last_unit(0, 2, "targets3")
-        last_unit(2, 3, "targets1")
+        last_unit(2, 3, "targets0")
         back_01 = turn_back(0, 2, "product0")
         z_01 = empty_back(back_01, 0, nc.scalar.copy)
         last_unit(3, 4, "targets3")
-        back_2 = turn_back(2, 3, "targets2")
+        back_2 = turn_back(2, 3, "product3")
         z_2 = empty_back(back_2, 2, nc.vector.tensor_copy)
         back_3 = turn_back(3, 4, "product2")
         z_3 = empty_back(back_3, 3, nc.scalar.copy)
@@ -295,6 +301,6 @@ def tile_picked_lapl_none_p_kernel(tc, x_words, x_scales, w1, w2_words, w2_scale
         second_product(res_012[:, 0 : 2 * P], z_01, 0)
         second_product(res_012[:, 2 * P : 3 * P], z_2, 2)
         store(res_012[:], 0)
-        res_3 = psum.tile([P, P], F32, name="res_3", tag="product3")
+        res_3 = psum.tile([P, P], F32, name="res_3", tag="targets1")
         second_product(res_3[:], z_3, 3)
         store(res_3[:], 3 * P)

@@ -32,13 +32,16 @@ LINE = 4
 HALVES = ((0, BANK), (BANK, S))
 FIRST_PIECES = ((0, 256), (256, 512), (512, 768), (768, 896), (896, 1024))
 LAST_PIECE = 3 * S // 4
+FAR = 48 * 1024
 
 
 def tile_picked_lapl_none_p_kernel(tc, x_words, x_scales, w1, w2_words, w2_scales, gate, offs, cen, pos1, pos2, pos3, out):
     nc = tc.nc
     with ExitStack() as ctx:
+        low = ctx.enter_context(tc.tile_pool(name="low", bufs=1))
         keep = ctx.enter_context(tc.tile_pool(name="keep", bufs=1))
         shared = ctx.enter_context(tc.tile_pool(name="shared", bufs=1))
+        high = ctx.enter_context(tc.tile_pool(name="high", bufs=1))
         psum = ctx.enter_context(tc.psum_pool(name="psum", bufs=1))
 
         def raw_tag(a, g):
@@ -175,6 +178,7 @@ def tile_picked_lapl_none_p_kernel(tc, x_words, x_scales, w1, w2_words, w2_scale
                 else:
                     nc.scalar.activation(h[:, c0:c1], acc[:], COPY)
 
+
         zt_bf = keep.tile([P, BLOCKS * H], BF16, name="zt_bf", align_bytes=64)
         zt_pairs = zt_bf[:].rearrange("v (u b p e) -> v u b p e", u=2, b=BLOCKS, e=2)
         zt_words = zt_bf[:].bitcast(F32).rearrange("v (u b p) -> v u b p", u=2, b=BLOCKS)
@@ -189,11 +193,8 @@ def tile_picked_lapl_none_p_kernel(tc, x_words, x_scales, w1, w2_words, w2_scale
                 nc.vector.tensor_tensor(terms[:, n, :], h[:].indirect(pos_sb[d][:, entries(b0, b1)]), neg_gate[:, d, b0 * P : b1 * P], MULT)
             return [terms[:, n, :] for n in range(len(lists))]
 
-        def centre(h, a, offset=None):
-            if offset is None:
-                own = keep.tile([P, V], F32, name="own%d" % a, align_bytes=64)
-            else:
-                own = shared.tile([P, V], F32, name="own%d" % a, offset=offset, align_bytes=64)
+        def centre(h, a, tag=""):
+            own = keep.tile([P, V], F32, name="own%d" % a, tag=tag or "own%d" % a, align_bytes=64)
             nc.scalar.activation(own[:], h[:].indirect(cen_sb[:]), COPY)
             return own[:]
 
@@ -249,7 +250,7 @@ def tile_picked_lapl_none_p_kernel(tc, x_words, x_scales, w1, w2_words, w2_scale
         def sum_bank(a, tag):
             return psum.tile([P, V], F32, name="sums%d" % a, tag=tag)[:]
 
-        h = [keep.tile([P, S], F32, name="h%d" % a, align_bytes=64) for a in range(ROW_TILES)]
+        h = [(low, high)[a % 2].tile([P, S], F32, name="h%d" % a, offset=a % 2 * FAR + a // 2 * 4 * S, align_bytes=64) for a in range(ROW_TILES)]
         first_product(h[0], 0, FIRST_PIECES, ("product1", "product2", "product3", "product0", "targets3"))
         round_w1(1, 0, PASSES, "w1_codes0_1", nc.vector.tensor_copy)
         quantize_w1(1, 0, PASSES)
@@ -268,17 +269,18 @@ def tile_picked_lapl_none_p_kernel(tc, x_words, x_scales, w1, w2_words, w2_scale
         terms1 = neighbours(h[1], 1, (0,), 0, BLOCKS)
         quantize_w1(3, 0, PASSES)
         terms1 = terms1 + neighbours(h[1], 1, (1, 2), 0, BLOCKS, "w1_planes1_0")
-        own1 = centre(h[1], 1)
-        first_product(h[3], 3, FIRST_PIECES[:2], ("product3", "targets2"))
-        own2 = centre(h[2], 2, 16384)
-        first_product(h[3], 3, HALVES[1:], ("product3",))
-        sums1 = sum_bank(1, "targets1")
-        add_all(sums1, terms1[:2] + [own1] + terms1[2:])
-        round_z(sums1, 1, 0)
-        terms2 = neighbours(h[2], 2, (0, 1, 2), 0, BLOCKS)
+        own2 = centre(h[2], 2)
+        first_product(h[3], 3, HALVES, ("product2", "product0"))
         own3 = centre(h[3], 3)
+        terms2 = neighbours(h[2], 2, (0, 1, 2), 0, BLOCKS)
         sums2 = sum_bank(2, "targets2")
-        add_all(sums2, [own2] + terms2)
+        add_turned(sums2, own2, first=True)
+        own1 = centre(h[1], 1, "own2")
+        sums1 = sum_bank(1, "targets1")
+        add_all(sums1, terms1 + [own1])
+        round_z(sums1, 1, 0)
+        for d in range(D):
+            add_turned(sums2, terms2[d], last=(d == D - 1))
         round_z(sums2, 2, 0)
 
         def last_unit(b0, b1, tag):

@@ -260,27 +260,24 @@ def tile_picked_lapl_none_p_kernel(tc, x_words, x_scales, w1, w2_words, w2_scale
         round_w1(2, 0, PASSES)
         quantize_w1(2, 0, PASSES)
         terms0 = terms0 + neighbours(h[0], 0, (2,), 0, BLOCKS, "w1_bf2_0")
-        first_product(h[2], 2, HALVES[:1], ("product3",))
         round_w1(3, 0, PASSES, "w1_planes1_0")
+        first_product(h[2], 2, HALVES, ("product3", "targets0"))
         sums0 = sum_bank(0, "product1")
-        first_product(h[2], 2, HALVES[1:], ("product3",))
+        own1 = centre(h[1], 1)
         add_all(sums0, [own0] + terms0)
         round_z(sums0, 0, 0)
         terms1 = neighbours(h[1], 1, (0,), 0, BLOCKS)
         quantize_w1(3, 0, PASSES)
         terms1 = terms1 + neighbours(h[1], 1, (1, 2), 0, BLOCKS, "w1_planes1_0")
-        own2 = centre(h[2], 2)
         first_product(h[3], 3, HALVES, ("product2", "product0"))
+        own2 = centre(h[2], 2, "w1_codes3_0")
         own3 = centre(h[3], 3)
         terms2 = neighbours(h[2], 2, (0, 1, 2), 0, BLOCKS)
         sums2 = sum_bank(2, "targets2")
-        add_turned(sums2, own2, first=True)
-        own1 = centre(h[1], 1, "own2")
         sums1 = sum_bank(1, "targets1")
-        add_all(sums1, terms1 + [own1])
+        add_all(sums1, terms1[:1] + [own1] + terms1[1:])
         round_z(sums1, 1, 0)
-        for d in range(D):
-            add_turned(sums2, terms2[d], last=(d == D - 1))
+        add_all(sums2, terms2[:1] + [own2] + terms2[1:])
         round_z(sums2, 2, 0)
 
         def last_unit(b0, b1, tag):

@@ -263,21 +263,26 @@ def tile_picked_lapl_none_p_kernel(tc, x_words, x_scales, w1, w2_words, w2_scale
         round_w1(3, 0, PASSES, "w1_planes1_0")
         first_product(h[2], 2, HALVES, ("product3", "targets0"))
         sums0 = sum_bank(0, "product1")
-        own1 = centre(h[1], 1)
+        fetched = keep.tile([P, V], F32, name="fetched", align_bytes=64)
+        nc.scalar.activation(fetched[:], h[2][:].indirect(pos_sb[2][:]), COPY)
         add_all(sums0, [own0] + terms0)
         round_z(sums0, 0, 0)
         terms1 = neighbours(h[1], 1, (0,), 0, BLOCKS)
         quantize_w1(3, 0, PASSES)
         terms1 = terms1 + neighbours(h[1], 1, (1, 2), 0, BLOCKS, "w1_planes1_0")
         first_product(h[3], 3, HALVES, ("product2", "product0"))
+        own1 = centre(h[1], 1, "w1_planes3_0")
         own2 = centre(h[2], 2, "w1_codes3_0")
         own3 = centre(h[3], 3)
-        terms2 = neighbours(h[2], 2, (0, 1, 2), 0, BLOCKS)
+        terms2 = neighbours(h[2], 2, (0, 1), 0, BLOCKS)
+        weighted = keep.tile([P, V], F32, name="weighted", align_bytes=64)
+        nc.vector.tensor_tensor(weighted[:], fetched[:], neg_gate[:, 2, :], MULT)
+        terms2.append(weighted[:])
         sums2 = sum_bank(2, "targets2")
         sums1 = sum_bank(1, "targets1")
-        add_all(sums1, terms1[:1] + [own1] + terms1[1:])
+        add_all(sums1, terms1 + [own1])
         round_z(sums1, 1, 0)
-        add_all(sums2, terms2[:1] + [own2] + terms2[1:])
+        add_all(sums2, terms2[:2] + [own2] + terms2[2:])
         round_z(sums2, 2, 0)
 
         def last_unit(b0, b1, tag):

@@ -26,11 +26,10 @@ LIST_COLUMN = 16
 BANK = 512
 ROW_TILES = H // P
 BLOCKS = V // P
-GATE_ROWS = 96
-GATE_RUN = D * V // GATE_ROWS
+GATE_RUN = D * V // P
 LINE = 4
 HALVES = ((0, BANK), (BANK, S))
-FIRST_PIECES = ((0, 256), (256, 512), (512, 768), (768, 896), (896, 1024))
+FIRST_PIECES = ((0, 512), (512, 768), (768, 1024))
 LAST_PIECE = 3 * S // 4
 FAR = 48 * 1024
 
@@ -69,36 +68,42 @@ def tile_picked_lapl_none_p_kernel(tc, x_words, x_scales, w1, w2_words, w2_scale
             for a in range(a0, a1):
                 w1_raw[a, g] = raw[:, :, (a - a0) * P : (a - a0 + 1) * P]
 
-        x_planes_all = shared.tile([P, T], U8, name="x_planes_all", offset=1024)
-        nc.sync.dma_start(x_planes_all[0:32, :].bitcast(I32), x_scales.rearrange("g r t -> (g r) t").bitcast(I32))
+        gate_col = keep.tile([P, GATE_RUN], F32, name="gate_col")
+        halves = gate.rearrange("d r v -> (d r v)")[(P - 1) * V :].rearrange("(j x) -> j x", j=2)[:, 0 : D * V // 2]
+        nc.scalar.dma_start(gate_col[:], halves.rearrange("j (m e) -> m j e", e=GATE_RUN))
+        neg_col = keep.tile([P, GATE_RUN], F32, name="neg_col")
+        nc.scalar.activation(neg_col[:], gate_col[:], COPY, scale=-1.0)
+        x_planes_all = keep.tile([P, T], U8, name="x_planes_all")
+        nc.sync.dma_start(x_planes_all[0:32, :].bitcast(I32), x_scales.bitcast(I32).rearrange("g r t -> r g t"))
         offs_sb = load_list("offs_sb", offs)
         nc.vector.memset(x_planes_all[32:64, :].bitcast(I32), 0)
         nc.vector.memset(x_planes_all[64:P, :].bitcast(I32), 0)
         x_words_all = [load_words("x_words_all0", x_words[0], offset=8192)]
-        gate_col = keep.tile([P, GATE_RUN], F32, name="gate_col")
-        nc.vector.memset(gate_col[GATE_ROWS:P, :], 0.0)
-        nc.sync.dma_start(gate_col[0:GATE_ROWS, :], gate[:, 0, :].rearrange("d (m e) -> m d e", e=GATE_RUN))
-        load_w1(0, 1, 0, 5120)
+        load_w1(0, 1, 0, 2048)
+        x_words_all.append(load_words("x_words_all1", x_words[1], offset=24576))
+        load_w1(0, 1, 1, 0)
+        load_w1(1, 2, 0, 4096)
+        load_w1(1, 2, 1, 6144)
+        pos_sb = [load_list("pos0_sb", pos1)]
         cen_sb = load_list("cen_sb", cen)
-        pos_sb = [load_list("pos%d_sb" % d, src) for d, src in enumerate((pos1, pos2, pos3))]
-        x_words_all.append(load_words("x_words_all1", x_words[1]))
+        pos_sb = pos_sb + [load_list("pos1_sb", pos2), load_list("pos2_sb", pos3)]
+        for n in range(4):
+            load_w1(2 + n // 2, 3 + n // 2, n % 2, 32768 + 2048 * n)
+        w2_codes = load_words("w2_codes", w2_words[0])
 
-        x_plane = [keep.tile([P, S], U8, name="x_plane%d" % g, align_bytes=64) for g in range(PASSES)]
-        for g in range(PASSES):
-            nc.vector.memset(x_plane[g][:].bitcast(I32), 0)
+        x_plane = keep.tile([P, PASSES * S], U8, name="x_plane", align_bytes=64)
+        nc.vector.memset(x_plane[:].bitcast(I32), 0)
         ident = keep.tile([P, P], F32, name="ident")
         make_identity(nc, ident[:])
 
         neg_gate = keep.tile([P, D, V], F32, name="neg_gate")
         for b in range(GATE_RUN // LINE):
-            spread = psum.tile([P, LINE, P], F32, name="spread%d" % b, tag="targets%d" % b)
+            spread = psum.tile([P, LINE, P], F32, name="spread%d" % b, tag="product%d" % (b + 1))
             for e in range(LINE):
-                nc.tensor.transpose(spread[:, e, :], gate_col[:, b * LINE + e : b * LINE + e + 1].to_broadcast([P, P]), ident[:])
-            nc.scalar.activation(
-                neg_gate[:].rearrange("q d (m e) -> q d m e", e=GATE_RUN)[:, :, :, b * LINE : (b + 1) * LINE],
-                spread[:, :, 0:GATE_ROWS].rearrange("q e (m d) -> q d m e", d=D),
-                COPY,
-                scale=-1.0,
+                nc.tensor.transpose(spread[:, e, :], neg_col[:, b * LINE + e : b * LINE + e + 1].to_broadcast([P, P]), ident[:])
+            nc.scalar.copy(
+                neg_gate[:].rearrange("q d v -> q (d v)").rearrange("q (j m e) -> q j m e", j=2, e=GATE_RUN)[:, :, :, b * LINE : (b + 1) * LINE],
+                spread[:].rearrange("q e (m j) -> q j m e", j=2),
             )
 
         w1_bf, w1_codes, w1_planes = {}, {}, {}
@@ -122,24 +127,11 @@ def tile_picked_lapl_none_p_kernel(tc, x_words, x_scales, w1, w2_words, w2_scale
         x_planes = keep.tile([P, S], U8, name="x_planes", align_bytes=64)
         nc.vector.tensor_copy(x_planes[:], x_planes_all[:].indirect(offs_sb[:]))
 
-        def place_rows(g, q):
-            rows = x_planes[16 * g + 4 * q : 16 * g + 4 * q + 4, :]
-            nc.sync.dma_start(x_plane[g][32 * q : 32 * q + 4, :].bitcast(I32), rows.bitcast(I32))
-
         for q in range(QUADRANTS):
-            place_rows(0, q)
-        load_w1(0, 1, 1, 0)
-        for q in range(QUADRANTS):
-            place_rows(1, q)
-        load_w1(1, 2, 0, 2048)
+            nc.scalar.dma_start(x_plane[32 * q : 32 * q + 4, :].bitcast(I32), x_planes[8 * q : 8 * q + 8, :].bitcast(I32))
         x_first = keep.tile([P, S], U32, name="x_first", align_bytes=64)
         nc.vector.tensor_copy(x_first[:], x_words_all[0][:].indirect(offs_sb[:]))
         round_w1(0, 0, 1)
-        load_w1(1, 2, 1, 8192)
-        load_w1(2, 3, 0, 10240)
-        load_w1(2, 3, 1, 12288)
-        load_w1(3, 4, 0, 4096)
-        load_w1(3, 4, 1, 6144)
         quantize_w1(0, 0, 1)
         w2_plane = keep.tile([P, N], U8, name="w2_plane", tag="w1_bf0_0", align_bytes=64)
         nc.gpsimd.memset(w2_plane[:], 0)
@@ -152,7 +144,6 @@ def tile_picked_lapl_none_p_kernel(tc, x_words, x_scales, w1, w2_words, w2_scale
         x_third = shared.tile([P, S - BANK], U32, name="x_third", offset=0, align_bytes=64)
         for c0, c1 in ((BANK, LAST_PIECE), (LAST_PIECE, S)):
             nc.vector.tensor_copy(x_third[:, c0 - BANK : c1 - BANK], x_words_all[1][:].indirect(offs_sb[:, c0 // LIST_COLUMN : c1 // LIST_COLUMN]))
-        w2_codes = load_words("w2_codes", w2_words[0], "x_words_all1")
 
         def x_codes(g, c0, c1):
             if g == 0:
@@ -168,12 +159,12 @@ def tile_picked_lapl_none_p_kernel(tc, x_words, x_scales, w1, w2_words, w2_scale
                         lhsT=w1_codes[a, g].bitcast(FP8X4),
                         lhsT_scale=w1_planes[a, g],
                         rhs=x_codes(g, c0, c1).bitcast(FP8X4),
-                        rhs_scale=x_plane[g][:, c0:c1],
+                        rhs_scale=x_plane[:, g * S + c0 : g * S + c1],
                         start=(g == 0),
                         stop=(g == PASSES - 1),
                     )
             for acc, (c0, c1) in zip(accs, pieces):
-                if (a, c0) == (0, 768):
+                if (a, c0) == (0, 512):
                     nc.vector.tensor_copy(h[:, c0:c1], acc[:])
                 else:
                     nc.scalar.activation(h[:, c0:c1], acc[:], COPY)
@@ -251,7 +242,7 @@ def tile_picked_lapl_none_p_kernel(tc, x_words, x_scales, w1, w2_words, w2_scale
             return psum.tile([P, V], F32, name="sums%d" % a, tag=tag)[:]
 
         h = [(low, high)[a % 2].tile([P, S], F32, name="h%d" % a, offset=a % 2 * FAR + a // 2 * 4 * S, align_bytes=64) for a in range(ROW_TILES)]
-        first_product(h[0], 0, FIRST_PIECES, ("product1", "product2", "product3", "product0", "targets3"))
+        first_product(h[0], 0, FIRST_PIECES, ("product1", "product2", "product3"))
         round_w1(1, 0, PASSES, "w1_codes0_1", nc.vector.tensor_copy)
         quantize_w1(1, 0, PASSES)
         first_product(h[1], 1, HALVES, ("product1", "product2"))

@@ -29,22 +29,24 @@ BLOCKS = V // P
 GATE_RUN = D * V // P
 LINE = 4
 HALVES = ((0, BANK), (BANK, S))
-FIRST_PIECES = ((0, 512), (512, 768), (768, 1024))
+FIRST_PIECES = ((0, 256), (256, 512), (512, 768), (768, 1024))
 LAST_PIECE = 3 * S // 4
-FAR = 48 * 1024
 
 
 def tile_picked_lapl_none_p_kernel(tc, x_words, x_scales, w1, w2_words, w2_scales, gate, offs, cen, pos1, pos2, pos3, out):
     nc = tc.nc
     with ExitStack() as ctx:
-        low = ctx.enter_context(tc.tile_pool(name="low", bufs=1))
         keep = ctx.enter_context(tc.tile_pool(name="keep", bufs=1))
         shared = ctx.enter_context(tc.tile_pool(name="shared", bufs=1))
-        high = ctx.enter_context(tc.tile_pool(name="high", bufs=1))
         psum = ctx.enter_context(tc.psum_pool(name="psum", bufs=1))
 
         def raw_tag(a, g):
             return "w1_raw%d_%d" % (a, g)
+
+        def place(shape, dtype, name, where):
+            if isinstance(where, int):
+                return shared.tile(shape, dtype, name=name, offset=where, align_bytes=64)
+            return keep.tile(shape, dtype, name=name, tag=where or name, align_bytes=64)
 
         def load_list(name, src):
             tile = keep.tile(list(src.shape), U16, name=name)
@@ -68,28 +70,17 @@ def tile_picked_lapl_none_p_kernel(tc, x_words, x_scales, w1, w2_words, w2_scale
             for a in range(a0, a1):
                 w1_raw[a, g] = raw[:, :, (a - a0) * P : (a - a0 + 1) * P]
 
-        gate_col = keep.tile([P, GATE_RUN], F32, name="gate_col")
-        halves = gate.rearrange("d r v -> (d r v)")[(P - 1) * V :].rearrange("(j x) -> j x", j=2)[:, 0 : D * V // 2]
-        nc.scalar.dma_start(gate_col[:], halves.rearrange("j (m e) -> m j e", e=GATE_RUN))
-        neg_col = keep.tile([P, GATE_RUN], F32, name="neg_col")
-        nc.scalar.activation(neg_col[:], gate_col[:], COPY, scale=-1.0)
         x_planes_all = keep.tile([P, T], U8, name="x_planes_all")
         nc.sync.dma_start(x_planes_all[0:32, :].bitcast(I32), x_scales.bitcast(I32).rearrange("g r t -> r g t"))
         offs_sb = load_list("offs_sb", offs)
         nc.vector.memset(x_planes_all[32:64, :].bitcast(I32), 0)
         nc.vector.memset(x_planes_all[64:P, :].bitcast(I32), 0)
         x_words_all = [load_words("x_words_all0", x_words[0], offset=8192)]
+        gate_col = keep.tile([P, GATE_RUN], F32, name="gate_col")
+        halves = gate.rearrange("d r v -> (d r v)")[(P - 1) * V :].rearrange("(j x) -> j x", j=2)[:, 0 : D * V // 2]
+        nc.sync.dma_start(gate_col[:], halves.rearrange("j (m e) -> m j e", e=GATE_RUN))
         load_w1(0, 1, 0, 2048)
         x_words_all.append(load_words("x_words_all1", x_words[1], offset=24576))
-        load_w1(0, 1, 1, 0)
-        load_w1(1, 2, 0, 4096)
-        load_w1(1, 2, 1, 6144)
-        pos_sb = [load_list("pos0_sb", pos1)]
-        cen_sb = load_list("cen_sb", cen)
-        pos_sb = pos_sb + [load_list("pos1_sb", pos2), load_list("pos2_sb", pos3)]
-        for n in range(4):
-            load_w1(2 + n // 2, 3 + n // 2, n % 2, 32768 + 2048 * n)
-        w2_codes = load_words("w2_codes", w2_words[0])
 
         x_plane = keep.tile([P, PASSES * S], U8, name="x_plane", align_bytes=64)
         nc.vector.memset(x_plane[:].bitcast(I32), 0)
@@ -98,18 +89,20 @@ def tile_picked_lapl_none_p_kernel(tc, x_words, x_scales, w1, w2_words, w2_scale
 
         neg_gate = keep.tile([P, D, V], F32, name="neg_gate")
         for b in range(GATE_RUN // LINE):
-            spread = psum.tile([P, LINE, P], F32, name="spread%d" % b, tag="product%d" % (b + 1))
+            spread = psum.tile([P, LINE, P], F32, name="spread%d" % b, tag="targets%d" % b)
             for e in range(LINE):
-                nc.tensor.transpose(spread[:, e, :], neg_col[:, b * LINE + e : b * LINE + e + 1].to_broadcast([P, P]), ident[:])
-            nc.scalar.copy(
+                nc.tensor.transpose(spread[:, e, :], gate_col[:, b * LINE + e : b * LINE + e + 1].to_broadcast([P, P]), ident[:])
+            nc.scalar.activation(
                 neg_gate[:].rearrange("q d v -> q (d v)").rearrange("q (j m e) -> q j m e", j=2, e=GATE_RUN)[:, :, :, b * LINE : (b + 1) * LINE],
                 spread[:].rearrange("q e (m j) -> q j m e", j=2),
+                COPY,
+                scale=-1.0,
             )
 
         w1_bf, w1_codes, w1_planes = {}, {}, {}
 
         def round_w1(a, g0, g1, tag="", copy=nc.scalar.copy):
-            w1_bf[a, g0] = keep.tile([P, g1 - g0, P * PACK], BF16, name="w1_bf%d_%d" % (a, g0), tag=tag or "w1_bf%d_%d" % (a, g0), align_bytes=64)
+            w1_bf[a, g0] = place([P, g1 - g0, P * PACK], BF16, "w1_bf%d_%d" % (a, g0), tag)
             for g in range(g0, g1):
                 copy(
                     w1_bf[a, g0][:, g - g0, :].rearrange("p (c i j) -> p c j i", i=LINE, j=PACK),
@@ -128,7 +121,16 @@ def tile_picked_lapl_none_p_kernel(tc, x_words, x_scales, w1, w2_words, w2_scale
         nc.vector.tensor_copy(x_planes[:], x_planes_all[:].indirect(offs_sb[:]))
 
         for q in range(QUADRANTS):
-            nc.scalar.dma_start(x_plane[32 * q : 32 * q + 4, :].bitcast(I32), x_planes[8 * q : 8 * q + 8, :].bitcast(I32))
+            nc.sync.dma_start(x_plane[32 * q : 32 * q + 4, :].bitcast(I32), x_planes[8 * q : 8 * q + 8, :].bitcast(I32))
+        load_w1(0, 1, 1, 0)
+        load_w1(1, 2, 0, 4096)
+        load_w1(1, 2, 1, 6144)
+        pos_sb = [load_list("pos0_sb", pos1)]
+        cen_sb = load_list("cen_sb", cen)
+        pos_sb = pos_sb + [load_list("pos1_sb", pos2), load_list("pos2_sb", pos3)]
+        for n in range(4):
+            load_w1(2 + n // 2, 3 + n // 2, n % 2, 32768 + 2048 * n)
+        w2_codes = load_words("w2_codes", w2_words[0])
         x_first = keep.tile([P, S], U32, name="x_first", align_bytes=64)
         nc.vector.tensor_copy(x_first[:], x_words_all[0][:].indirect(offs_sb[:]))
         round_w1(0, 0, 1)
@@ -137,37 +139,35 @@ def tile_picked_lapl_none_p_kernel(tc, x_words, x_scales, w1, w2_words, w2_scale
         nc.gpsimd.memset(w2_plane[:], 0)
         for q in range(QUADRANTS):
             nc.sync.dma_start(w2_plane[32 * q : 32 * q + 4, :].bitcast(I32), w2_scales[0, 4 * q : 4 * q + 4, :].bitcast(I32))
-        x_second = shared.tile([P, BANK], U32, name="x_second", offset=16384, align_bytes=64)
-        nc.vector.tensor_copy(x_second[:], x_words_all[1][:].indirect(offs_sb[:, 0 : BANK // LIST_COLUMN]))
+        x_second = shared.tile([P, LAST_PIECE], U32, name="x_second", offset=16384, align_bytes=64)
+        nc.vector.tensor_copy(x_second[:], x_words_all[1][:].indirect(offs_sb[:, 0 : LAST_PIECE // LIST_COLUMN]))
         round_w1(0, 1, 2)
         quantize_w1(0, 1, 2)
-        x_third = shared.tile([P, S - BANK], U32, name="x_third", offset=0, align_bytes=64)
-        for c0, c1 in ((BANK, LAST_PIECE), (LAST_PIECE, S)):
-            nc.vector.tensor_copy(x_third[:, c0 - BANK : c1 - BANK], x_words_all[1][:].indirect(offs_sb[:, c0 // LIST_COLUMN : c1 // LIST_COLUMN]))
+        x_third = shared.tile([P, S - LAST_PIECE], U32, name="x_third", offset=0, align_bytes=64)
+        nc.vector.tensor_copy(x_third[:], x_words_all[1][:].indirect(offs_sb[:, LAST_PIECE // LIST_COLUMN : S // LIST_COLUMN]))
 
         def x_codes(g, c0, c1):
             if g == 0:
                 return x_first[:, c0:c1]
-            return x_second[:, c0:c1] if c1 <= BANK else x_third[:, c0 - BANK : c1 - BANK]
+            return x_second[:, c0:c1] if c1 <= LAST_PIECE else x_third[:, c0 - LAST_PIECE : c1 - LAST_PIECE]
 
         def first_product(h, a, pieces, banks):
             accs = [psum.tile([P, c1 - c0], F32, name="acc%d_%d" % (a, c0), tag=bank) for (c0, c1), bank in zip(pieces, banks)]
             for g in range(PASSES):
                 for acc, (c0, c1) in zip(accs, pieces):
-                    nc.tensor.matmul_mx(
-                        out=acc[:],
-                        lhsT=w1_codes[a, g].bitcast(FP8X4),
-                        lhsT_scale=w1_planes[a, g],
-                        rhs=x_codes(g, c0, c1).bitcast(FP8X4),
-                        rhs_scale=x_plane[:, g * S + c0 : g * S + c1],
-                        start=(g == 0),
-                        stop=(g == PASSES - 1),
-                    )
+                    cuts = (c0, LAST_PIECE, c1) if g == 1 and c0 < LAST_PIECE < c1 else (c0, c1)
+                    for n0, n1 in zip(cuts, cuts[1:]):
+                        nc.tensor.matmul_mx(
+                            out=acc[:, n0 - c0 : n1 - c0],
+                            lhsT=w1_codes[a, g].bitcast(FP8X4),
+                            lhsT_scale=w1_planes[a, g],
+                            rhs=x_codes(g, n0, n1).bitcast(FP8X4),
+                            rhs_scale=x_plane[:, g * S + n0 : g * S + n1],
+                            start=(g == 0),
+                            stop=(g == PASSES - 1 and n1 == c1),
+                        )
             for acc, (c0, c1) in zip(accs, pieces):
-                if (a, c0) == (0, 512):
-                    nc.vector.tensor_copy(h[:, c0:c1], acc[:])
-                else:
-                    nc.scalar.activation(h[:, c0:c1], acc[:], COPY)
+                nc.scalar.activation(h[:, c0:c1], acc[:], COPY)
 
 
         zt_bf = keep.tile([P, BLOCKS * H], BF16, name="zt_bf", align_bytes=64)
@@ -179,7 +179,7 @@ def tile_picked_lapl_none_p_kernel(tc, x_words, x_scales, w1, w2_words, w2_scale
 
         def neighbours(h, a, lists, b0, b1, tag=""):
             name = "terms%d_%d_%d" % (a, lists[0], b0)
-            terms = keep.tile([P, len(lists), (b1 - b0) * P], F32, name=name, tag=tag or name, align_bytes=64)
+            terms = place([P, len(lists), (b1 - b0) * P], F32, name, tag)
             for n, d in enumerate(lists):
                 nc.vector.tensor_tensor(terms[:, n, :], h[:].indirect(pos_sb[d][:, entries(b0, b1)]), neg_gate[:, d, b0 * P : b1 * P], MULT)
             return [terms[:, n, :] for n in range(len(lists))]
@@ -241,14 +241,14 @@ def tile_picked_lapl_none_p_kernel(tc, x_words, x_scales, w1, w2_words, w2_scale
         def sum_bank(a, tag):
             return psum.tile([P, V], F32, name="sums%d" % a, tag=tag)[:]
 
-        h = [(low, high)[a % 2].tile([P, S], F32, name="h%d" % a, offset=a % 2 * FAR + a // 2 * 4 * S, align_bytes=64) for a in range(ROW_TILES)]
-        first_product(h[0], 0, FIRST_PIECES, ("product1", "product2", "product3"))
-        round_w1(1, 0, PASSES, "w1_codes0_1", nc.vector.tensor_copy)
+        h = [shared.tile([P, S], F32, name="h%d" % a, offset=(40960, 32768, 36864, 45056)[a], align_bytes=64) for a in range(ROW_TILES)]
+        first_product(h[0], 0, FIRST_PIECES, ("product1", "product2", "product3", "product0"))
+        round_w1(1, 0, PASSES, 24576, nc.vector.tensor_copy)
         quantize_w1(1, 0, PASSES)
-        first_product(h[1], 1, HALVES, ("product1", "product2"))
         own0 = centre(h[0], 0)
-        terms0 = neighbours(h[0], 0, (0, 1), 0, BLOCKS, "w1_codes0_1")
         round_w1(2, 0, PASSES)
+        first_product(h[1], 1, HALVES, ("product1", "product2"))
+        terms0 = neighbours(h[0], 0, (0, 1), 0, BLOCKS, 24576)
         quantize_w1(2, 0, PASSES)
         terms0 = terms0 + neighbours(h[0], 0, (2,), 0, BLOCKS, "w1_bf2_0")
         round_w1(3, 0, PASSES, "w1_planes1_0")

@@ -243,26 +243,27 @@ def tile_picked_lapl_none_p_kernel(tc, x_words, x_scales, w1, w2_words, w2_scale
 
         h = [shared.tile([P, S], F32, name="h%d" % a, offset=(40960, 32768, 36864, 45056)[a], align_bytes=64) for a in range(ROW_TILES)]
         first_product(h[0], 0, FIRST_PIECES, ("product1", "product2", "product3", "product0"))
-        round_w1(1, 0, PASSES, 24576, nc.vector.tensor_copy)
-        quantize_w1(1, 0, PASSES)
+        for g in range(PASSES):
+            round_w1(1, g, g + 1, 24576 + 1024 * g, nc.vector.tensor_copy)
+        for g in range(PASSES):
+            quantize_w1(1, g, g + 1)
         own0 = centre(h[0], 0)
         round_w1(2, 0, PASSES)
         first_product(h[1], 1, HALVES, ("product1", "product2"))
-        terms0 = neighbours(h[0], 0, (0, 1), 0, BLOCKS, 24576)
+        terms0 = neighbours(h[0], 0, (0, 1, 2), 0, BLOCKS)
         quantize_w1(2, 0, PASSES)
-        terms0 = terms0 + neighbours(h[0], 0, (2,), 0, BLOCKS, "w1_bf2_0")
-        round_w1(3, 0, PASSES, "w1_planes1_0")
+        round_w1(3, 0, PASSES, "w1_planes1_1")
+        own1 = centre(h[1], 1)
         first_product(h[2], 2, HALVES, ("product3", "targets0"))
-        sums0 = sum_bank(0, "product1")
+        sums0 = sum_bank(0, "targets3")
         fetched = keep.tile([P, V], F32, name="fetched", align_bytes=64)
         nc.scalar.activation(fetched[:], h[2][:].indirect(pos_sb[2][:]), COPY)
         add_all(sums0, [own0] + terms0)
         round_z(sums0, 0, 0)
         terms1 = neighbours(h[1], 1, (0,), 0, BLOCKS)
         quantize_w1(3, 0, PASSES)
-        terms1 = terms1 + neighbours(h[1], 1, (1, 2), 0, BLOCKS, "w1_planes1_0")
+        terms1 = terms1 + neighbours(h[1], 1, (1, 2), 0, BLOCKS, "w1_planes1_1")
         first_product(h[3], 3, HALVES, ("product2", "product0"))
-        own1 = centre(h[1], 1, "w1_planes3_0")
         own2 = centre(h[2], 2, "w1_codes3_0")
         own3 = centre(h[3], 3)
         terms2 = neighbours(h[2], 2, (0, 1), 0, BLOCKS)

@@ -129,7 +129,7 @@ def tile_picked_lapl_none_p_kernel(tc, x_words, x_scales, w1, w2_words, w2_scale
         cen_sb = load_list("cen_sb", cen)
         pos_sb = pos_sb + [load_list("pos1_sb", pos2), load_list("pos2_sb", pos3)]
         for n in range(4):
-            load_w1(2 + n // 2, 3 + n // 2, n % 2, 32768 + 2048 * n)
+            load_w1(2 + n // 2, 3 + n // 2, n % 2, (34816, 49152, 36864, 53248)[n])
         w2_codes = load_words("w2_codes", w2_words[0])
         x_first = keep.tile([P, S], U32, name="x_first", align_bytes=64)
         nc.vector.tensor_copy(x_first[:], x_words_all[0][:].indirect(offs_sb[:]))
@@ -244,7 +244,7 @@ def tile_picked_lapl_none_p_kernel(tc, x_words, x_scales, w1, w2_words, w2_scale
         h = [shared.tile([P, S], F32, name="h%d" % a, offset=(40960, 32768, 36864, 45056)[a], align_bytes=64) for a in range(ROW_TILES)]
         first_product(h[0], 0, FIRST_PIECES, ("product1", "product2", "product3", "product0"))
         for g in range(PASSES):
-            round_w1(1, g, g + 1, 24576 + 1024 * g, nc.vector.tensor_copy)
+            round_w1(1, g, g + 1, ("w1_bf0_1", "")[g], nc.vector.tensor_copy)
         for g in range(PASSES):
             quantize_w1(1, g, g + 1)
         own0 = centre(h[0], 0)
@@ -262,7 +262,7 @@ def tile_picked_lapl_none_p_kernel(tc, x_words, x_scales, w1, w2_words, w2_scale
         round_z(sums0, 0, 0)
         terms1 = neighbours(h[1], 1, (0,), 0, BLOCKS)
         quantize_w1(3, 0, PASSES)
-        terms1 = terms1 + neighbours(h[1], 1, (1, 2), 0, BLOCKS, "w1_planes1_1")
+        terms1 = terms1 + neighbours(h[1], 1, (1, 2), 0, BLOCKS, 53248)
         first_product(h[3], 3, HALVES, ("product2", "product0"))
         own2 = centre(h[2], 2, "w1_codes3_0")
         own3 = centre(h[3], 3)

@@ -80,7 +80,9 @@ def tile_picked_lapl_none_p_kernel(tc, x_words, x_scales, w1, w2_words, w2_scale
         halves = gate.rearrange("d r v -> (d r v)")[(P - 1) * V :].rearrange("(j x) -> j x", j=2)[:, 0 : D * V // 2]
         nc.sync.dma_start(gate_col[:], halves.rearrange("j (m e) -> m j e", e=GATE_RUN))
         load_w1(0, 1, 0, 2048)
-        x_words_all.append(load_words("x_words_all1", x_words[1], offset=24576))
+        x_words_all.append(shared.tile([P, T], U32, name="x_words_all1", offset=24576, align_bytes=64))
+        second_words = x_words[1].rearrange("p n t -> p (n t)").bitcast(I32)
+        nc.sync.dma_start(x_words_all[1][:, 0 : 3 * T // 4].bitcast(I32), second_words[:, 0 : 3 * T // 4])
 
         x_plane = keep.tile([P, PASSES * S], U8, name="x_plane", align_bytes=64)
         nc.vector.memset(x_plane[:].bitcast(I32), 0)
@@ -122,6 +124,7 @@ def tile_picked_lapl_none_p_kernel(tc, x_words, x_scales, w1, w2_words, w2_scale
 
         for q in range(QUADRANTS):
             nc.sync.dma_start(x_plane[32 * q : 32 * q + 4, :].bitcast(I32), x_planes[8 * q : 8 * q + 8, :].bitcast(I32))
+        nc.sync.dma_start(x_words_all[1][:, 3 * T // 4 : T].bitcast(I32), second_words[:, 3 * T // 4 : T])
         load_w1(0, 1, 1, 0)
         load_w1(1, 2, 0, 4096)
         load_w1(1, 2, 1, 6144)
@@ -153,8 +156,9 @@ def tile_picked_lapl_none_p_kernel(tc, x_words, x_scales, w1, w2_words, w2_scale
 
         def first_product(h, a, pieces, banks):
             accs = [psum.tile([P, c1 - c0], F32, name="acc%d_%d" % (a, c0), tag=bank) for (c0, c1), bank in zip(pieces, banks)]
-            for g in range(PASSES):
-                for acc, (c0, c1) in zip(accs, pieces):
+            steps = [(g, n) for g in range(PASSES) for n in range(len(pieces))]
+            for g, n in steps if a == 0 else sorted(steps, key=lambda step: step[1]):
+                for acc, (c0, c1) in [(accs[n], pieces[n])]:
                     cuts = (c0, LAST_PIECE, c1) if g == 1 and c0 < LAST_PIECE < c1 else (c0, c1)
                     for n0, n1 in zip(cuts, cuts[1:]):
                         nc.tensor.matmul_mx(

@@ -170,8 +170,11 @@ def tile_picked_lapl_none_p_kernel(tc, x_words, x_scales, w1, w2_words, w2_scale
                             start=(g == 0),
                             stop=(g == PASSES - 1 and n1 == c1),
                         )
-            for acc, (c0, c1) in zip(accs, pieces):
-                nc.scalar.activation(h[:, c0:c1], acc[:], COPY)
+            return [(h[:, c0:c1], acc[:]) for acc, (c0, c1) in zip(accs, pieces)]
+
+        def empty(pieces):
+            for into, acc in pieces:
+                nc.scalar.activation(into, acc, COPY)
 
 
         zt_bf = keep.tile([P, BLOCKS * H], BF16, name="zt_bf", align_bytes=64)
@@ -246,28 +249,30 @@ def tile_picked_lapl_none_p_kernel(tc, x_words, x_scales, w1, w2_words, w2_scale
             return psum.tile([P, V], F32, name="sums%d" % a, tag=tag)[:]
 
         h = [shared.tile([P, S], F32, name="h%d" % a, offset=(40960, 32768, 36864, 45056)[a], align_bytes=64) for a in range(ROW_TILES)]
-        first_product(h[0], 0, FIRST_PIECES, ("product1", "product2", "product3", "product0"))
+        empty(first_product(h[0], 0, FIRST_PIECES, ("product1", "product2", "product3", "product0")))
         for g in range(PASSES):
             round_w1(1, g, g + 1, ("w1_bf0_1", "")[g], nc.vector.tensor_copy)
         for g in range(PASSES):
             quantize_w1(1, g, g + 1)
         own0 = centre(h[0], 0)
         round_w1(2, 0, PASSES)
-        first_product(h[1], 1, HALVES, ("product1", "product2"))
+        empty(first_product(h[1], 1, HALVES, ("product1", "product2")))
         terms0 = neighbours(h[0], 0, (0, 1, 2), 0, BLOCKS)
         quantize_w1(2, 0, PASSES)
         round_w1(3, 0, PASSES, "w1_planes1_1")
         own1 = centre(h[1], 1)
-        first_product(h[2], 2, HALVES, ("product3", "targets0"))
         sums0 = sum_bank(0, "targets3")
-        fetched = keep.tile([P, V], F32, name="fetched", align_bytes=64)
-        nc.scalar.activation(fetched[:], h[2][:].indirect(pos_sb[2][:]), COPY)
         add_all(sums0, [own0] + terms0)
         round_z(sums0, 0, 0)
+        empty(first_product(h[2], 2, HALVES, ("product3", "targets0")))
         terms1 = neighbours(h[1], 1, (0,), 0, BLOCKS)
         quantize_w1(3, 0, PASSES)
         terms1 = terms1 + neighbours(h[1], 1, (1, 2), 0, BLOCKS, 53248)
-        first_product(h[3], 3, HALVES, ("product2", "product0"))
+        halves3 = first_product(h[3], 3, HALVES, ("product2", "product0"))
+        empty(halves3[:1])
+        fetched = keep.tile([P, V], F32, name="fetched", align_bytes=64)
+        nc.scalar.activation(fetched[:], h[2][:].indirect(pos_sb[2][:]), COPY)
+        empty(halves3[1:])
         own2 = centre(h[2], 2, "w1_codes3_0")
         own3 = centre(h[3], 3)
         terms2 = neighbours(h[2], 2, (0, 1), 0, BLOCKS)
@@ -275,7 +280,7 @@ def tile_picked_lapl_none_p_kernel(tc, x_words, x_scales, w1, w2_words, w2_scale
         nc.vector.tensor_tensor(weighted[:], fetched[:], neg_gate[:, 2, :], MULT)
         terms2.append(weighted[:])
         sums2 = sum_bank(2, "targets2")
-        sums1 = sum_bank(1, "targets1")
+        sums1 = sum_bank(1, "product3")
         add_all(sums1, terms1 + [own1])
         round_z(sums1, 1, 0)
         add_all(sums2, terms2[:2] + [own2] + terms2[2:])
@@ -292,7 +297,7 @@ def tile_picked_lapl_none_p_kernel(tc, x_words, x_scales, w1, w2_words, w2_scale
         back_01 = turn_back(0, 2, "product0")
         z_01 = empty_back(back_01, 0, nc.scalar.copy)
         last_unit(3, 4, "targets3")
-        back_2 = turn_back(2, 3, "product3")
+        back_2 = turn_back(2, 3, "targets1")
         z_2 = empty_back(back_2, 2, nc.vector.tensor_copy)
         back_3 = turn_back(3, 4, "product2")
         z_3 = empty_back(back_3, 3, nc.scalar.copy)
@@ -301,6 +306,6 @@ def tile_picked_lapl_none_p_kernel(tc, x_words, x_scales, w1, w2_words, w2_scale
         second_product(res_012[:, 0 : 2 * P], z_01, 0)
         second_product(res_012[:, 2 * P : 3 * P], z_2, 2)
         store(res_012[:], 0)
-        res_3 = psum.tile([P, P], F32, name="res_3", tag="targets1")
+        res_3 = psum.tile([P, P], F32, name="res_3", tag="product3")
         second_product(res_3[:], z_3, 3)
         store(res_3[:], 3 * P)

@@ -281,18 +281,21 @@ def tile_picked_lapl_none_p_kernel(tc, x_words, x_scales, w1, w2_words, w2_scale
         terms2.append(weighted[:])
         sums2 = sum_bank(2, "targets2")
         sums1 = sum_bank(1, "product3")
-        add_all(sums1, terms1 + [own1])
-        round_z(sums1, 1, 0)
-        add_all(sums2, terms2[:2] + [own2] + terms2[2:])
-        round_z(sums2, 2, 0)
+        add_all(sums1, terms1[:1] + [own1] + terms1[1:])
+        add_all(sums2, terms2 + [own2])
+        round_z(sums1[:, 0 : V // 2], 1, 0)
+        round_z(sums2[:, 0 : V // 2], 2, 0)
 
         def last_unit(b0, b1, tag):
             bank = psum.tile([P, (b1 - b0) * P], F32, name="sums3_%d" % b0, tag=tag)[:]
             terms = neighbours(h[3], 3, (0, 1, 2), b0, b1)
-            add_all(bank, terms[:2] + [own3[:, b0 * P : b1 * P]] + terms[2:])
+            ahead = 2 if b0 == 0 else 0
+            add_all(bank, terms[:ahead] + [own3[:, b0 * P : b1 * P]] + terms[ahead:])
             round_z(bank, 3, b0)
 
         last_unit(0, 2, "targets3")
+        round_z(sums1[:, V // 2 : V], 1, 2)
+        round_z(sums2[:, V // 2 : V], 2, 2)
         last_unit(2, 3, "targets0")
         back_01 = turn_back(0, 2, "product0")
         z_01 = empty_back(back_01, 0, nc.scalar.copy)

@@ -268,11 +268,12 @@ def tile_picked_lapl_none_p_kernel(tc, x_words, x_scales, w1, w2_words, w2_scale
         terms1 = neighbours(h[1], 1, (0,), 0, BLOCKS)
         quantize_w1(3, 0, PASSES)
         terms1 = terms1 + neighbours(h[1], 1, (1, 2), 0, BLOCKS, 53248)
-        halves3 = first_product(h[3], 3, HALVES, ("product2", "product0"))
-        empty(halves3[:1])
+        halves3 = first_product(h[3], 3, HALVES[:1], ("product2",))
+        empty(halves3)
+        halves3 = first_product(h[3], 3, HALVES[1:], ("product2",))
         fetched = keep.tile([P, V], F32, name="fetched", align_bytes=64)
         nc.scalar.activation(fetched[:], h[2][:].indirect(pos_sb[2][:]), COPY)
-        empty(halves3[1:])
+        empty(halves3)
         own2 = centre(h[2], 2, "w1_codes3_0")
         own3 = centre(h[3], 3)
         terms2 = neighbours(h[2], 2, (0, 1), 0, BLOCKS)

@@ -80,9 +80,7 @@ def tile_picked_lapl_none_p_kernel(tc, x_words, x_scales, w1, w2_words, w2_scale
         halves = gate.rearrange("d r v -> (d r v)")[(P - 1) * V :].rearrange("(j x) -> j x", j=2)[:, 0 : D * V // 2]
         nc.sync.dma_start(gate_col[:], halves.rearrange("j (m e) -> m j e", e=GATE_RUN))
         load_w1(0, 1, 0, 2048)
-        x_words_all.append(shared.tile([P, T], U32, name="x_words_all1", offset=24576, align_bytes=64))
-        second_words = x_words[1].rearrange("p n t -> p (n t)").bitcast(I32)
-        nc.sync.dma_start(x_words_all[1][:, 0 : 3 * T // 4].bitcast(I32), second_words[:, 0 : 3 * T // 4])
+        x_words_all.append(load_words("x_words_all1", x_words[1], offset=24576))
 
         x_plane = keep.tile([P, PASSES * S], U8, name="x_plane", align_bytes=64)
         nc.vector.memset(x_plane[:].bitcast(I32), 0)
@@ -124,7 +122,6 @@ def tile_picked_lapl_none_p_kernel(tc, x_words, x_scales, w1, w2_words, w2_scale
 
         for q in range(QUADRANTS):
             nc.sync.dma_start(x_plane[32 * q : 32 * q + 4, :].bitcast(I32), x_planes[8 * q : 8 * q + 8, :].bitcast(I32))
-        nc.sync.dma_start(x_words_all[1][:, 3 * T // 4 : T].bitcast(I32), second_words[:, 3 * T // 4 : T])
         load_w1(0, 1, 1, 0)
         load_w1(1, 2, 0, 4096)
         load_w1(1, 2, 1, 6144)

from contextlib import ExitStack

import concourse.mybir as mybir
from concourse.masks import make_identity

K, T, S, D, V, H, N = 1024, 2048, 1024, 3, 512, 512, 128
FLOPS = 2 * K * H * S + 2 * H * N * V

F32 = mybir.dt.float32
BF16 = mybir.dt.bfloat16
I32 = mybir.dt.int32
U32 = mybir.dt.uint32
U16 = mybir.dt.uint16
U8 = mybir.dt.uint8
FP8X4 = mybir.dt.float8_e4m3fn_x4
COPY = mybir.ActivationFunctionType.Copy
MULT = mybir.AluOpType.mult
ADD = mybir.AluOpType.add

P = 128
PACK = 4
K_PASS = P * PACK
PASSES = K // K_PASS
QUADRANTS = 4
LIST_COLUMN = 16
BANK = 512
ROW_TILES = H // P
BLOCKS = V // P
GATE_RUN = D * V // P
LINE = 4
HALVES = ((0, BANK), (BANK, S))
FIRST_PIECES = ((0, 256), (256, 512), (512, 768), (768, 1024))
LAST_PIECE = 3 * S // 4


def tile_picked_lapl_none_p_kernel(tc, x_words, x_scales, w1, w2_words, w2_scales, gate, offs, cen, pos1, pos2, pos3, out):
    nc = tc.nc
    with ExitStack() as ctx:
        keep = ctx.enter_context(tc.tile_pool(name="keep", bufs=1))
        shared = ctx.enter_context(tc.tile_pool(name="shared", bufs=1))
        psum = ctx.enter_context(tc.psum_pool(name="psum", bufs=1))

        def raw_tag(a, g):
            return "w1_raw%d_%d" % (a, g)

        def place(shape, dtype, name, where):
            if isinstance(where, int):
                return shared.tile(shape, dtype, name=name, offset=where, align_bytes=64)
            return keep.tile(shape, dtype, name=name, tag=where or name, align_bytes=64)

        def load_list(name, src):
            tile = keep.tile(list(src.shape), U16, name=name)
            nc.sync.dma_start(tile[:], src)
            return tile

        def load_words(name, src, tag="", offset=None):
            if offset is None:
                tile = keep.tile([P, src.shape[1]], U32, name=name, tag=tag or name, align_bytes=64)
            else:
                tile = shared.tile([P, src.shape[1]], U32, name=name, offset=offset, align_bytes=64)
            nc.sync.dma_start(tile[:].bitcast(I32), src.rearrange("p n t -> p (n t)").bitcast(I32))
            return tile

        w1_raw = {}

        def load_w1(a0, a1, g, offset):
            raw = shared.tile([P, PACK, (a1 - a0) * P], F32, name=raw_tag(a0, g), offset=offset)
            rows = w1[g * K_PASS : (g + 1) * K_PASS, a0 * P : a1 * P]
            nc.sync.dma_start(raw[:], rows.rearrange("(p j) c -> p j c", j=PACK))
            for a in range(a0, a1):
                w1_raw[a, g] = raw[:, :, (a - a0) * P : (a - a0 + 1) * P]

        x_planes_all = keep.tile([P, T], U8, name="x_planes_all")
        nc.sync.dma_start(x_planes_all[0:32, :].bitcast(I32), x_scales.bitcast(I32).rearrange("g r t -> r g t"))
        offs_sb = load_list("offs_sb", offs)
        nc.vector.memset(x_planes_all[32:64, :].bitcast(I32), 0)
        nc.vector.memset(x_planes_all[64:P, :].bitcast(I32), 0)
        x_words_all = [load_words("x_words_all0", x_words[0], offset=8192)]
        gate_col = keep.tile([P, GATE_RUN], F32, name="gate_col")
        halves = gate.rearrange("d r v -> (d r v)")[(P - 1) * V :].rearrange("(j x) -> j x", j=2)[:, 0 : D * V // 2]
        nc.sync.dma_start(gate_col[:], halves.rearrange("j (m e) -> m j e", e=GATE_RUN))
        load_w1(0, 1, 0, 2048)
        x_words_all.append(load_words("x_words_all1", x_words[1], offset=24576))

        x_plane = keep.tile([P, PASSES * S], U8, name="x_plane", align_bytes=64)
        nc.vector.memset(x_plane[:].bitcast(I32), 0)
        ident = keep.tile([P, P], F32, name="ident")
        make_identity(nc, ident[:])

        neg_gate = keep.tile([P, D, V], F32, name="neg_gate")
        for b in range(GATE_RUN // LINE):
            spread = psum.tile([P, LINE, P], F32, name="spread%d" % b, tag="targets%d" % b)
            for e in range(LINE):
                nc.tensor.transpose(spread[:, e, :], gate_col[:, b * LINE + e : b * LINE + e + 1].to_broadcast([P, P]), ident[:])
            nc.scalar.activation(
                neg_gate[:].rearrange("q d v -> q (d v)").rearrange("q (j m e) -> q j m e", j=2, e=GATE_RUN)[:, :, :, b * LINE : (b + 1) * LINE],
                spread[:].rearrange("q e (m j) -> q j m e", j=2),
                COPY,
                scale=-1.0,
            )

        w1_bf, w1_codes, w1_planes = {}, {}, {}

        def round_w1(a, g0, g1, tag="", copy=nc.scalar.copy):
            w1_bf[a, g0] = place([P, g1 - g0, P * PACK], BF16, "w1_bf%d_%d" % (a, g0), tag)
            for g in range(g0, g1):
                copy(
                    w1_bf[a, g0][:, g - g0, :].rearrange("p (c i j) -> p c j i", i=LINE, j=PACK),
                    w1_raw[a, g].rearrange("p j (c i) -> p c j i", i=LINE),
                )

        def quantize_w1(a, g0, g1):
            codes = keep.tile([P, (g1 - g0) * P], U32, name="w1_codes%d_%d" % (a, g0), tag="w1_codes%d_%d" % (a, g0), align_bytes=64)
            planes = keep.tile([P, (g1 - g0) * P], U8, name="w1_planes%d_%d" % (a, g0), tag="w1_planes%d_%d" % (a, g0), align_bytes=64)
            nc.vector.quantize_mx(out=codes[:].bitcast(FP8X4), scales=planes[:], in_=w1_bf[a, g0][:].rearrange("p g c -> p (g c)"))
            for g in range(g0, g1):
                w1_codes[a, g] = codes[:, (g - g0) * P : (g - g0 + 1) * P]
                w1_planes[a, g] = planes[:, (g - g0) * P : (g - g0 + 1) * P]

        x_planes = keep.tile([P, S], U8, name="x_planes", align_bytes=64)
        nc.vector.tensor_copy(x_planes[:], x_planes_all[:].indirect(offs_sb[:]))

        for q in range(QUADRANTS):
            nc.sync.dma_start(x_plane[32 * q : 32 * q + 4, :].bitcast(I32), x_planes[8 * q : 8 * q + 8, :].bitcast(I32))
        load_w1(0, 1, 1, 0)
        load_w1(1, 2, 0, 4096)
        load_w1(1, 2, 1, 6144)
        pos_sb = [load_list("pos0_sb", pos1)]
        cen_sb = load_list("cen_sb", cen)
        pos_sb = pos_sb + [load_list("pos1_sb", pos2), load_list("pos2_sb", pos3)]
        for n in range(4):
            load_w1(2 + n // 2, 3 + n // 2, n % 2, (34816, 49152, 36864, 53248)[n])
        w2_codes = load_words("w2_codes", w2_words[0])
        x_first = keep.tile([P, S], U32, name="x_first", align_bytes=64)
        nc.vector.tensor_copy(x_first[:], x_words_all[0][:].indirect(offs_sb[:]))
        round_w1(0, 0, 1)
        quantize_w1(0, 0, 1)
        w2_plane = keep.tile([P, N], U8, name="w2_plane", tag="w1_bf0_0", align_bytes=64)
        nc.gpsimd.memset(w2_plane[:], 0)
        for q in range(QUADRANTS):
            nc.sync.dma_start(w2_plane[32 * q : 32 * q + 4, :].bitcast(I32), w2_scales[0, 4 * q : 4 * q + 4, :].bitcast(I32))
        x_second = shared.tile([P, LAST_PIECE], U32, name="x_second", offset=16384, align_bytes=64)
        nc.vector.tensor_copy(x_second[:], x_words_all[1][:].indirect(offs_sb[:, 0 : LAST_PIECE // LIST_COLUMN]))
        round_w1(0, 1, 2)
        quantize_w1(0, 1, 2)
        x_third = shared.tile([P, S - LAST_PIECE], U32, name="x_third", offset=0, align_bytes=64)
        nc.vector.tensor_copy(x_third[:], x_words_all[1][:].indirect(offs_sb[:, LAST_PIECE // LIST_COLUMN : S // LIST_COLUMN]))

        def x_codes(g, c0, c1):
            if g == 0:
                return x_first[:, c0:c1]
            return x_second[:, c0:c1] if c1 <= LAST_PIECE else x_third[:, c0 - LAST_PIECE : c1 - LAST_PIECE]

        def first_product(h, a, pieces, banks):
            accs = [psum.tile([P, c1 - c0], F32, name="acc%d_%d" % (a, c0), tag=bank) for (c0, c1), bank in zip(pieces, banks)]
            steps = [(g, n) for g in range(PASSES) for n in range(len(pieces))]
            for g, n in steps if a == 0 else sorted(steps, key=lambda step: step[1]):
                for acc, (c0, c1) in [(accs[n], pieces[n])]:
                    cuts = (c0, LAST_PIECE, c1) if g == 1 and c0 < LAST_PIECE < c1 else (c0, c1)
                    for n0, n1 in zip(cuts, cuts[1:]):
                        nc.tensor.matmul_mx(
                            out=acc[:, n0 - c0 : n1 - c0],
                            lhsT=w1_codes[a, g].bitcast(FP8X4),
                            lhsT_scale=w1_planes[a, g],
                            rhs=x_codes(g, n0, n1).bitcast(FP8X4),
                            rhs_scale=x_plane[:, g * S + n0 : g * S + n1],
                            start=(g == 0),
                            stop=(g == PASSES - 1 and n1 == c1),
                        )
            return [(h[:, c0:c1], acc[:]) for acc, (c0, c1) in zip(accs, pieces)]

        def empty(pieces):
            for into, acc in pieces:
                nc.scalar.activation(into, acc, COPY)


        zt_bf = keep.tile([P, BLOCKS * H], BF16, name="zt_bf", align_bytes=64)
        zt_pairs = zt_bf[:].rearrange("v (u b p e) -> v u b p e", u=2, b=BLOCKS, e=2)
        zt_words = zt_bf[:].bitcast(F32).rearrange("v (u b p) -> v u b p", u=2, b=BLOCKS)

        def entries(b0, b1):
            return slice(b0 * P // LIST_COLUMN, b1 * P // LIST_COLUMN)

        def neighbours(h, a, lists, b0, b1, tag=""):
            name = "terms%d_%d_%d" % (a, lists[0], b0)
            terms = place([P, len(lists), (b1 - b0) * P], F32, name, tag)
            for n, d in enumerate(lists):
                nc.vector.tensor_tensor(terms[:, n, :], h[:].indirect(pos_sb[d][:, entries(b0, b1)]), neg_gate[:, d, b0 * P : b1 * P], MULT)
            return [terms[:, n, :] for n in range(len(lists))]

        def centre(h, a, tag=""):
            own = keep.tile([P, V], F32, name="own%d" % a, tag=tag or "own%d" % a, align_bytes=64)
            nc.scalar.activation(own[:], h[:].indirect(cen_sb[:]), COPY)
            return own[:]

        def add_turned(bank, summand, first=False, last=False):
            count = summand.shape[1] // P
            for n in range(count):
                nc.tensor.matmul(
                    bank[:, n * P : (n + 1) * P],
                    summand[:, n * P : (n + 1) * P],
                    ident[:],
                    start=(first and n == 0),
                    stop=(last and n == count - 1),
                    is_transpose=True,
                )

        def add_all(bank, summands):
            for n, summand in enumerate(summands):
                add_turned(bank, summand, first=(n == 0), last=(n == len(summands) - 1))

        def round_z(bank, a, b0):
            count = bank.shape[1] // P
            rows = P // PACK
            nc.scalar.copy(
                zt_pairs[:, :, b0 : b0 + count, a * rows : (a + 1) * rows, :],
                bank.rearrange("v (b p u e) -> v u b p e", b=count, u=2, e=2),
            )

        def turn_back(b0, b1, tag):
            back = psum.tile([P, b1 - b0, 2, P], F32, name="back%d" % b0, tag=tag)
            for b in range(b0, b1):
                for u in range(2):
                    nc.tensor.transpose(back[:, b - b0, u, :], zt_words[:, u, b, :], ident[:])
            return back

        def empty_back(back, b0, copy):
            z_bf = keep.tile([P, back.shape[1] * K_PASS], BF16, name="z_bf%d" % b0, align_bytes=64)
            copy(z_bf[:].bitcast(F32).rearrange("p (b v u) -> p b v u", u=2, v=P), back[:].rearrange("p b u v -> p b v u"))
            return z_bf

        def second_product(res, z_bf, b0):
            z_codes = keep.tile([P, res.shape[1]], U32, name="z_codes%d" % b0, align_bytes=64)
            z_plane = keep.tile([P, res.shape[1]], U8, name="z_plane%d" % b0, align_bytes=64)
            nc.vector.quantize_mx(out=z_codes[:].bitcast(FP8X4), scales=z_plane[:], in_=z_bf[:])
            nc.tensor.matmul_mx(
                out=res, lhsT=w2_codes[:].bitcast(FP8X4), lhsT_scale=w2_plane[:], rhs=z_codes[:].bitcast(FP8X4), rhs_scale=z_plane[:], start=True, stop=True
            )

        def store(res, c0):
            res_sb = keep.tile([P, res.shape[1]], F32, name="res_sb%d" % c0)
            nc.scalar.activation(res_sb[:], res, COPY)
            nc.sync.dma_start(out[:, c0 : c0 + res.shape[1]], res_sb[:])

        def sum_bank(a, tag):
            return psum.tile([P, V], F32, name="sums%d" % a, tag=tag)[:]

        h = [shared.tile([P, S], F32, name="h%d" % a, offset=(40960, 32768, 36864, 45056)[a], align_bytes=64) for a in range(ROW_TILES)]
        empty(first_product(h[0], 0, FIRST_PIECES, ("product1", "product2", "product3", "product0")))
        for g in range(PASSES):
            round_w1(1, g, g + 1, ("w1_bf0_1", "")[g], nc.vector.tensor_copy)
        for g in range(PASSES):
            quantize_w1(1, g, g + 1)
        own0 = centre(h[0], 0)
        round_w1(2, 0, PASSES)
        empty(first_product(h[1], 1, HALVES, ("product1", "product2")))
        terms0 = neighbours(h[0], 0, (0, 1, 2), 0, BLOCKS)
        quantize_w1(2, 0, PASSES)
        round_w1(3, 0, PASSES, "w1_planes1_1")
        own1 = centre(h[1], 1)
        sums0 = sum_bank(0, "targets3")
        add_all(sums0, [own0] + terms0)
        round_z(sums0, 0, 0)
        empty(first_product(h[2], 2, HALVES, ("product3", "targets0")))
        terms1 = neighbours(h[1], 1, (0,), 0, BLOCKS)
        quantize_w1(3, 0, PASSES)
        terms1 = terms1 + neighbours(h[1], 1, (1, 2), 0, BLOCKS, 53248)
        halves3 = first_product(h[3], 3, HALVES[:1], ("product2",))
        empty(halves3)
        halves3 = first_product(h[3], 3, HALVES[1:], ("product2",))
        fetched = keep.tile([P, V], F32, name="fetched", align_bytes=64)
        nc.scalar.activation(fetched[:], h[2][:].indirect(pos_sb[2][:]), COPY)
        empty(halves3)
        own2 = centre(h[2], 2, "w1_codes3_0")
        own3 = centre(h[3], 3)
        terms2 = neighbours(h[2], 2, (0, 1), 0, BLOCKS)
        weighted = keep.tile([P, V], F32, name="weighted", align_bytes=64)
        nc.vector.tensor_tensor(weighted[:], fetched[:], neg_gate[:, 2, :], MULT)
        terms2.append(weighted[:])
        sums2 = sum_bank(2, "targets2")
        sums1 = sum_bank(1, "product3")
        add_all(sums1, terms1[:1] + [own1] + terms1[1:])
        add_all(sums2, terms2 + [own2])
        round_z(sums1[:, 0 : V // 2], 1, 0)
        round_z(sums2[:, 0 : V // 2], 2, 0)

        def last_unit(b0, b1, tag):
            bank = psum.tile([P, (b1 - b0) * P], F32, name="sums3_%d" % b0, tag=tag)[:]
            terms = neighbours(h[3], 3, (0, 1, 2), b0, b1)
            ahead = 2 if b0 == 0 else 0
            add_all(bank, terms[:ahead] + [own3[:, b0 * P : b1 * P]] + terms[ahead:])
            round_z(bank, 3, b0)

        last_unit(0, 2, "targets3")
        round_z(sums1[:, V // 2 : V], 1, 2)
        round_z(sums2[:, V // 2 : V], 2, 2)
        last_unit(2, 3, "targets0")
        back_01 = turn_back(0, 2, "product0")
        z_01 = empty_back(back_01, 0, nc.scalar.copy)
        last_unit(3, 4, "targets3")
        back_2 = turn_back(2, 3, "targets1")
        z_2 = empty_back(back_2, 2, nc.vector.tensor_copy)
        back_3 = turn_back(3, 4, "product2")
        z_3 = empty_back(back_3, 3, nc.scalar.copy)

        res_012 = psum.tile([P, 3 * P], F32, name="res_012", tag="product1")
        second_product(res_012[:, 0 : 2 * P], z_01, 0)
        second_product(res_012[:, 2 * P : 3 * P], z_2, 2)
        store(res_012[:], 0)
        res_3 = psum.tile([P, P], F32, name="res_3", tag="product3")
        second_product(res_3[:], z_3, 3)
        store(res_3[:], 3 * P)
